import numpy as np, ml_dtypes
CORES = [3,11,19,27,35,43,51,59]
N = 8
BF = ml_dtypes.bfloat16
V, G, ST, RO = 1280, 1056, 5, 3
D, B, Q = 32, 192, 32
C, W = 256, 2336
def pack(xx, yy, nl, al):
    h = lambda a: np.ascontiguousarray(a).reshape(N, 128, V)
    return {"xf": h(xx).astype(np.float32).astype(BF), "lab": h(yy).astype(np.float32).astype(BF), "nb": h(nl).astype(np.int32), "asc": h(al).astype(np.int32)}
def signs(rng, *shape):
    return rng.integers(0, 2, shape) * 2 - 1
def both(c):
    return np.concatenate([c, np.roll(c, -1, axis=0)[..., :G]], axis=-1)
def alike(rng, c, want):
    o = np.argsort(c, axis=2, kind="stable"); n = np.sum(c < 0, axis=2)[:, :, None]; m = c.shape[2]
    j = np.where(want < 0, rng.random(want.shape) * n, n + rng.random(want.shape) * (m - n)).astype(np.int64)
    return np.take_along_axis(o, np.minimum(j, m - 1), 2)
def parts(rng):
    pat = signs(rng, 1, 8, 16, 1); c = signs(rng, N, 8, V)
    yy = c[:, :, None, :] * pat; yy = np.where(rng.random(yy.shape) < 0.1, -yy, yy)
    xx = rng.integers(0, 16, (N, 8, 16, V)); nl = rng.integers(0, W, (N, 8, 16, V))
    al = alike(rng, c, np.repeat(c[:, :, None, :], 16, axis=2).reshape(N, 8, 16 * V)).reshape(N, 8, 16, V)
    al = np.where(rng.random(al.shape) < 0.1, rng.integers(0, V, al.shape), al)
    r, g, i, v = np.indices((N, 8, 4, V))
    nl[r, g, rng.integers(1, 16, r.shape), al[:, :, :4]] = v
    share = rng.choice(np.array([0.1, 0.4, 0.7, 0.95]), (N, 8, 1))
    nl[:, :, 0] = alike(rng, both(c), np.where(rng.random((N, 8, V)) < share, -c, c))
    return xx, yy, nl, al
def setup_inputs(rng):
    return pack(*parts(rng))
def setup_inputs_spread(rng):
    s = (N, 8, 16, V)
    xx = np.minimum((16 * np.power(rng.random(s), np.exp2(rng.integers(-3, 4, (N, 8, 1, V))))).astype(np.int64), 15)
    yy = np.where(rng.random(s) < rng.random((N, 8, 1, V)), 1, -1)
    ex = rng.choice(np.array([0.4, 1.0, 2.5]), (N, 8, 1, 1)); ea = rng.choice(np.array([0.4, 1.0, 2.5]), (N, 8, 1, 1))
    nl = np.minimum((W * np.power(rng.random(s), ex)).astype(np.int64), W - 1)
    al = np.minimum((V * np.power(rng.random(s), ea)).astype(np.int64), V - 1)
    return pack(xx, yy, nl, al)
def setup_inputs_ends(rng):
    v = np.arange(V); odd = (np.arange(8) % 2)[None, :, None]; z = ST * (C - 1)
    pat = signs(rng, 1, 8, 16, 1); c = signs(rng, N, 8, V)
    kind = rng.integers(0, 10, (N, 8, V)); kind[..., 1] = 0; kind[..., V - 2] = 0; kind[..., 2] = 2; kind[..., V - 3] = 2; kind[..., V - 1] = 4
    nz = np.where(kind < 2, 16, np.where(kind < 4, 0, rng.integers(7, 10, kind.shape))); nz[..., V - 1] = 8
    o = np.argsort(rng.random((N, 8, 16, V)), axis=2)
    nl = np.where(kind[:, :, None, :] >= 7, rng.integers(0, W, o.shape), np.where(o < nz[:, :, None, :], 0, W - 1))
    nl[..., 0] = np.where((np.arange(16) == 0) | (np.arange(16) > 9), W - 1, 0)
    nl[..., G - 1] = rng.integers(1, G - 1, (N, 8, 16))
    ka = rng.integers(0, 10, (N, 8, V))[:, :, None, :]
    al = np.where(ka < 2, 0, np.where(ka < 4, V - 1, np.where(ka < 7, (V - 1) * rng.integers(0, 2, o.shape), rng.integers(0, V, o.shape))))
    bad = (v % ST < RO) & (rng.random((N, 8, V)) < np.where(odd == 1, 0.9, 0.2))
    bad[..., ST * (C - 2)] = True; bad[..., z:] = False; bad[..., 1] = False; bad[..., 2] = False; bad[..., G - 1] = False; bad[..., 0] = odd[..., 0] == 1
    c = np.where(bad, 1, c); c[..., 0] = 1; c[..., G - 1] = -1; c[..., z] = -c[..., V - 1]
    al = np.where(bad[:, :, None, :], 0, al); al[..., G - 1] = V - 1; al[..., z:] = V - 1; al[:, 0::2, :, 0] = V - 1
    nl[:, :, 0] = np.where(bad, W - 1, nl[:, :, 0]); nl[:, :, 0, z] = np.where(c[..., V - 1] > 0, 0, W - 1)
    kx = rng.integers(0, 5, (N, 8, V))[:, :, None, :]
    xx = np.where(kx == 0, 0, np.where(kx == 1, 15, 15 * rng.integers(0, 2, o.shape)))
    return pack(xx, c[:, :, None, :] * pat, nl, al)
def setup_inputs_corners(rng):
    xx, yy, nl, al = parts(rng); pat = signs(rng, 8, 16, 1)
    cand = np.arange(C) * ST; rest = np.flatnonzero(np.arange(V) % ST != 0); gh = V + np.flatnonzero(np.arange(G) % ST != 0)
    for r in range(N):
        turn = rng.permutation(8); few = int(rng.integers(1, 9))
        for g in range(8):
            nd, nf, nq = ((D, B, Q), (D + 1, B + 1, Q + 1), (C, B + 1, B), (D - 1, B - 1, Q - 1), (few, 16 * few, few), (0, 0, 0), (D, B, 0), (D, 1, 1))[int(turn[g])]
            o = rng.permutation(rest); hp, hm, hq = int(o[0]), int(o[1]), int(o[2])
            c = signs(rng, V); c[cand] = 1; c[hp] = 1; c[hq] = 1; c[hm] = -1; yy[r, g] = c * pat[g]
            nl[r, g, :, hp] = rng.permutation(np.array([hq] * 9 + [hm] * 7))
            will = np.sort(rng.permutation(C)[:nd]) * ST; die = will[:D]; late = will[D:]
            nl[r, g, 0, cand] = hm; nl[r, g, 0, will] = hq; al[r, g][:, cand] = hp
            al[r, g][:, late] = o[rng.integers(3 + nf, len(o), (16, len(late)))]
            if nd == 0: continue
            bs = np.sort(o[3:3 + nf]); m = 16 * len(die)
            al[r, g][:, die] = rng.permutation(np.concatenate([bs, bs[rng.integers(0, nf, m - nf)]])).reshape(16, -1)
            ask = np.zeros(nf, bool); ask[rng.permutation(min(nf, B))[:nq]] = True
            fresh = np.where(ask, gh[rng.integers(0, len(gh), (16, nf))], rest[rng.integers(0, len(rest), (16, nf))])
            dead = die[rng.integers(0, len(die), (16, nf))]
            li = np.where(np.arange(16)[:, None] == rng.integers(0, 16, nf), dead, fresh)
            t = rng.random(nf); li = np.where(~ask & (t < 0.2), fresh, np.where(~ask & (t < 0.3), dead, li))
            nl[r, g][:, bs] = li
    return pack(xx, yy, nl, al)
def setup_inputs_alike(rng):
    xx, yy, nl, al = parts(rng); me = np.arange(V)
    base = rng.integers(0, 16, (N, 8, 16, 4)); base[:, 0] = base[:, 0, :, :1]
    xx = np.take_along_axis(base, rng.integers(0, 4, (N, 8, 1, V)), 3)
    hub = rng.integers(0, W, (N, 8, 24)); hub[..., :4] = np.array([0, V - 1, V, W - 1]); hub[..., 4:8] = ST * np.arange(1, 5); hub[..., 8:12] = V + ST * np.arange(4)
    nl[:, 1::2] = np.take_along_axis(hub[:, 1::2], rng.integers(0, 24, (N, 4, 16 * V)), 2).reshape(N, 4, 16, V)
    nl[:, 2] = np.where(rng.random((N, 16, V)) < 0.3, me, nl[:, 2])
    nl[:, 4] = rng.integers(V, W, (N, 16, V)); nl[:, 6] = rng.integers(0, V, (N, 16, V))
    al[:, 3] = rng.choice(np.array([0, V - 1, V // 2, 3]), (N, 16, V))
    al[:, 5] = np.where(rng.random((N, 16, V)) < 0.5, me, al[:, 5]); al[:, 7] = al[:, 7, :1]
    return pack(xx, yy, nl, al)
def setup_inputs_shared(rng):
    xx, yy, nl, al = parts(rng); pat = signs(rng, 8, 16, 1); v = np.arange(V); K = B // 4; h = K // 2
    cand = np.flatnonzero(v % ST < RO); gh = V + np.flatnonzero(np.arange(G) % ST >= RO)
    q = np.arange(B) // 2 % K; far = np.arange(K) % h % 4 == 3
    for r in range(N):
        for g in range(8):
            m = np.sort(rng.permutation(C)[:2 * K]) * ST + RO; bs = np.stack([m, m + 1], axis=1).reshape(-1)
            o = rng.permutation(np.setdiff1d(v[v % ST >= RO], bs)); hp, hq, hm = int(o[0]), int(o[1]), int(o[2])
            u = o[3:3 + K]; rest = o[3 + K:]; old = rest[:64]; more = np.concatenate([rest, gh])
            die = np.sort(rng.permutation(C)[:D]) * ST
            ws = np.concatenate([rng.permutation(C)[:h] * ST + 1, rng.permutation(C)[:h] * ST + 2])
            c = signs(rng, V); c[cand] = 1; c[hp] = 1; c[hq] = 1; c[hm] = -1; yy[r, g] = c * pat[g]
            nl[r, g, :, hp] = rng.permutation(np.array([hq] * 9 + [hm] * 7))
            nl[r, g, 0, cand] = hm; nl[r, g, 0, die] = hq; nl[r, g, 0, ws] = hq
            al[r, g][:, cand] = hp; al[r, g][:, ws] = old[rng.integers(0, 64, (16, K))]
            al[r, g][:, die] = rng.permutation(np.concatenate([bs, bs[rng.integers(0, B, 16 * D - B)]])).reshape(16, -1)
            base = rng.integers(0, 13, (16, h)); base = np.where(far[:h], 15 * (base & 1), base); base = np.concatenate([base, base], axis=1)
            x = xx[r, g]
            x[:, bs] = base[:, q] + np.where(far[q], 0, rng.integers(0, 2, (16, B)))
            x[:, u] = np.where(far, base, base + 1)
            x[:, ws] = np.where(far, 15 - base, base + 2 * (np.arange(K) >= h))
            lu = np.where(far, u, more[rng.integers(0, len(more), (16, K))]); a = np.where(far, 15, rng.integers(0, 16, K))
            lu[a, np.arange(K)] = ws; lu[(a[:h] + 5) & 15, np.arange(h)] = np.where(far[:h], u[:h], ws[h:])
            nl[r, g][:, u] = lu
            li = more[rng.integers(0, len(more), (16, B))]; a = rng.integers(0, 16, B)
            li[a, np.arange(B)] = die[rng.integers(0, D, B)]; li[(a + rng.integers(1, 16, B)) & 15, np.arange(B)] = u[q]
            nl[r, g][:, bs] = li
    return pack(xx, yy, nl, al)
def check_inputs(d):
    bad = []
    for k, lo, hi in (("xf", 0, 15), ("lab", -1, 1), ("nb", 0, W - 1), ("asc", 0, V - 1)):
        a = np.asarray(d[k]).astype(np.float64)
        if not np.all((a >= lo) & (a <= hi)): bad.append("range of " + k)
        elif k == "xf" and not np.all(a == np.floor(a)): bad.append("xf holds whole numbers")
        elif k == "lab" and not np.all(np.abs(a) == 1): bad.append("lab holds -1 and 1")
    return bad
def take(tab, ix):
    return np.take_along_axis(tab, ix[:, :, None, :], 3)
def alive(lv, names):
    return np.take_along_axis(lv, names.reshape(N, 8, -1), 2).reshape(names.shape)
def apart(X, xb, names):
    return np.stack([np.sum(np.abs(take(X, names[:, :, i]) - xb), axis=2) for i in range(16)], axis=2)
def reference(xf, lab, nb, asc):
    X = both(xf.astype(np.float32).astype(np.int32).reshape(N, 8, 16, V)); Y = both(lab.astype(np.float32).astype(np.int32).reshape(N, 8, 16, V))
    nl = nb.astype(np.int64).reshape(N, 8, 16, V); al = asc.astype(np.int64).reshape(N, 8, 16, V)
    S = np.zeros((N, 8, 16, V), np.int32)
    for i in range(16): S = S + take(Y, nl[:, :, i])
    died = np.zeros((N, 8, V), np.int64); flag = np.zeros((N, 8, V), bool); last = np.zeros(N, np.int64); BIG = 1 << 20
    for t in range(RO):
        v = np.arange(C) * ST + t; av = al[:, :, :, v]
        e = take(Y, nl[:, :, 0, v]) - Y[:, :, :, v]; loss = np.zeros((N, 8, C), np.int64)
        for i in range(16):
            ya = take(Y, av[:, :, i]); sa = take(S, av[:, :, i])
            loss = loss + np.sum(ya * sa > 0, axis=2) - np.sum(ya * (sa + e) > 0, axis=2)
        will = loss <= (last & 7)[:, None, None]
        die = will & (np.add.accumulate(will.astype(np.int64), axis=2) <= D)
        died[:, :, v] = np.where(die, t + 1, died[:, :, v]); last = np.sum(die.astype(np.int64), axis=(1, 2))
        live = died == 0; lv = both(live)
        r, g, i, j = np.nonzero(np.repeat(die[:, :, None, :], 16, axis=2)); flag[r, g, av[r, g, i, j]] = True; flag = flag & live
        tr = flag & (np.add.accumulate(flag.astype(np.int64), axis=2) <= B); flag = flag & ~tr
        b = np.argsort(~tr, axis=2, kind="stable")[..., :B]; ok = np.take_along_axis(tr, b, 2)
        lb = take(nl, b); on = alive(lv, lb); xb = take(X, b)
        k = np.argmax(~on, axis=2); need = ok & np.any(~on, axis=2) & np.any(on, axis=2)
        iu = np.argmin(np.where(on, apart(X, xb, lb), BIG), axis=2); u = np.take_along_axis(lb, iu[:, :, None, :], 2)[:, :, 0]
        asks = need & (u >= V); served = asks & (np.add.accumulate(asks.astype(np.int64), axis=2) <= Q)
        far = take(np.roll(nl, -1, axis=0), np.maximum(u - V, 0)); far = np.where(far < G, V + far, -1)
        lu = np.where((u < V)[:, :, None, :], take(nl, np.minimum(u, V - 1)), far); nm = np.maximum(lu, 0)
        fit = (lu >= 0) & alive(lv, nm) & (lu != b[:, :, None, :]) & ((need & (u < V)) | served)[:, :, None, :]
        for i in range(16): fit = fit & (lu != lb[:, :, i:i + 1])
        iw = np.argmin(np.where(fit, apart(X, xb, nm), BIG), axis=2); w = np.take_along_axis(nm, iw[:, :, None, :], 2)[:, :, 0]
        r, g, s = np.nonzero(np.any(fit, axis=2)); bb = b[r, g, s]; ww = w[r, g, s]; kk = k[r, g, s]; old = nl[r, g, kk, bb]
        nl[r, g, kk, bb] = ww; S[r, g, :, bb] = S[r, g, :, bb] + Y[r, g, :, ww] - Y[r, g, :, old]
        m = ww < V; r, g, bb, ww = r[m], g[m], bb[m], ww[m]
        first = np.unique((r * 8 + g) * V + ww, return_index=True)[1]
        r, g, bb, ww = r[first], g[first], bb[first], ww[first]; al[r, g, (bb + t) & 15, ww] = bb
    return {"yn": nl.reshape(N, 128, V).astype(np.float32), "yd": died.astype(np.float32)}

@@ -1,0 +1,541 @@
+from concourse.mybir import AluOpType as AL, ActivationFunctionType as AF, AxisListType as AX
+
+V, G, W = 1280, 1056, 2336
+CEN = 1168.0
+BIGK = 4096.0 * 4000
+DEADX = 131072.0
+LOSS0 = 192 * 31.5 * 16
+PAIRS = [128, 128, 128, 112, 72, 40, 32]
+PBANK = [0, 1, 4, 0, 2, 3, 7]
+NLAST = 16
+NSTEP = 28
+NMAX, NPE = 6, 4
+
+SB = {
+    "NBI": (1280, "int32"), "NBU": (1280, "uint16"), "NB": (1480, "float32"), "GH": (1480, "float32"),
+    "ASC": (1632, "int32"), "X": (2880, "bfloat16"), "Y": (2352, "bfloat16"), "GS": (20480, "bfloat16"),
+    "Z": (1472, "bfloat16"), "QT": (1472, "bfloat16"), "ZA": (1280, "bfloat16"), "YD": (1440, "float32"),
+    "ONE": (384, "bfloat16"), "BO": (128, "bfloat16"), "ID": (128, "bfloat16"), "NID": (128, "bfloat16"), "ZR": (128, "bfloat16"),
+    "ID16": (128, "bfloat16"), "IDB": (128, "bfloat16"), "IDF": (128, "float32"), "IDH": (128, "float16"), "NIH": (128, "float16"),
+    "BOH": (128, "float16"), "BO4": (128, "bfloat16"), "TRI": (128, "bfloat16"), "LK": (128, "bfloat16"), "N32": (128, "bfloat16"),
+    "O16": (128, "bfloat16"), "SEL": (2048, "float16"), "QM": (16, "float32"),
+    "F1": (144, "bfloat16"), "FA": (144, "bfloat16"), "FB": (144, "bfloat16"), "FN": (144, "bfloat16"),
+    "FH": (144, "float16"), "FW": (144, "float16"), "FE": (144, "float16"),
+    "KU": (128, "bfloat16"), "KC": (128, "bfloat16"), "KN": (128, "bfloat16"), "KT": (192, "float32"),
+    "PI": (8, "int32"), "PC": (16, "float32"), "IP": (128, "bfloat16"), "IS": (192, "bfloat16"), "IOF": (1472, "float32"),
+    "SG": (81, "float32"), "SJ": (81, "bfloat16"), "ST": (12, "float32"), "DU": (12, "float32"),
+    "RS": (192, "float32"), "TM": (192, "float16"), "RPI": (12, "int32"), "RP": (12, "uint16"), "C32": (288, "bfloat16"),
+    "CX": (32, "bfloat16"), "CD": (96, "float32"), "JK": (1680, "bfloat16"), "HM": (256, "bfloat16"), "HS": (512, "bfloat16"), "HH": (512, "float16"),
+    "TC": (32, "float16"), "F4": (144, "bfloat16"), "ND": (12, "float32"), "AK": (32, "bfloat16"),
+    "OA": (256, "uint16"), "NO": (16, "uint16"), "EP": (256, "bfloat16"), "C1": (256, "bfloat16"), "C2": (256, "bfloat16"),
+    "SM": (256, "bfloat16"), "T1": (256, "float16"), "T2": (256, "bfloat16"), "WL": (288, "bfloat16"), "CC": (288, "bfloat16"),
+    "EI": (8, "int32"), "EF": (8, "float32"), "AC": (12, "float32"), "DV": (8, "float32"), "DX": (8, "uint16"),
+    "DO0": (8, "uint16"), "DO1": (8, "uint16"), "DO2": (8, "uint16"), "DR0": (8, "uint16"), "DR1": (8, "uint16"), "DR2": (8, "uint16"),
+    "NA": (34, "float32"), "NJ": (8, "float32"), "LI": (34, "int32"), "LO": (34, "float32"), "OH": (34 * 128, "bfloat16"), "SN": (34 * 81, "bfloat16"),
+    "CS": (80, "float32"), "FL": (92, "bfloat16"), "FS": (93, "bfloat16"), "CU": (96, "float32"), "DF": (160, "float32"), "CT": (81, "float32"),
+    "HU": (12, "uint16"), "HB": (12, "bfloat16"), "CM": (192, "bfloat16"), "BU": (12, "uint16"),
+    "LU": (192, "uint16"), "LH": (192, "float16"), "LF": (192, "float32"), "XB": (192, "bfloat16"), "DD": (3072, "bfloat16"), "EQ": (17 * 192, "bfloat16"),
+    "TK": (192, "float32"), "TS": (192, "float32"), "KI": (32, "int32"), "KF": (32, "float32"), "TH": (192, "float16"), "UR": (576, "float16"),
+    "SD": (192, "bfloat16"), "KL": (192, "float16"), "FK": (12, "float32"), "UO": (24, "uint16"), "UF": (24, "float32"),
+    "LG": (192, "float32"), "L2": (192, "float32"), "MU": (192, "uint16"), "MH": (192, "float16"),
+    "OO": (12, "uint16"), "QP": (192, "bfloat16"), "YO": (192, "bfloat16"), "YB": (192, "bfloat16"), "RG": (384, "float32"), "RB": (192, "float16"), "LQ": (2048, "bfloat16"), "LV": (768, "bfloat16"),
+    "DZ0": (1632, "bfloat16"), "DZ1": (1632, "bfloat16"), "WS": (12, "uint16"), "LT": (128, "bfloat16"),
+    "WR": (576, "float16"), "WO": (24, "uint16"), "WF": (48, "float32"), "QN": (384, "bfloat16"), "EE": (12 * 192, "bfloat16"), "LS": (192, "bfloat16"),
+    "MS0": (204, "float32"), "MS1": (204, "float32"), "MS2": (204, "float32"), "MR0": (204, "float32"), "MR1": (204, "float32"), "MO": (12, "uint16"),
+}
+PLACE = {}
+SCRATCH = {}
+for _k, (_n, _d) in SB.items():
+    if _n <= 200 and _k[:2] not in ("DO", "DR"):
+        _at = SCRATCH.get("pool_" + _d, (0, [128, 0]))[1][1]
+        PLACE[_k] = ("pool_" + _d, _at)
+        SCRATCH["pool_" + _d] = ("sbuf", [128, _at + (_n + 15) // 16 * 16], _d)
+    else:
+        SCRATCH[_k] = ("sbuf", [128, _n], _d)
+for _b in range(8):
+    SCRATCH["P%d" % _b] = ("psum", [128, 512], "float32")
+LOADS = ["l_lab", "l_nb", "l_asc", "l_xf", "s_yd", "s_y0", "s_y1"]
+MSGS = ["lab", "xf", "nb", "d0", "d1", "d2", "u0", "u1"]
+SEMAPHORES = ["qV", "qA", "qP", "qG"] + LOADS + ["r_" + m for m in MSGS] + ["w_" + m for m in MSGS]
+
+
+def A(name, lo=None, hi=None, st=None, p=None, ind=None):
+    n = SB[name][0] if name in SB else 512
+    return (name, 0 if lo is None else lo, n if hi is None else hi, st, p, ind)
+
+
+def rank_program(g, core, T, topo):
+    rank = T.rank_of(core)
+    if rank is None:
+        return
+    dst = T.cores[(rank - 1) % len(T.cores)]
+    rid, pid = topo.addr(dst)[0], topo.addr(dst)[1]
+    mask = topo.mask(core, dst)
+    ne = len(topo.engines(core, dst))
+    Q = {"V": g.vector, "A": g.scalar, "P": g.tensor, "G": g, "S": g.sync}
+    ops = []
+
+    def R(a):
+        if not isinstance(a, tuple):
+            return a
+        ps = slice(None) if a[4] is None else slice(*a[4])
+        nm, at = PLACE.get(a[0], (a[0], 0))
+        r = T[nm][ps, at + a[1]:at + a[2]:a[3]] if a[3] else T[nm][ps, at + a[1]:at + a[2]]
+        return r.indirect(R(a[5])) if a[5] else r
+
+    def add(q, emit, outs, ins, token=None):
+        rd = [a for a in ins if isinstance(a, tuple)]
+        rd = rd + [a[5] for a in rd + outs if a[5]]
+        ops.append([q, emit, rd, outs, token])
+
+    def cp(o, i): add("V", lambda: g.vector.tensor_copy(R(o), R(i)), [o], [i])
+    def tt(o, a, b, op): add("V", lambda: g.vector.tensor_tensor(R(o), R(a), R(b), op), [o], [a, b])
+    def ts(o, a, s1, op0, s2=None, op1=None):
+        if op1 is None:
+            add("V", lambda: g.vector.tensor_scalar(R(o), R(a), R(s1), None, op0), [o], [a, s1])
+        else:
+            add("V", lambda: g.vector.tensor_scalar(R(o), R(a), R(s1), R(s2), op0, op1), [o], [a, s1, s2])
+    def scan(o, a, b, init, op0, op1): add("V", lambda: g.vector.tensor_tensor_scan(R(o), R(a), R(b), init, op0, op1), [o], [a, b])
+    def tr(o, i): add("V", lambda: g.vector.transpose(R(o), R(i)), [o], [i])
+    def ms(o, c): add("V", lambda: g.vector.memset(R(o), c), [o], [])
+    def act(o, i, f, bias=0.0, scale=1.0, acc=None):
+        if acc is None:
+            add("A", lambda: g.scalar.activation(R(o), R(i), f, bias=R(bias), scale=scale), [o], [i, bias])
+        else:
+            add("A", lambda: g.scalar.activation(R(o), R(i), f, bias=R(bias), scale=scale, accum_out=R(acc)), [o, acc], [i, bias])
+    def mm(o, l, r, start, stop): add("P", lambda: g.tensor.matmul(R(o), R(l), R(r), start, stop), [o], [l, r])
+    def iota(o, pat, base=0, cm=0):
+        if SB[o[0]][1] == "int32":
+            add("G", lambda: g.iota(R(o), pat, base, cm), [o], [])
+        else:
+            add("G", lambda: g.iota(R(o), pat, base, cm, allow_small_or_imprecise_dtypes=True), [o], [])
+    def fill(o, c): iota(o, [[0, o[2] - o[1]]], c)
+    def sel(o, i, pat, op, base, cm): add("G", lambda: g.affine_select(R(o), R(i), pat, op, 0.0, base, cm), [o], [i])
+    def load(q, o, src, sem): add(q, lambda: Q[q].dma_start(R(o), src).then_inc(T.sem[sem], 16), [o], [], (sem, 16))
+    def store(q, d, i, sem): add(q, lambda: Q[q].dma_start(d, R(i)).then_inc(T.sem[sem], 16), [], [i], (sem, 16))
+    def send(m, o, i, after=()):
+        add("G", lambda: g.remote_dma(R(o), R(i), T.sem["r_" + m], T.sem["w_" + m], pid, rid, mask), list(after), [i], ("w_" + m, ne))
+    def recv(m, o): add("X", None, [o], [], ("r_" + m, ne))
+    def wrap(o, f, buf, lo, n, first=True, last=True):
+        for q in range(16):
+            mm(o, A(f, 16 - q, 144 - q), A(buf, lo + q, lo + n, 16), first and q == 0, last and q == 15)
+    def col(name, c): return A(name, c, c + 1)
+    def gat(name, lo, hi, off): return A(name, lo, hi, ind=off)
+    def slab(name, i, n=1): return A(name, 192 * i, 192 * (i + n))
+    PQ, P16 = col("PC", 0), col("PC", 1)
+
+    load("S", A("Y", 0, V), T.lab[:], "l_lab")
+    load("A", A("NBI"), T.nb[:], "l_nb")
+    recv("lab", A("Y", V, W)); recv("xf", A("X", V, W)); recv("nb", A("GH", 8, 8 + G))
+    for t in range(3): recv("d%d" % t, A("DR%d" % t, 0, 2))
+    for t in range(2): recv("u%d" % t, A("MR%d" % t))
+    iota(col("PI", 0), [[0, 1]], 0, 1)
+    ms(A("ONE"), 1.0)
+    iota(A("KT"), [[0, 12], [1, 16]])
+    sel(A("BO"), A("ONE", 0, 128), [[-16, 8], [0, 16]], AL.is_ge, 0, 1)
+    sel(A("BO"), A("BO"), [[16, 8], [0, 16]], AL.is_ge, 15, -1)
+    sel(A("ID"), A("ONE", 0, 128), [[-1, 128]], AL.is_equal, 0, 1)
+    send("lab", A("Y", V, W), A("Y", 0, G), [col("JK", 0), col("X", 0), col("ASC", 0)])
+    load("S", A("X", 0, V), T.xf[:], "l_xf")
+    load("S", A("ASC", 0, V), T.asc[:], "l_asc")
+    for f in ["F1", "FA", "FB", "FN", "F4", "FH", "FE", "KU", "KC", "ZR"]: ms(A(f), 0.0)
+    ms(col("AK", 16), 0.0)
+    ts(col("PI", 1), col("PI", 0), 15, AL.bitwise_and)
+    ms(A("Y", W), 0.0); ms(A("WL", 256), 1.0); ms(A("C32"), 32.0); ms(A("CX"), DEADX)
+    cp(PQ, col("PI", 1))
+    tt(P16, col("PI", 0), col("PI", 1), AL.subtract)
+    ms(A("FL", 80), 1.0); ms(col("FS", 0), 0.0); ms(col("CT", 0), 0.0); ms(A("O16"), 1.0 / 16); ms(col("EF", 0), LOSS0)
+    ms(col("PC", 5), 31.5); ms(col("PC", 6), -31.5 / 64); ms(col("PC", 7), -1.6e7)
+    ts(A("QM"), A("KT", 0, 16), PQ, AL.is_equal)
+    ts(A("RS"), A("KT"), 0.0, AL.is_equal, 2.0 ** 26, AL.mult)
+    ms(col("PC", 11), 64.5 / 64)
+    ts(col("PC", 8), PQ, 1.0, AL.is_lt, 16.0, AL.mult)
+    ts(col("PC", 10), col("PC", 8), PQ, AL.add, -1.0, AL.add)
+    ts(col("PC", 3), PQ, -1.0, AL.mult, -32.0, AL.add)
+    ts(A("FE", 16, 144, 16), A("BO", 0, 128, 16), col("QM", 0), AL.mult)
+    cp(A("FH", 16, 144, 16), A("BO", 0, 128, 16))
+    for f, c in [("F1", 1.0), ("FA", 65536.0), ("FB", 131072.0), ("FN", -65536.0), ("F4", 4096.0)]:
+        act(A(f, 16, 144, 16), A("BO", 0, 128, 16), AF.Copy, 0.0, c)
+    for f, s, c in [("NID", "ID", -1.0), ("ID16", "ID", 16.0), ("IDB", "ID", 2.0 ** 25), ("IDF", "ID", 1.0), ("N32", "ID", -32.0), ("BO4", "BO", 192.0)]:
+        act(A(f), A(s), AF.Copy, 0.0, c)
+    act(A("KU", p=(0, 1)), A("KT", 0, 128, p=(0, 1)), AF.Copy, 0.0, 4096.0)
+    ms(A("KU", p=(32, 33)), CEN + 8); ms(A("KC", p=(0, 1)), CEN)
+    cp(A("BOH"), A("BO")); cp(A("IDH"), A("ID")); ts(A("NIH"), A("ID"), -1.0, AL.mult)
+    for t in range(3): act(A("LV", 256 * t, 256 * t + 256), A("Y", t, t + 1276, 5), AF.Copy)
+    ms(A("LQ"), 0.0)
+    cp(A("NBU"), A("NBI"))
+    cp(A("NB", 8, 8 + V), A("NBI"))
+    iota(A("IP"), [[1, 128]]); iota(A("IS"), [[1, 192]]); iota(A("SG"), [[16, 81]]); iota(A("SJ"), [[1, 81]])
+    iota(A("ST"), [[16, 12]]); iota(A("RPI"), [[1, 12]])
+    sel(A("TRI"), A("BO"), [[1, 128]], AL.is_ge, 0, -1)
+    sel(A("LT"), A("BO"), [[1, 128]], AL.is_gt, 0, -1)
+    iota(A("HM", 0, 128), [[0, 4], [-1, 2], [0, 16]], 1); iota(A("HM", 128, 256), [[0, 4], [1, 2], [0, 16]])
+    for e in range(2):
+        for h in range(2):
+            sel(A("HS", 256 * e + 128 * h, 256 * e + 128 * h + 128), A("HM", 128 * h, 128 * h + 128), [[-1, 128]], AL.is_equal, 16 * (h - e), 1)
+    send("nb", A("GH", 8, 8 + G), A("NB", 8, 8 + G), [col("JK", 0)])
+    send("xf", A("X", V, W), A("X", 0, G))
+    fill(A("ASC", V), V); fill(A("X", W), int(DEADX)); fill(A("NB", 0, 8), W); fill(A("NB", 8 + V), W)
+    fill(A("GH", 0, 8), W); fill(A("GH", 8 + G), W); fill(A("Z", V), 0); fill(A("QT", V), 0)
+    iota(A("CD"), [[1, 3], [0, 32]], 1)
+    iota(A("IOF"), [[1, 1472]]); fill(A("YD"), 0); fill(A("DZ0"), 0)
+    for q in range(1, 16): act(A("LQ", 129 * q, 128 * q + 128, 16), A("LT", q, 128, 16), AF.Copy, 0.0, 2048.0)
+
+    def cand_names(t):
+        ts(A("T1"), A("NB", 8 + t, 8 + t + 1276, 5), CEN, AL.subtract)
+        wrap(A("P5", 0, 16), "FE", "T1", 0, 256)
+
+    def cand_terms(t):
+        ts(A("NO"), A("P5", 0, 16), CEN, AL.add)
+        tt(A("EP"), gat("Y", 0, W, A("NO")), A("LV", 256 * t, 256 * t + 256), AL.subtract)
+        ts(A("C1"), A("EP"), 2.0, AL.is_equal, 64.0, AL.mult)
+    def cand_terms1(): act(A("C2"), A("EP"), AF.Abs, col("PC", 5), 32.0)
+    def cand_terms2(): ts(A("P6", 0, 256), A("C2"), -1.0, AL.mult, 31.5, AL.add)
+
+    cand_names(0)
+    for i in range(16): ts(A("SEL", 128 * i, 128 * i + 128), A("BO"), col("QM", i), AL.mult)
+    act(A("SG"), A("SG"), AF.Copy, -0.5)
+    ts(A("DU"), A("ST"), PQ, AL.add, 1440.0, AL.add)
+    ts(A("ST"), A("ST"), PQ, AL.add, 0.5, AL.add)
+    cp(A("RP"), A("RPI"))
+
+    def z_post(j, lo, n):
+        act(A("ZA", lo, lo + n), A("P%d" % j, 0, n), AF.Abs, col("PC", 6), 0.5)
+        if j in (3, 7): later.append((j, lo, n))
+        else: q_keep(j, lo, n)
+    def q_keep(j, lo, n): act(A("QT", lo, lo + n), A("P%d" % j, 0, n), AF.Copy)
+    later = []
+    def z_post2(j, lo, n):
+        ts(A("ZA", lo, lo + n), A("ZA", lo, lo + n), 64.5 / 64, AL.min, 64.5 / 64, AL.subtract)
+        tt(A("Z", lo, lo + n), A("ZA", lo, lo + n), A("P%d" % j, 256, 256 + n), AL.mult)
+    lo = 0; prev = None
+    for k, (j, n) in enumerate(zip(PBANK, PAIRS)):
+        cp(A("GS", 16 * lo, 16 * (lo + n)), gat("Y", 0, W, A("NBU", lo, lo + n)))
+        act(A("GS", 16 * (lo + n), 16 * (lo + 2 * n)), gat("Y", 0, W, A("NBU", lo + n, lo + 2 * n)), AF.Copy)
+        if k == 0: cand_terms(0)
+        if k == 1: cand_terms1()
+        if k == 2: cand_terms2(); cp(A("OA"), A("ASC", 0, 1276, 5))
+        if k == 3: tt(A("LK"), A("LT"), A("N32"), AL.add); cp(A("HH"), A("HS"))
+        if prev: z_post(*prev)
+        mm(A("P%d" % j, 256, 256 + 2 * n), A("ID"), A("Y", lo, lo + 2 * n), True, True)
+        mm(A("P%d" % j, 0, 2 * n), A("NID"), A("Y", lo, lo + 2 * n), True, False)
+        for i in range(16):
+            mm(A("P%d" % j, 0, 2 * n), A("ID"), A("GS", 16 * lo + i, 16 * (lo + 2 * n), 16), False, i == 15)
+        if prev: z_post2(*prev)
+        prev = (j, lo, 2 * n); lo += 2 * n
+    z_post(*prev); z_post2(*prev)
+
+    KEY, XP, KO = A("P0", 0, 192), A("P1", 0, 192), A("P3", 64, 256)
+    def pslab(i): return A("P%d" % (4 + i // 2 % 4), 192 * (i % 2), 192 * (i % 2) + 192)
+    def key_open():
+        mm(KEY, A("KU"), A("ONE", 0, 192), True, False)
+        for i in range(NMAX): mm(KEY, A("FN", 16 - i, 144 - i), A("XB"), False, False)
+    def wrap_t(o, src, alone=True):
+        if not alone: mm(o, A("ZR"), A("ONE", 0, 12), True, False)
+        for e in range(2):
+            for h in range(2):
+                mm(A(o[0], o[1] + e, o[2], 2), A("HH", 256 * e + 128 * h, 256 * e + 128 * h + 128), A(src[0], src[1] + h, src[2], 2),
+                   alone and h == 0, alone and h == 1)
+    def sub_open():
+        for j in range(NPE // 2):
+            mm(A("P%d" % (4 + j), 0, 384), A("ZR"), A("ONE"), True, False)
+            for e in range(2): mm(pslab(2 * j + e), A("NID"), A("XB"), False, False)
+    def distances(names):
+        def gi(i): return A("GS", i, 3072, 16)
+        r0 = 16 - NPE
+        for j in range(NPE): mm(pslab(j), A("ID"), gi(r0 + j), False, j % 2 == 1)
+        for i in range(NMAX): mm(KEY, A("FN", 16 - i, 144 - i), gi(i), False, False)
+        for j in range(NPE // 2): act(slab("DD", r0 + 2 * j, 2), A("P%d" % (4 + j), 0, 384), AF.Abs)
+        for i in range(r0, 16): mm(KEY, A("FA", 16 - i, 144 - i), slab("DD", i), False, False)
+        for i in range(NMAX, r0):
+            tt(slab("DD", i), gi(i), XP, AL.subtract)
+            if i % 2 == 1: act(slab("DD", i - 1, 2), slab("DD", i - 1, 2), AF.Abs)
+        for i in range(NMAX): tt(slab("DD", i), gi(i), XP, AL.max)
+        for e in list(range(NMAX, r0 - 2)) + [0, 1, r0 - 2, r0 - 1] + list(range(2, NMAX)):
+            mm(KEY, A("FB" if e < NMAX else "FA", 16 - e, 144 - e), slab("DD", e), False, False)
+        mm(KEY, A("IDH"), names, False, True)
+
+    parts = [(0, 96, "P0"), (96, 192, "P1"), (192, 256, "P4")]
+    def z_gather(h, nv):
+        c0, c2 = parts[h][:2]; c1 = c0 + nv
+        if c2 > c1: act(A("GS", 16 * c1, 16 * c2), gat("Z", 0, V, A("OA", c1, c2)), AF.Copy)
+        if c1 > c0: cp(A("GS", 16 * c0, 16 * c1), gat("Z", 0, V, A("OA", c0, c1)))
+    def z_sum(h, last=False):
+        c0, c2, pb = parts[h]
+        for j in range(16):
+            mm(A(pb, 0, c2 - c0), A("ID"), A("GS", 16 * c0 + j, 16 * c2, 16), j == 0, last and j == 15)
+
+    for t in range(3):
+        more = t < 2
+        DO, DR, MS = A("DO%d" % t, 0, 2), A("DR%d" % t, 0, 2), "MS%d" % t
+        if t == 0:
+            for h, nv in enumerate([48, 48, 32]):
+                z_gather(h, nv); z_sum(h, True)
+        for c0, c2, pb in parts:
+            act(A("SM", c0, c2), A(pb, 0, c2 - c0), AF.Copy, 192.0)
+            tt(A("T1", c0, c2), A(pb, 0, c2 - c0), A("C1", c0, c2), AL.mult)
+            if c0 > 0:
+                c0 = 0 if c2 < 256 else c0
+                tt(A("T2", c0, c2), A("SM", c0, c2), A("P6", c0, c2), AL.mult)
+                mm(A("P2", c0, c2), A("BO4"), A("C2", c0, c2), True, False)
+                mm(A("P2", c0, c2), A("BOH"), A("T1", c0, c2), False, False)
+                mm(A("P2", c0, c2), A("BO"), A("T2", c0, c2), False, True)
+        if t == 0:
+            for x in later: q_keep(*x)
+        ts(A("WL", 0, 256), A("P2", 0, 256), col("EF", 0), AL.is_le)
+        scan(A("CC"), A("WL"), A("C32"), 0.0, AL.add, AL.min)
+        act(A("JK", 0, 288), A("CC"), AF.Sign, col("ST", 0), -1.0, col("AC", 0))
+        ts(A("JK", 288, 576), A("CC"), col("ST", 1), AL.is_le)
+        add("V", lambda: g.vector.tensor_reduce(R(col("AC", 1)), R(A("JK", 288, 576)), AX.X, AL.add), [col("AC", 1)], [A("JK", 288, 576)])
+        ts(col(DO[0], 0), col("AC", 0), 2.5, AL.mult, 720.0 + t, AL.add)
+        ts(col(DO[0], 1), col("AC", 1), 5.0, AL.mult, float(t), AL.add)
+        send("d%d" % t, DR, DO)
+        if t == 0: fill(A("DZ1"), 0)
+        ts(A("NA", 0, 32), gat("ASC", 0, 1440, DO), -1.0, AL.mult)
+        ts(A("LI", 0, 32), gat("ASC", 0, 1440, DO), 15, AL.bitwise_and)
+        ts(A("NA", 32, 34), DO, -1.0, AL.mult)
+        ts(A("LO", 0, 32), A("LI", 0, 32), P16, AL.add)
+        ts(A("DV", 0, 2), DO, float(V), AL.is_ge, 1440.0, AL.mult)
+        if t > 0: mm(A("P3", 0, 81), A("IDF"), A("CT"), True, False)
+        if more: mm(A("P7", 0, 1), A("O16"), col("CC", 255), True, True)
+        for d in range(32):
+            if d < NSTEP:
+                act(A("SN", 81 * d, 81 * d + 81), A("SG"), AF.Sign, col("NA", d))
+            else:
+                ts(A("SN", 81 * d, 81 * d + 81), A("SJ"), col("NJ", d - NSTEP), AL.is_gt, 2.0, AL.mult)
+            ts(A("OH", 128 * d, 128 * d + 128), A("IP"), col("LO", d), AL.is_equal, 256.0, AL.mult)
+            if d == 0: tt(A("DV", 2, 4), A("DV", 0, 2), A("NA", 32, 34), AL.subtract)
+            if d == 1: cp(A("DX", 0, 2), A("DV", 2, 4))
+            if d == 2:
+                cp(gat("X", 0, 2880, A("DX", 0, 2)), A("CX"))
+                wrap(A("P4", 0, 80), "F1", "X", 0, V)
+            if d == 3: ts(A("NJ", 0, 32 - NSTEP), A("NA", NSTEP, 32), -1.0 / 16, AL.mult, 1.0 / 32, AL.add)
+            if d == 12: act(A("DF", 0, 80), A("P4", 0, 80), AF.Copy)
+            if d % 3 == 0 or d == 31:
+                for e in range(max(d - 2, 0) if d < 31 else d, d + 1):
+                    mm(A("P3", 0, 81), A("OH", 128 * e, 128 * e + 128), A("SN", 81 * e, 81 * e + 81), t == 0 and e == 0, e == 31)
+        tt(A("CS"), A("P3", 0, 80), A("DF", 0, 80), AL.add)
+        tt(A("FL", 0, 80), A("P3", 1, 81), A("CS"), AL.is_gt)
+        scan(A("FS", 1, 93), A("FL"), A("ONE", 0, 92), 0.0, AL.add, AL.mult)
+        mm(A("P5", 0, 92), A("BO"), A("FS", 1, 93), True, True)
+        mm(A("P4", 0, 92), A("BO"), A("FS", 0, 92), True, False)
+        mm(A("P4", 0, 92), A("TRI"), A("FL"), False, True)
+        for c in range(12):
+            act(A("JK", 576 + 92 * c, 668 + 92 * c), A("P5", 0, 92), AF.Sign, col("ST", c), -1.0, col("AC", c))
+        cp(A("CU", 0, 92), A("P4", 0, 92))
+        if t > 0: cp(A("MO"), A("MR%d" % (t - 1), 192, 204))
+        cp(gat("YD", 0, 1440, DO), A("CD", 32 * t, 32 * t + 32))
+        if not more: store("S", T.yd[:], A("YD", 0, V, p=(0, 128, 16)), "s_yd")
+        if t > 0: cp(gat("GH", 8, 1480, A("MO")), A("MR%d" % (t - 1), 0, 192))
+        if t == 1: cp(gat("QT", 0, 1472, A("BU")), A("QN", 0, 192))
+        cp(gat("X", V, 2720, DR), A("CX"))
+        ts(A("HU"), A("AC"), 92.0, AL.add, 0.5, AL.mult)
+        act(A("HB"), A("AC"), AF.Copy, 46.0, 0.5)
+        tt(A("CM"), gat("CU", 0, 92, A("HU")), A("IS"), AL.is_le)
+        mm(A("P6", 0, 12), A("ID16"), A("HB"), True, False)
+        wrap(A("P6", 0, 12), "F1", "CM", 0, 192, False, True)
+        if more:
+            mm(A("P7", 64, 256), A("BO"), A("CM"), True, True)
+            ts(A("DF", 80, 160), A("CU", 0, 80), 192.0, AL.is_gt, 512.0, AL.mult)
+            cp(A("OA"), A("ASC", t + 1, t + 1277, 5))
+        cp(A("BU"), A("P6", 0, 12))
+        B = A("BU")
+        cp(A("LU"), gat("NB", 8, 1480, B))
+        act(A("XB"), gat("X", 0, 1472, B), AF.Copy)
+        mm(XP, A("ID"), A("XB"), True, True)
+        key_open(); sub_open()
+        nu = 80 if more else 96
+        act(A("GS", 16 * nu, 3072), gat("X", 0, W + 16, A("LU", nu, 192)), AF.Copy)
+        ts(A("LH"), A("LU"), CEN, AL.subtract)
+        if more:
+            cp(col("EI", 0), col("P7", 0))
+            ts(A("RG", 0, 192), A("P7", 64, 256), col("PC", 10) if t else PQ, AL.is_equal)
+            ts(col("EI", 1), col("EI", 0), 7, AL.bitwise_and)
+            tt(A("DF", 0, 80), A("FL", 0, 80), A("DF", 80, 160), AL.mult)
+        cp(A("GS", 0, 16 * nu), gat("X", 0, W + 16, A("LU", 0, nu)))
+        distances(A("LH"))
+        def sel_mm(i): mm(pslab(i), A("SEL", 128 * i, 128 * i + 128), A("LH"), True, True)
+        if more:
+            ts(col("EF", 0), col("EI", 1), LOSS0, AL.add)
+            tt(A("RB"), gat("IOF", 0, 1472, B), A("RG", 0, 192), AL.mult)
+        tr(A("TK"), KEY)
+        if more: act(A(MS, 192, 204), A("P6", 0, 12), AF.Copy)
+        act(A("SD"), KEY, AF.Sign, col("PC", 7))
+        wrap(A("P4", 0, 12), "F4", "SD", 0, 192)
+        act(A("ND"), A("P4", 0, 12), AF.Copy, 65536.0 - V)
+        mm(A("P3", 256, 448), A("LK"), A("SD"), True, True)
+        scan(A("TS"), A("RS"), A("TK"), 0.0, AL.add, AL.min)
+        ts(A("KI", 0, 12), A("TS", 15, 192, 16), BIGK, AL.min)
+        ts(A("KI", 16, 28), A("KI", 0, 12), 4095, AL.bitwise_and)
+        ts(A("TC", 0, 12), A("KI", 16, 28), float(V), AL.subtract)
+        wrap_t(A("P2", 256, 268), A("TC", 0, 12))
+        for i in range(2, 6): sel_mm(i)
+        if more:
+            act(A("RG", 192, 384), A("RG", 0, 192), AF.Copy, 1.0, -1.0)
+            act(A("YB"), gat("Y", 0, 1472, B), AF.Copy, 0.0, -1.0)
+        ts(KO, A("P3", 256, 448), col("PC", 3), AL.is_equal)
+        tt(A("UF", 12, 24), A("P2", 256, 268), A("ND"), AL.min)
+        ts(A("AK", 0, 12), A("UF", 12, 24), 8.0, AL.is_ge)
+        ts(A("UO", 0, 12), A("UF", 12, 24), float(V), AL.add, V + 8.0, AL.min)
+        scan(A("AK", 17, 29), A("AK", 0, 12), A("ONE", 0, 12), 0.0, AL.add, AL.mult)
+        mm(A("P2", 272, 284), A("TRI"), A("AK", 0, 12), True, False)
+        mm(A("P2", 272, 284), A("BO"), A("AK", 16, 28), False, True)
+        for i in (6, 7, 0, 1): sel_mm(i)
+        tt(A("KL"), A("LH"), KO, AL.mult)
+        ts(A("UF", 0, 12), A("P2", 272, 284), 32.0, AL.is_gt, 4096.0, AL.mult)
+        tt(A("UF", 0, 12), A("UF", 0, 12), A("UF", 12, 24), AL.add)
+        key_open()
+        ts(A("UO", 12, 24), A("UF", 0, 12), 0.0, AL.max, V + 8.0, AL.min)
+        mm(A("P2", 0, 192), A("BOH"), A("KL"), True, True)
+        if more: wrap(A("P2", 288, 300), "FH", "KL", 0, 192)
+        mm(A("P3", 256, 448), A("KC"), A("ONE", 0, 192), True, False)
+        mm(A("P3", 256, 448), A("IDH"), A("LH"), False, False)
+        mm(A("P3", 256, 448), A("NIH"), A("KL"), False, not more)
+        ts(A("LG"), gat("GH", 0, 1480, A("UO", 12, 24)), float(G), AL.min, float(V), AL.add)
+        tt(A("L2"), gat("NB", 0, 1480, A("UO", 0, 12)), A("LG"), AL.min)
+        cp(A("MU"), A("L2"))
+        nu = 16
+        act(A("GS", 16 * nu, 3072), gat("X", 0, W + 16, A("MU", nu, 192)), AF.Copy)
+        ts(A("MH"), A("MU"), CEN, AL.subtract)
+        tt(slab("EQ", 16), gat("IOF", 0, 1472, B), A("L2"), AL.is_equal)
+        for i in range(16):
+            tt(slab("EQ", i), pslab(i), A("MH"), AL.is_equal)
+            if i % 2 == 1:
+                if i < 8:
+                    sel_mm(i + 7); sel_mm(i + 8)
+                if i == 11: sub_open()
+                for e in ([16] if i == 1 else []) + [i - 1, i]:
+                    mm(KEY, A("IDB"), slab("EQ", e), False, False)
+        tr(A("TK"), A("P2", 0, 192))
+        if more: ts(A("OO"), A("P2", 288, 300), CEN, AL.add)
+        cp(A("GS", 0, 16 * nu), gat("X", 0, W + 16, A("MU", 0, nu)))
+        ts(A("FK"), A("TK", 15, 192, 16), BIGK + CEN + 8, AL.add)
+        if more: act(A("YO"), gat("Y", 0, W + 16, A("OO")), AF.Copy)
+        distances(A("MH"))
+        if more: tt(A("QP"), gat("QT", 0, 1472, B), A("YO"), AL.subtract)
+        tr(A("TK"), KEY)
+        scan(A("TS"), A("RS"), A("TK"), 0.0, AL.add, AL.min)
+        tt(A("KI", 0, 12), A("TS", 15, 192, 16), A("FK"), AL.min)
+        ts(A("KI", 16, 28), A("KI", 0, 12), 4095, AL.bitwise_and)
+        if more:
+            ts(A("TC", 0, 12), A("KI", 16, 28), CEN + 8, AL.subtract)
+            wrap_t(A("P1", 256, 268), A("TC", 0, 12))
+            ts(A("KF", 0, 12), A("KI", 0, 12), BIGK, AL.is_ge, 4096.0, AL.mult)
+        ts(A("TH"), gat("KI", 16, 28, A("RP")), CEN + 8, AL.subtract)
+        if not more:
+            tr(A("WR", 0, 192), A("TH"))
+            tt(A("LF"), A("WR", 0, 192), KO, AL.mult)
+            tt(A(MS, 0, 192), A("LF"), A("P3", 256, 448), AL.add)
+            cp(gat("NB", 8, 1480, B), A(MS, 0, 192))
+            store("S", T.yn[:, 0:640], A("NB", 8, 648), "s_y0")
+            store("A", T.yn[:, 640:V], A("NB", 648, 8 + V), "s_y1")
+            break
+        ts(A("WO", 0, 12), A("P1", 256, 268), CEN, AL.add)
+        tr(A("WR", 0, 192), A("TH"))
+        tt(A("QN", 0, 192), gat("Y", 0, W + 16, A("WO", 0, 12)), A("QP"), AL.add)
+        act(A("QN", 192, 384), A("QN", 0, 192), AF.Abs, col("PC", 6), 0.5)
+        act(A("QN", 192, 384), A("QN", 192, 384), AF.Relu, col("PC", 11), -1.0)
+        tt(A("TH"), A("WR", 0, 192), KO, AL.mult)
+        mm(A("P3", 256, 448), A("IDH"), A("TH"), False, True)
+        act(A(MS, 0, 192), A("P3", 256, 448), AF.Copy)
+        send("u%d" % t, A("MR%d" % t), A(MS))
+        tt(A("KF", 16, 28), A("KF", 0, 12), A("KI", 16, 28), AL.add)
+        ts(A("KF", 0, 12), A("KF", 16, 28), V + 8.0, AL.is_ge, 4096.0, AL.mult)
+        tt(A("KF", 16, 28), A("KF", 0, 12), A("KF", 16, 28), AL.add)
+        tt(gat("Z", 0, 1472, B), A("QN", 192, 384), A("YB"), AL.mult)
+        z_gather(0, 0)
+        ts(A("TC", 16, 28), A("KF", 16, 28), 8.0, AL.subtract, 2000.0, AL.min)
+        wrap_t(A("P2", 304, 316), A("TC", 16, 28))
+        wrap_t(A("P7", 0, 12), A("TC", 16, 28), False)
+        ts(A("MH"), gat("KF", 16, 28, A("RP")), 8.0, AL.subtract, 2000.0, AL.min)
+        cp(A("WF", 0, 12), A("P2", 304, 316))
+        tr(A("WR", 192, 384), A("MH"))
+        ts(A("WO", 12, 24), A("P2", 304, 316), 1440.0, AL.min)
+        mm(A("P5", 0, 192), A("ZR"), A("ONE", 0, 192), True, False)
+        for c in range(12):
+            ts(A("EE", 208 * c, 192 * (c + 1)), A("WR", 192 + 16 * c, 384), col("WF", c), AL.is_equal)
+            if c < 11: mm(A("P5", 16 * (c + 1), 192), A("BO"), A("EE", 208 * c + 16, 192 * (c + 1)), False, c == 10)
+        act(A("LS"), A("P5", 0, 192), AF.Sign)
+        for q in range(1, 16):
+            mm(A("P7", 0, 12), A("LQ", 128 * q, 128 * q + 128), A("EE", q, 2304, 208), False, False)
+        tt(A("TH"), gat("ASC", 0, 1632, A("WO", 12, 24)), A("RG", 0, 192), AL.mult)
+        wrap(A("P2", 288, 300), "FH", "TH", 0, 192)
+        wrap(A("P7", 0, 12), "FA", "LS", 0, 192, False, True)
+        cp(gat("NB", 8, 1480, B), A(MS, 0, 192))
+        cp(A("OO"), A("P2", 288, 300))
+        cand_names(t + 1)
+        act(A("YO"), gat("Z", 0, 1472, B), AF.Copy)
+        act(A("QP"), gat("Z", 0, 1472, A("OO")), AF.Copy, 0.0, -1.0)
+        tt(A("MH"), gat("ASC", 0, 1632, A("WO", 12, 24)), A("RG", 192, 384), AL.mult)
+        mm(A("P2", 0, 192), A("IDH"), A("RB"), True, False)
+        mm(A("P2", 0, 192), A("IDH"), A("MH"), False, True)
+        z_sum(0)
+        z_gather(1, 0)
+        tt(A("WF", 12, 24), A("P7", 0, 12), A("DU"), AL.min)
+        cand_terms(t + 1)
+        cp(A("WS"), A("WF", 12, 24))
+        act(A("L2"), A("P2", 0, 192), AF.Copy)
+        cand_terms1()
+        tt(gat("DZ%d" % t, 0, 1632, A("WS")), A("YO"), A("QP"), AL.add)
+        z_gather(2, NLAST)
+        z_sum(1)
+        for h, (c0, c2, pb) in enumerate(parts):
+            if h == 2: z_sum(2)
+            mm(A(pb, 0, c2 - c0), A("ID"), A("DZ%d" % t, t + 1 + 5 * c0, t + 1 + 5 * c2 - 4, 5), False, True)
+        cand_terms2()
+        cp(gat("ASC", 0, 1632, A("WS")), A("L2"))
+        scan(A("CT", 1, 81), A("DF", 0, 80), A("ONE", 0, 80), 0.0, AL.add, AL.mult)
+
+    emit_all(ops, Q, T)
+
+
+def emit_all(ops, Q, T):
+    hist = {}
+    deps = []
+    for n, (q, emit, rd, wr, token) in enumerate(ops):
+        d = set()
+        for a, w in [(a, False) for a in rd] + [(a, True) for a in wr]:
+            bank = a[0] not in SB
+            for m, lo, hi, w2 in hist.get(a[0], ()):
+                same = ops[m][0] == q and ops[m][4] is None and token is None
+                meet = lo < a[2] and a[1] < hi
+                if same:
+                    if meet and q != "P" and w2: d.add(m)
+                elif bank or (meet and (w or w2)): d.add(m)
+        d.discard(n)
+        deps.append(d)
+        for a, w in [(a, False) for a in rd] + [(a, True) for a in wr]:
+            hist.setdefault(a[0], []).append((n, a[1], a[2], w))
+    know = {q: ({}, set()) for q in Q}
+    after = {}
+    waits = []
+    for n, (q, emit, rd, wr, token) in enumerate(ops):
+        if q == "X":
+            after[n] = ({}, {n}); waits.append([]); continue
+        kq, kd = know[q]
+        ws = []
+        for m in sorted(deps[n], reverse=True):
+            if ops[m][4] is None:
+                if kq.get(ops[m][0], -1) >= m: continue
+            elif m in kd: continue
+            ws.append(m)
+            for e, v in after[m][0].items(): kq[e] = max(kq.get(e, -1), v)
+            kd |= after[m][1]
+        waits.append(ws)
+        a0, a1 = dict(kq), set(kd)
+        if token is None: a0[q] = n
+        else: a1.add(n)
+        after[n] = (a0, a1)
+    needed = set(m for ws in waits for m in ws)
+    count = {}; tok = {}
+    for n, (q, emit, rd, wr, token) in enumerate(ops):
+        if token is not None: tok[n] = token
+        elif n in needed:
+            count[q] = count.get(q, 0) + 1; tok[n] = ("q" + q, count[q])
+    for n, (q, emit, rd, wr, token) in enumerate(ops):
+        if q == "X": continue
+        for m in waits[n]: Q[q].wait_ge(T.sem[tok[m][0]], tok[m][1])
+        ins = emit()
+        if token is None and n in needed: ins.then_inc(T.sem[tok[n][0]], 1)
+    for n, (q, emit, rd, wr, token) in enumerate(ops):
+        if token is not None and n not in needed: Q["S"].wait_ge(T.sem[token[0]], token[1])

@@ -3,45 +3,52 @@ from concourse.mybir import AluOpType as AL, ActivationFunctionType as AF, AxisL
 V, G, W = 1280, 1056, 2336
 CEN = 1168.0
 BIGK = 4096.0 * 4000
+RND = 1.5 * 2 ** 35
 DEADX = 131072.0
 LOSS0 = 192 * 31.5 * 16
 PAIRS = [128, 128, 128, 112, 72, 40, 32]
 PBANK = [0, 1, 4, 0, 2, 3, 7]
-NLAST = 16
 NSTEP = 28
-NMAX, NPE = 6, 4
+NEAR = ([(0, 48, "V"), (48, 96, "A"), (96, 144, "V"), (144, 192, "A")], [(0, 96, "abs", [3, 4, 5, 6]), (96, 192, "max", [])])
+OFFER = ([(0, 64, "A"), (64, 128, "A"), (128, 176, "A"), (176, 192, "V")], [(0, 64, "abs", [3, 4]), (64, 128, "max", []), (128, 192, "max", [])])
+EQB = [5, 6, 7]
+ZG0 = [(0, 48, "V"), (48, 96, "A"), (96, 144, "V"), (144, 192, "A"), (192, 224, "V"), (224, 256, "A")]
+ZG1 = [(0, 48, "A"), (48, 96, "A"), (96, 144, "A"), (144, 192, "A"), (192, 224, "V"), (224, 256, "V")]
 
 SB = {
-    "NBI": (1280, "int32"), "NBU": (1280, "uint16"), "NB": (1480, "float32"), "GH": (1480, "float32"),
+    "NBI": (1280, "int32"), "NBU": (1280, "uint16"), "NB": (2760, "float32"), "NBC": (1056, "float32"),
     "ASC": (1632, "int32"), "X": (2880, "bfloat16"), "Y": (2352, "bfloat16"), "GS": (20480, "bfloat16"),
     "Z": (1472, "bfloat16"), "QT": (1472, "bfloat16"), "ZA": (1280, "bfloat16"), "YD": (1440, "float32"),
-    "ONE": (384, "bfloat16"), "BO": (128, "bfloat16"), "ID": (128, "bfloat16"), "NID": (128, "bfloat16"), "ZR": (128, "bfloat16"),
+    "ONE": (384, "bfloat16"), "BO": (128, "bfloat16"), "BN": (128, "bfloat16"), "ID": (128, "bfloat16"), "NID": (128, "bfloat16"), "ZR": (128, "bfloat16"),
     "ID16": (128, "bfloat16"), "IDB": (128, "bfloat16"), "IDF": (128, "float32"), "IDH": (128, "float16"), "NIH": (128, "float16"),
-    "BOH": (128, "float16"), "BO4": (128, "bfloat16"), "TRI": (128, "bfloat16"), "LK": (128, "bfloat16"), "N32": (128, "bfloat16"),
-    "O16": (128, "bfloat16"), "SEL": (2048, "float16"), "QM": (16, "float32"),
+    "BOH": (128, "float16"), "BO4": (128, "bfloat16"), "TRI": (128, "bfloat16"), "TRA": (128, "bfloat16"), "I256": (128, "bfloat16"),
+    "LK": (128, "bfloat16"), "N32": (128, "bfloat16"), "I192": (128, "bfloat16"),
+    "O16": (128, "bfloat16"), "SEL": (2048, "float16"), "SELB": (2048, "bfloat16"), "QM": (16, "float32"), "QB": (16, "float32"),
     "F1": (144, "bfloat16"), "FA": (144, "bfloat16"), "FB": (144, "bfloat16"), "FN": (144, "bfloat16"),
-    "FH": (144, "float16"), "FW": (144, "float16"), "FE": (144, "float16"),
-    "KU": (128, "bfloat16"), "KC": (128, "bfloat16"), "KN": (128, "bfloat16"), "KT": (192, "float32"),
+    "FH": (144, "float16"), "FE": (144, "float16"),
+    "KU": (128, "bfloat16"), "KC": (128, "bfloat16"), "KT": (192, "float32"),
     "PI": (8, "int32"), "PC": (16, "float32"), "IP": (128, "bfloat16"), "IS": (192, "bfloat16"), "IOF": (1472, "float32"),
-    "SG": (81, "float32"), "SJ": (81, "bfloat16"), "ST": (12, "float32"), "DU": (12, "float32"),
-    "RS": (192, "float32"), "TM": (192, "float16"), "RPI": (12, "int32"), "RP": (12, "uint16"), "C32": (288, "bfloat16"),
+    "SG": (81, "float32"), "SJ": (81, "bfloat16"), "ST": (12, "float32"), "DU": (12, "float32"), "SEG": (12, "float32"),
+    "RS1": (192, "float32"), "RS2": (192, "float32"), "RPI": (12, "int32"), "RP": (12, "uint16"), "C32": (288, "bfloat16"),
     "CX": (32, "bfloat16"), "CD": (96, "float32"), "JK": (1680, "bfloat16"), "HM": (256, "bfloat16"), "HS": (512, "bfloat16"), "HH": (512, "float16"),
-    "TC": (32, "float16"), "F4": (144, "bfloat16"), "ND": (12, "float32"), "AK": (32, "bfloat16"),
+    "TC": (64, "float16"), "F4": (144, "bfloat16"), "ND": (12, "float32"), "AK": (32, "bfloat16"), "DP": (48, "bfloat16"),
     "OA": (256, "uint16"), "NO": (16, "uint16"), "EP": (256, "bfloat16"), "C1": (256, "bfloat16"), "C2": (256, "bfloat16"),
-    "SM": (256, "bfloat16"), "T1": (256, "float16"), "T2": (256, "bfloat16"), "WL": (288, "bfloat16"), "CC": (288, "bfloat16"),
-    "EI": (8, "int32"), "EF": (8, "float32"), "AC": (12, "float32"), "DV": (8, "float32"), "DX": (8, "uint16"),
+    "SM": (256, "bfloat16"), "T1": (256, "float16"), "TN": (256, "float16"), "T2": (256, "bfloat16"), "WL": (288, "bfloat16"), "CC": (288, "bfloat16"),
+    "EI": (8, "int32"), "EF": (8, "float32"), "AC": (12, "float32"), "AD": (8, "float32"), "DV": (8, "float32"), "DX": (8, "uint16"),
     "DO0": (8, "uint16"), "DO1": (8, "uint16"), "DO2": (8, "uint16"), "DR0": (8, "uint16"), "DR1": (8, "uint16"), "DR2": (8, "uint16"),
     "NA": (34, "float32"), "NJ": (8, "float32"), "LI": (34, "int32"), "LO": (34, "float32"), "OH": (34 * 128, "bfloat16"), "SN": (34 * 81, "bfloat16"),
-    "CS": (80, "float32"), "FL": (92, "bfloat16"), "FS": (93, "bfloat16"), "CU": (96, "float32"), "DF": (160, "float32"), "CT": (81, "float32"),
+    "CS": (80, "float32"), "FL": (92, "bfloat16"), "FS": (93, "bfloat16"), "CU": (96, "float32"), "DF": (160, "float32"), "DG": (80, "float32"), "CT": (81, "float32"),
     "HU": (12, "uint16"), "HB": (12, "bfloat16"), "CM": (192, "bfloat16"), "BU": (12, "uint16"),
-    "LU": (192, "uint16"), "LH": (192, "float16"), "LF": (192, "float32"), "XB": (192, "bfloat16"), "DD": (3072, "bfloat16"), "EQ": (17 * 192, "bfloat16"),
-    "TK": (192, "float32"), "TS": (192, "float32"), "KI": (32, "int32"), "KF": (32, "float32"), "TH": (192, "float16"), "UR": (576, "float16"),
-    "SD": (192, "bfloat16"), "KL": (192, "float16"), "FK": (12, "float32"), "UO": (24, "uint16"), "UF": (24, "float32"),
-    "LG": (192, "float32"), "L2": (192, "float32"), "MU": (192, "uint16"), "MH": (192, "float16"),
-    "OO": (12, "uint16"), "QP": (192, "bfloat16"), "YO": (192, "bfloat16"), "YB": (192, "bfloat16"), "RG": (384, "float32"), "RB": (192, "float16"), "LQ": (2048, "bfloat16"), "LV": (768, "bfloat16"),
+    "LU": (192, "uint16"), "LH": (192, "float16"), "LF": (192, "float32"), "LW": (192, "float32"), "XB": (192, "bfloat16"), "DD": (3072, "bfloat16"), "EQ": (17 * 192, "bfloat16"),
+    "TK": (192, "float32"), "TF": (192, "float32"), "TS": (192, "float32"), "KR": (32, "float32"), "KN": (16, "float32"), "TH": (192, "float16"), "TW": (192, "float16"), "TA": (192, "float16"),
+    "SD": (192, "bfloat16"), "KL": (192, "float16"), "UO": (12, "uint16"), "UF": (12, "float32"),
+    "L2": (192, "float32"), "MU": (192, "uint16"), "MH": (192, "float16"), "MA": (192, "float16"), "BH": (192, "float16"),
+    "OO": (12, "uint16"), "OZ": (12, "uint16"), "QP": (192, "bfloat16"), "YO": (192, "bfloat16"), "ZN": (192, "bfloat16"), "ZO": (192, "bfloat16"), "YB": (192, "bfloat16"),
+    "FZ": (384, "bfloat16"), "ZC": (192, "bfloat16"), "ZS": (192, "bfloat16"), "ZW": (192, "bfloat16"),
+    "RG": (384, "float32"), "RB": (192, "float16"), "LQ": (2048, "bfloat16"), "LV": (768, "bfloat16"),
     "DZ0": (1632, "bfloat16"), "DZ1": (1632, "bfloat16"), "WS": (12, "uint16"), "LT": (128, "bfloat16"),
-    "WR": (576, "float16"), "WO": (24, "uint16"), "WF": (48, "float32"), "QN": (384, "bfloat16"), "EE": (12 * 192, "bfloat16"), "LS": (192, "bfloat16"),
-    "MS0": (204, "float32"), "MS1": (204, "float32"), "MS2": (204, "float32"), "MR0": (204, "float32"), "MR1": (204, "float32"), "MO": (12, "uint16"),
+    "WR": (192, "float16"), "WO": (24, "uint16"), "WF": (48, "float32"), "QN": (192, "bfloat16"), "EE": (12 * 192, "bfloat16"), "LS": (192, "bfloat16"),
+    "MS": (192, "float32"), "MC0": (204, "float32"), "MC1": (204, "float32"), "MR0": (204, "float32"), "MR1": (204, "float32"), "MO": (12, "uint16"),
 }
 PLACE = {}
 SCRATCH = {}
@@ -83,13 +90,13 @@ def rank_program(g, core, T, topo):
         r = T[nm][ps, at + a[1]:at + a[2]:a[3]] if a[3] else T[nm][ps, at + a[1]:at + a[2]]
         return r.indirect(R(a[5])) if a[5] else r
 
-    def add(q, emit, outs, ins, token=None):
+    def add(q, emit, outs, ins, token=None, kind=None):
         rd = [a for a in ins if isinstance(a, tuple)]
         rd = rd + [a[5] for a in rd + outs if a[5]]
-        ops.append([q, emit, rd, outs, token])
+        ops.append([q, emit, rd, outs, token, call_time(q, kind, outs, ins), kind])
 
     def cp(o, i): add("V", lambda: g.vector.tensor_copy(R(o), R(i)), [o], [i])
-    def tt(o, a, b, op): add("V", lambda: g.vector.tensor_tensor(R(o), R(a), R(b), op), [o], [a, b])
+    def tt(o, a, b, op): add("V", lambda: g.vector.tensor_tensor(R(o), R(a), R(b), op), [o], [a, b], None, "tt")
     def ts(o, a, s1, op0, s2=None, op1=None):
         if op1 is None:
             add("V", lambda: g.vector.tensor_scalar(R(o), R(a), R(s1), None, op0), [o], [a, s1])
@@ -100,10 +107,11 @@ def rank_program(g, core, T, topo):
     def ms(o, c): add("V", lambda: g.vector.memset(R(o), c), [o], [])
     def act(o, i, f, bias=0.0, scale=1.0, acc=None):
         if acc is None:
-            add("A", lambda: g.scalar.activation(R(o), R(i), f, bias=R(bias), scale=scale), [o], [i, bias])
+            add("A", lambda: g.scalar.activation(R(o), R(i), f, bias=R(bias), scale=R(scale)), [o], [i, bias, scale])
         else:
             add("A", lambda: g.scalar.activation(R(o), R(i), f, bias=R(bias), scale=scale, accum_out=R(acc)), [o, acc], [i, bias])
-    def mm(o, l, r, start, stop): add("P", lambda: g.tensor.matmul(R(o), R(l), R(r), start, stop), [o], [l, r])
+    def mm(o, l, r, start, stop):
+        add("P", lambda: g.tensor.matmul(R(o), R(l), R(r), start, stop), [o], [l, r], None, None if start or stop else "mid")
     def iota(o, pat, base=0, cm=0):
         if SB[o[0]][1] == "int32":
             add("G", lambda: g.iota(R(o), pat, base, cm), [o], [])
@@ -111,24 +119,24 @@ def rank_program(g, core, T, topo):
             add("G", lambda: g.iota(R(o), pat, base, cm, allow_small_or_imprecise_dtypes=True), [o], [])
     def fill(o, c): iota(o, [[0, o[2] - o[1]]], c)
     def sel(o, i, pat, op, base, cm): add("G", lambda: g.affine_select(R(o), R(i), pat, op, 0.0, base, cm), [o], [i])
-    def load(q, o, src, sem): add(q, lambda: Q[q].dma_start(R(o), src).then_inc(T.sem[sem], 16), [o], [], (sem, 16))
-    def store(q, d, i, sem): add(q, lambda: Q[q].dma_start(d, R(i)).then_inc(T.sem[sem], 16), [], [i], (sem, 16))
+    def load(q, o, src, sem): add(q, lambda: Q[q].dma_start(R(o), src).then_inc(T.sem[sem], 16), [o], [], (sem, 16), "dma")
+    def store(q, d, i, sem): add(q, lambda: Q[q].dma_start(d, R(i)).then_inc(T.sem[sem], 16), [], [i], (sem, 16), "dma")
     def send(m, o, i, after=()):
-        add("G", lambda: g.remote_dma(R(o), R(i), T.sem["r_" + m], T.sem["w_" + m], pid, rid, mask), list(after), [i], ("w_" + m, ne))
-    def recv(m, o): add("X", None, [o], [], ("r_" + m, ne))
+        add("G", lambda: g.remote_dma(R(o), R(i), T.sem["r_" + m], T.sem["w_" + m], pid, rid, mask), list(after), [i], ("w_" + m, ne), "send")
+        add("X", None, [o], [], ("r_" + m, ne), "wait")
     def wrap(o, f, buf, lo, n, first=True, last=True):
         for q in range(16):
             mm(o, A(f, 16 - q, 144 - q), A(buf, lo + q, lo + n, 16), first and q == 0, last and q == 15)
     def col(name, c): return A(name, c, c + 1)
     def gat(name, lo, hi, off): return A(name, lo, hi, ind=off)
     def slab(name, i, n=1): return A(name, 192 * i, 192 * (i + n))
+    def fetch(q, o, i):
+        if q == "V": cp(o, i)
+        else: act(o, i, AF.Copy)
     PQ, P16 = col("PC", 0), col("PC", 1)
 
     load("S", A("Y", 0, V), T.lab[:], "l_lab")
-    load("A", A("NBI"), T.nb[:], "l_nb")
-    recv("lab", A("Y", V, W)); recv("xf", A("X", V, W)); recv("nb", A("GH", 8, 8 + G))
-    for t in range(3): recv("d%d" % t, A("DR%d" % t, 0, 2))
-    for t in range(2): recv("u%d" % t, A("MR%d" % t))
+    load("S", A("NBI"), T.nb[:], "l_nb")
     iota(col("PI", 0), [[0, 1]], 0, 1)
     ms(A("ONE"), 1.0)
     iota(A("KT"), [[0, 12], [1, 16]])
@@ -146,8 +154,10 @@ def rank_program(g, core, T, topo):
     tt(P16, col("PI", 0), col("PI", 1), AL.subtract)
     ms(A("FL", 80), 1.0); ms(col("FS", 0), 0.0); ms(col("CT", 0), 0.0); ms(A("O16"), 1.0 / 16); ms(col("EF", 0), LOSS0)
     ms(col("PC", 5), 31.5); ms(col("PC", 6), -31.5 / 64); ms(col("PC", 7), -1.6e7)
+    ms(col("PC", 12), 0.5 / 64); ms(col("PC", 13), -63.5 / 64)
     ts(A("QM"), A("KT", 0, 16), PQ, AL.is_equal)
-    ts(A("RS"), A("KT"), 0.0, AL.is_equal, 2.0 ** 26, AL.mult)
+    ts(A("QB"), A("QM"), 2.0 ** 25, AL.mult)
+    ms(A("RS1"), -1e9); ms(A("RS2"), -1e9); ms(A("RS1", 0, 192, 16), BIGK - CEN - 8)
     ms(col("PC", 11), 64.5 / 64)
     ts(col("PC", 8), PQ, 1.0, AL.is_lt, 16.0, AL.mult)
     ts(col("PC", 10), col("PC", 8), PQ, AL.add, -1.0, AL.add)
@@ -156,15 +166,17 @@ def rank_program(g, core, T, topo):
     cp(A("FH", 16, 144, 16), A("BO", 0, 128, 16))
     for f, c in [("F1", 1.0), ("FA", 65536.0), ("FB", 131072.0), ("FN", -65536.0), ("F4", 4096.0)]:
         act(A(f, 16, 144, 16), A("BO", 0, 128, 16), AF.Copy, 0.0, c)
-    for f, s, c in [("NID", "ID", -1.0), ("ID16", "ID", 16.0), ("IDB", "ID", 2.0 ** 25), ("IDF", "ID", 1.0), ("N32", "ID", -32.0), ("BO4", "BO", 192.0)]:
+    for f, s, c in [("NID", "ID", -1.0), ("ID16", "ID", 16.0), ("IDB", "ID", 2.0 ** 25), ("IDF", "ID", 1.0), ("N32", "ID", -32.0), ("BO4", "BO", 192.0),
+                    ("BN", "BO", -65536.0), ("I192", "ID", 192.0), ("I256", "ID", 256.0)]:
         act(A(f), A(s), AF.Copy, 0.0, c)
     act(A("KU", p=(0, 1)), A("KT", 0, 128, p=(0, 1)), AF.Copy, 0.0, 4096.0)
-    ms(A("KU", p=(32, 33)), CEN + 8); ms(A("KC", p=(0, 1)), CEN)
+    ms(A("KC", p=(0, 1)), CEN)
     cp(A("BOH"), A("BO")); cp(A("IDH"), A("ID")); ts(A("NIH"), A("ID"), -1.0, AL.mult)
     for t in range(3): act(A("LV", 256 * t, 256 * t + 256), A("Y", t, t + 1276, 5), AF.Copy)
     ms(A("LQ"), 0.0)
-    cp(A("NBU"), A("NBI"))
+    cp(A("NBU", 0, 256), A("NBI", 0, 256)); cp(A("NBU", 256), A("NBI", 256))
     cp(A("NB", 8, 8 + V), A("NBI"))
+    ts(A("NBC"), A("NBI", 0, G), float(G), AL.min, float(V), AL.add)
     iota(A("IP"), [[1, 128]]); iota(A("IS"), [[1, 192]]); iota(A("SG"), [[16, 81]]); iota(A("SJ"), [[1, 81]])
     iota(A("ST"), [[16, 12]]); iota(A("RPI"), [[1, 12]])
     sel(A("TRI"), A("BO"), [[1, 128]], AL.is_ge, 0, -1)
@@ -173,104 +185,109 @@ def rank_program(g, core, T, topo):
     for e in range(2):
         for h in range(2):
             sel(A("HS", 256 * e + 128 * h, 256 * e + 128 * h + 128), A("HM", 128 * h, 128 * h + 128), [[-1, 128]], AL.is_equal, 16 * (h - e), 1)
-    send("nb", A("GH", 8, 8 + G), A("NB", 8, 8 + G), [col("JK", 0)])
     send("xf", A("X", V, W), A("X", 0, G))
-    fill(A("ASC", V), V); fill(A("X", W), int(DEADX)); fill(A("NB", 0, 8), W); fill(A("NB", 8 + V), W)
-    fill(A("GH", 0, 8), W); fill(A("GH", 8 + G), W); fill(A("Z", V), 0); fill(A("QT", V), 0)
+    send("nb", A("NB", 8 + V, 8 + W), A("NBC"), [col("JK", 0)])
+    fill(A("ASC", V), V); fill(A("X", W), int(DEADX)); fill(A("NB", 0, 8), W); fill(A("NB", 8 + W), W)
+    fill(A("Z", V), 0); fill(A("QT", V), 0)
     iota(A("CD"), [[1, 3], [0, 32]], 1)
-    iota(A("IOF"), [[1, 1472]]); fill(A("YD"), 0); fill(A("DZ0"), 0)
+    iota(A("IOF"), [[1, 1472]]); fill(A("YD"), 0); fill(A("DZ0"), 0); fill(A("DZ1"), 0)
     for q in range(1, 16): act(A("LQ", 129 * q, 128 * q + 128, 16), A("LT", q, 128, 16), AF.Copy, 0.0, 2048.0)
 
-    def cand_names(t):
-        ts(A("T1"), A("NB", 8 + t, 8 + t + 1276, 5), CEN, AL.subtract)
-        wrap(A("P5", 0, 16), "FE", "T1", 0, 256)
-
     def cand_terms(t):
+        ts(A("TN"), A("NB", 8 + t, 8 + t + 1276, 5), CEN, AL.subtract)
+        wrap(A("P5", 0, 16), "FE", "TN", 0, 256)
         ts(A("NO"), A("P5", 0, 16), CEN, AL.add)
         tt(A("EP"), gat("Y", 0, W, A("NO")), A("LV", 256 * t, 256 * t + 256), AL.subtract)
         ts(A("C1"), A("EP"), 2.0, AL.is_equal, 64.0, AL.mult)
-    def cand_terms1(): act(A("C2"), A("EP"), AF.Abs, col("PC", 5), 32.0)
-    def cand_terms2(): ts(A("P6", 0, 256), A("C2"), -1.0, AL.mult, 31.5, AL.add)
+        act(A("C2"), A("EP"), AF.Abs, col("PC", 5), 32.0)
+        ts(A("P6", 0, 256), A("C2"), -1.0, AL.mult, 31.5, AL.add)
 
-    cand_names(0)
-    for i in range(16): ts(A("SEL", 128 * i, 128 * i + 128), A("BO"), col("QM", i), AL.mult)
+    cand_terms(0)
+    for i in range(16):
+        ts(A("SEL", 128 * i, 128 * i + 128), A("BO"), col("QM", i), AL.mult)
+        act(A("SELB", 128 * i, 128 * i + 128), A("BO"), AF.Copy, 0.0, col("QB", i))
     act(A("SG"), A("SG"), AF.Copy, -0.5)
-    ts(A("DU"), A("ST"), PQ, AL.add, 1440.0, AL.add)
+    ts(A("DU"), A("ST"), PQ, AL.add, 1440.0 - CEN, AL.add)
+    ts(A("SEG"), A("ST"), 256.0, AL.mult, BIGK, AL.add)
     ts(A("ST"), A("ST"), PQ, AL.add, 0.5, AL.add)
     cp(A("RP"), A("RPI"))
+    cp(A("OA"), A("ASC", 0, 1276, 5))
+    tt(A("LK"), A("LT"), A("N32"), AL.add); tt(A("TRA"), A("TRI"), A("I192"), AL.add); cp(A("HH"), A("HS"))
 
-    def z_post(j, lo, n):
-        act(A("ZA", lo, lo + n), A("P%d" % j, 0, n), AF.Abs, col("PC", 6), 0.5)
-        if j in (3, 7): later.append((j, lo, n))
-        else: q_keep(j, lo, n)
-    def q_keep(j, lo, n): act(A("QT", lo, lo + n), A("P%d" % j, 0, n), AF.Copy)
-    later = []
-    def z_post2(j, lo, n):
-        ts(A("ZA", lo, lo + n), A("ZA", lo, lo + n), 64.5 / 64, AL.min, 64.5 / 64, AL.subtract)
-        tt(A("Z", lo, lo + n), A("ZA", lo, lo + n), A("P%d" % j, 256, 256 + n), AL.mult)
-    lo = 0; prev = None
-    for k, (j, n) in enumerate(zip(PBANK, PAIRS)):
+    lo = 0; later = []
+    for j, n in zip(PBANK, PAIRS):
+        pb = "P%d" % j
         cp(A("GS", 16 * lo, 16 * (lo + n)), gat("Y", 0, W, A("NBU", lo, lo + n)))
         act(A("GS", 16 * (lo + n), 16 * (lo + 2 * n)), gat("Y", 0, W, A("NBU", lo + n, lo + 2 * n)), AF.Copy)
-        if k == 0: cand_terms(0)
-        if k == 1: cand_terms1()
-        if k == 2: cand_terms2(); cp(A("OA"), A("ASC", 0, 1276, 5))
-        if k == 3: tt(A("LK"), A("LT"), A("N32"), AL.add); cp(A("HH"), A("HS"))
-        if prev: z_post(*prev)
-        mm(A("P%d" % j, 256, 256 + 2 * n), A("ID"), A("Y", lo, lo + 2 * n), True, True)
-        mm(A("P%d" % j, 0, 2 * n), A("NID"), A("Y", lo, lo + 2 * n), True, False)
+        n = 2 * n
+        mm(A(pb, 256, 256 + n), A("ID"), A("Y", lo, lo + n), True, True)
+        mm(A(pb, 0, n), A("NID"), A("Y", lo, lo + n), True, False)
         for i in range(16):
-            mm(A("P%d" % j, 0, 2 * n), A("ID"), A("GS", 16 * lo + i, 16 * (lo + 2 * n), 16), False, i == 15)
-        if prev: z_post2(*prev)
-        prev = (j, lo, 2 * n); lo += 2 * n
-    z_post(*prev); z_post2(*prev)
+            mm(A(pb, 0, n), A("ID"), A("GS", 16 * lo + i, 16 * (lo + n), 16), False, i == 15)
+        act(A("ZA", lo, lo + n), A(pb, 0, n), AF.Abs, col("PC", 6), 0.5)
+        if j in (3, 7): later.append((A("QT", lo, lo + n), A(pb, 0, n)))
+        else: act(A("QT", lo, lo + n), A(pb, 0, n), AF.Copy)
+        ts(A("ZA", lo, lo + n), A("ZA", lo, lo + n), 64.5 / 64, AL.min, 64.5 / 64, AL.subtract)
+        tt(A("Z", lo, lo + n), A("ZA", lo, lo + n), A(pb, 256, 256 + n), AL.mult)
+        lo += n
+    for o, i in later: act(o, i, AF.Copy)
 
-    KEY, XP, KO = A("P0", 0, 192), A("P1", 0, 192), A("P3", 64, 256)
-    def pslab(i): return A("P%d" % (4 + i // 2 % 4), 192 * (i % 2), 192 * (i % 2) + 192)
-    def key_open():
-        mm(KEY, A("KU"), A("ONE", 0, 192), True, False)
-        for i in range(NMAX): mm(KEY, A("FN", 16 - i, 144 - i), A("XB"), False, False)
-    def wrap_t(o, src, alone=True):
-        if not alone: mm(o, A("ZR"), A("ONE", 0, 12), True, False)
+    KEY, XP, KO = A("P0", 0, 192), A("P1", 0, 192), A("P1", 192, 384)
+    def wrap_t(o, src, first=True, last=True):
+        if first: mm(o, A("ZR"), A("ONE", 0, 12), True, False)
         for e in range(2):
             for h in range(2):
                 mm(A(o[0], o[1] + e, o[2], 2), A("HH", 256 * e + 128 * h, 256 * e + 128 * h + 128), A(src[0], src[1] + h, src[2], 2),
-                   alone and h == 0, alone and h == 1)
-    def sub_open():
-        for j in range(NPE // 2):
-            mm(A("P%d" % (4 + j), 0, 384), A("ZR"), A("ONE"), True, False)
-            for e in range(2): mm(pslab(2 * j + e), A("NID"), A("XB"), False, False)
-    def distances(names):
-        def gi(i): return A("GS", i, 3072, 16)
-        r0 = 16 - NPE
-        for j in range(NPE): mm(pslab(j), A("ID"), gi(r0 + j), False, j % 2 == 1)
-        for i in range(NMAX): mm(KEY, A("FN", 16 - i, 144 - i), gi(i), False, False)
-        for j in range(NPE // 2): act(slab("DD", r0 + 2 * j, 2), A("P%d" % (4 + j), 0, 384), AF.Abs)
-        for i in range(r0, 16): mm(KEY, A("FA", 16 - i, 144 - i), slab("DD", i), False, False)
-        for i in range(NMAX, r0):
-            tt(slab("DD", i), gi(i), XP, AL.subtract)
-            if i % 2 == 1: act(slab("DD", i - 1, 2), slab("DD", i - 1, 2), AF.Abs)
-        for i in range(NMAX): tt(slab("DD", i), gi(i), XP, AL.max)
-        for e in list(range(NMAX, r0 - 2)) + [0, 1, r0 - 2, r0 - 1] + list(range(2, NMAX)):
-            mm(KEY, A("FB" if e < NMAX else "FA", 16 - e, 144 - e), slab("DD", e), False, False)
+                   False, last and e + h == 2)
+    def rows(c0, c1, banks, i, n=1):
+        per = 16 // len(banks)
+        return A("P%d" % banks[i // per], (c1 - c0) * (i % per), (c1 - c0) * (i % per + n))
+    def key_open(plan):
+        mm(KEY, A("KU"), A("ONE", 0, 192), True, False)
+        for c0, c1, how, banks in plan[1]:
+            if how == "max": mm(A("P0", c0, c1), A("BN"), A("XB", c0, c1), False, False)
+            if how == "abs":
+                per = 16 // len(banks)
+                for i in range(16):
+                    if i % per == 0: mm(A("P%d" % banks[i // per]), A("ZR"), A("ZA", 0, 512), True, False)
+                    mm(rows(c0, c1, banks, i), A("NID"), A("XB", c0, c1), False, False)
+    def distances(plan, off, names):
+        for c0, c1, q in plan[0]: fetch(q, A("GS", 16 * c0, 16 * c1), gat("X", 0, W + 16, A(off, c0, c1)))
+        for c0, c1, how, banks in plan[1]:
+            n = c1 - c0; key = A("P0", c0, c1)
+            def gi(i): return A("GS", 16 * c0 + i, 16 * c1, 16)
+            def dd(i, k=1): return A("DD", 16 * c0 + n * i, 16 * c0 + n * (i + k))
+            per = 16 // len(banks) if banks else 4
+            for i in range(16):
+                if how == "abs":
+                    mm(rows(c0, c1, banks, i), A("ID"), gi(i), False, i % per == per - 1)
+                    if i % per == per - 1: act(dd(i + 1 - per, per), rows(c0, c1, banks, i + 1 - per, per), AF.Abs)
+                elif how == "sub":
+                    tt(dd(i), gi(i), A("P1", c0, c1), AL.subtract)
+                    if i % per == per - 1: act(dd(i + 1 - per, per), dd(i + 1 - per, per), AF.Abs)
+                else:
+                    mm(key, A("FN", 16 - i, 144 - i), gi(i), False, False)
+                    tt(dd(i), gi(i), A("P1", c0, c1), AL.max)
+            for i in range(16): mm(key, A("FB" if how == "max" else "FA", 16 - i, 144 - i), dd(i), False, False)
         mm(KEY, A("IDH"), names, False, True)
+    def least(rs):
+        tr(A("TK"), KEY)
+        scan(A("TS"), A(rs), A("TK"), 0.0, AL.max, AL.min)
+        ts(A("KR", 0, 12), A("TS", 15, 192, 16), RND, AL.add, RND, AL.subtract)
+        tt(A("TC", 0, 12), A("TS", 15, 192, 16), A("KR", 0, 12), AL.subtract)
 
     parts = [(0, 96, "P0"), (96, 192, "P1"), (192, 256, "P4")]
-    def z_gather(h, nv):
-        c0, c2 = parts[h][:2]; c1 = c0 + nv
-        if c2 > c1: act(A("GS", 16 * c1, 16 * c2), gat("Z", 0, V, A("OA", c1, c2)), AF.Copy)
-        if c1 > c0: cp(A("GS", 16 * c0, 16 * c1), gat("Z", 0, V, A("OA", c0, c1)))
-    def z_sum(h, last=False):
-        c0, c2, pb = parts[h]
-        for j in range(16):
-            mm(A(pb, 0, c2 - c0), A("ID"), A("GS", 16 * c0 + j, 16 * c2, 16), j == 0, last and j == 15)
+    def z_sums(plan, dz):
+        for c0, c1, q in plan: fetch(q, A("GS", 16 * c0, 16 * c1), gat("Z", 0, V, A("OA", c0, c1)))
+        for c0, c2, pb in parts:
+            for j in range(16):
+                mm(A(pb, 0, c2 - c0), A("ID"), A("GS", 16 * c0 + j, 16 * c2, 16), j == 0, dz is None and j == 15)
+            if dz: mm(A(pb, 0, c2 - c0), A("ID"), A(dz[0], dz[1] + 5 * c0, dz[1] + 5 * c2 - 4, 5), False, True)
 
+    z_sums(ZG0, None)
     for t in range(3):
         more = t < 2
-        DO, DR, MS = A("DO%d" % t, 0, 2), A("DR%d" % t, 0, 2), "MS%d" % t
-        if t == 0:
-            for h, nv in enumerate([48, 48, 32]):
-                z_gather(h, nv); z_sum(h, True)
+        DO, DR, MC = A("DO%d" % t, 0, 2), A("DR%d" % t, 0, 2), "MC%d" % t
         for c0, c2, pb in parts:
             act(A("SM", c0, c2), A(pb, 0, c2 - c0), AF.Copy, 192.0)
             tt(A("T1", c0, c2), A(pb, 0, c2 - c0), A("C1", c0, c2), AL.mult)
@@ -280,40 +297,34 @@ def rank_program(g, core, T, topo):
                 mm(A("P2", c0, c2), A("BO4"), A("C2", c0, c2), True, False)
                 mm(A("P2", c0, c2), A("BOH"), A("T1", c0, c2), False, False)
                 mm(A("P2", c0, c2), A("BO"), A("T2", c0, c2), False, True)
-        if t == 0:
-            for x in later: q_keep(*x)
         ts(A("WL", 0, 256), A("P2", 0, 256), col("EF", 0), AL.is_le)
         scan(A("CC"), A("WL"), A("C32"), 0.0, AL.add, AL.min)
-        act(A("JK", 0, 288), A("CC"), AF.Sign, col("ST", 0), -1.0, col("AC", 0))
+        act(A("JK", 0, 288), A("CC"), AF.Sign, col("ST", 0), -1.0, col("AD", 0))
         ts(A("JK", 288, 576), A("CC"), col("ST", 1), AL.is_le)
-        add("V", lambda: g.vector.tensor_reduce(R(col("AC", 1)), R(A("JK", 288, 576)), AX.X, AL.add), [col("AC", 1)], [A("JK", 288, 576)])
-        ts(col(DO[0], 0), col("AC", 0), 2.5, AL.mult, 720.0 + t, AL.add)
-        ts(col(DO[0], 1), col("AC", 1), 5.0, AL.mult, float(t), AL.add)
+        add("V", lambda: g.vector.tensor_reduce(R(col("AD", 1)), R(A("JK", 288, 576)), AX.X, AL.add), [col("AD", 1)], [A("JK", 288, 576)], None, "wide")
+        ts(col(DO[0], 0), col("AD", 0), 2.5, AL.mult, 720.0 + t, AL.add)
+        ts(col(DO[0], 1), col("AD", 1), 5.0, AL.mult, float(t), AL.add)
         send("d%d" % t, DR, DO)
-        if t == 0: fill(A("DZ1"), 0)
-        ts(A("NA", 0, 32), gat("ASC", 0, 1440, DO), -1.0, AL.mult)
         ts(A("LI", 0, 32), gat("ASC", 0, 1440, DO), 15, AL.bitwise_and)
+        ts(A("NA", 0, 32), gat("ASC", 0, 1440, DO), -1.0, AL.mult)
         ts(A("NA", 32, 34), DO, -1.0, AL.mult)
         ts(A("LO", 0, 32), A("LI", 0, 32), P16, AL.add)
         ts(A("DV", 0, 2), DO, float(V), AL.is_ge, 1440.0, AL.mult)
-        if t > 0: mm(A("P3", 0, 81), A("IDF"), A("CT"), True, False)
+        tt(A("DV", 2, 4), A("DV", 0, 2), A("NA", 32, 34), AL.subtract)
+        cp(A("DX", 0, 2), A("DV", 2, 4))
+        cp(gat("X", 0, 2880, A("DX", 0, 2)), A("CX"))
+        wrap(A("P4", 0, 80), "F1", "X", 0, V)
+        act(A("DF", 0, 80), A("P4", 0, 80), AF.Copy)
         if more: mm(A("P7", 0, 1), A("O16"), col("CC", 255), True, True)
+        ts(A("NJ", 0, 32 - NSTEP), A("NA", NSTEP, 32), -1.0 / 16, AL.mult, 1.0 / 32, AL.add)
+        if t > 0: mm(A("P3", 0, 81), A("IDF"), A("CT"), True, False)
         for d in range(32):
             if d < NSTEP:
                 act(A("SN", 81 * d, 81 * d + 81), A("SG"), AF.Sign, col("NA", d))
             else:
                 ts(A("SN", 81 * d, 81 * d + 81), A("SJ"), col("NJ", d - NSTEP), AL.is_gt, 2.0, AL.mult)
             ts(A("OH", 128 * d, 128 * d + 128), A("IP"), col("LO", d), AL.is_equal, 256.0, AL.mult)
-            if d == 0: tt(A("DV", 2, 4), A("DV", 0, 2), A("NA", 32, 34), AL.subtract)
-            if d == 1: cp(A("DX", 0, 2), A("DV", 2, 4))
-            if d == 2:
-                cp(gat("X", 0, 2880, A("DX", 0, 2)), A("CX"))
-                wrap(A("P4", 0, 80), "F1", "X", 0, V)
-            if d == 3: ts(A("NJ", 0, 32 - NSTEP), A("NA", NSTEP, 32), -1.0 / 16, AL.mult, 1.0 / 32, AL.add)
-            if d == 12: act(A("DF", 0, 80), A("P4", 0, 80), AF.Copy)
-            if d % 3 == 0 or d == 31:
-                for e in range(max(d - 2, 0) if d < 31 else d, d + 1):
-                    mm(A("P3", 0, 81), A("OH", 128 * e, 128 * e + 128), A("SN", 81 * e, 81 * e + 81), t == 0 and e == 0, e == 31)
+            mm(A("P3", 0, 81), A("OH", 128 * d, 128 * d + 128), A("SN", 81 * d, 81 * d + 81), t == 0 and d == 0, d == 31)
         tt(A("CS"), A("P3", 0, 80), A("DF", 0, 80), AL.add)
         tt(A("FL", 0, 80), A("P3", 1, 81), A("CS"), AL.is_gt)
         scan(A("FS", 1, 93), A("FL"), A("ONE", 0, 92), 0.0, AL.add, AL.mult)
@@ -323,189 +334,232 @@ def rank_program(g, core, T, topo):
         for c in range(12):
             act(A("JK", 576 + 92 * c, 668 + 92 * c), A("P5", 0, 92), AF.Sign, col("ST", c), -1.0, col("AC", c))
         cp(A("CU", 0, 92), A("P4", 0, 92))
-        if t > 0: cp(A("MO"), A("MR%d" % (t - 1), 192, 204))
         cp(gat("YD", 0, 1440, DO), A("CD", 32 * t, 32 * t + 32))
         if not more: store("S", T.yd[:], A("YD", 0, V, p=(0, 128, 16)), "s_yd")
-        if t > 0: cp(gat("GH", 8, 1480, A("MO")), A("MR%d" % (t - 1), 0, 192))
-        if t == 1: cp(gat("QT", 0, 1472, A("BU")), A("QN", 0, 192))
+        if t > 0:
+            cp(A("MO"), A("MR%d" % (t - 1), 192, 204))
+            cp(gat("NB", 8 + V, 2760, A("MO")), A("MR%d" % (t - 1), 0, 192))
         cp(gat("X", V, 2720, DR), A("CX"))
         ts(A("HU"), A("AC"), 92.0, AL.add, 0.5, AL.mult)
         act(A("HB"), A("AC"), AF.Copy, 46.0, 0.5)
         tt(A("CM"), gat("CU", 0, 92, A("HU")), A("IS"), AL.is_le)
         mm(A("P6", 0, 12), A("ID16"), A("HB"), True, False)
         wrap(A("P6", 0, 12), "F1", "CM", 0, 192, False, True)
+        cp(A("BU"), A("P6", 0, 12))
         if more:
             mm(A("P7", 64, 256), A("BO"), A("CM"), True, True)
             ts(A("DF", 80, 160), A("CU", 0, 80), 192.0, AL.is_gt, 512.0, AL.mult)
             cp(A("OA"), A("ASC", t + 1, t + 1277, 5))
-        cp(A("BU"), A("P6", 0, 12))
+            cp(col("EI", 0), col("P7", 0))
+            ts(A("RG", 0, 192), A("P7", 64, 256), col("PC", 10) if t else PQ, AL.is_equal)
+            ts(col("EI", 1), col("EI", 0), 7, AL.bitwise_and)
+            ts(col("EF", 0), col("EI", 1), LOSS0, AL.add)
+            tt(A("DG"), A("FL", 0, 80), A("DF", 80, 160), AL.mult)
+            scan(A("CT", 1, 81), A("DG"), A("ONE", 0, 80), 0.0, AL.add, AL.mult)
+            cp(A(MC, 192, 204), A("BU"))
+            act(A("RG", 192, 384), A("RG", 0, 192), AF.Copy, 1.0, -1.0)
         B = A("BU")
         cp(A("LU"), gat("NB", 8, 1480, B))
         act(A("XB"), gat("X", 0, 1472, B), AF.Copy)
         mm(XP, A("ID"), A("XB"), True, True)
-        key_open(); sub_open()
-        nu = 80 if more else 96
-        act(A("GS", 16 * nu, 3072), gat("X", 0, W + 16, A("LU", nu, 192)), AF.Copy)
+        key_open(NEAR)
         ts(A("LH"), A("LU"), CEN, AL.subtract)
-        if more:
-            cp(col("EI", 0), col("P7", 0))
-            ts(A("RG", 0, 192), A("P7", 64, 256), col("PC", 10) if t else PQ, AL.is_equal)
-            ts(col("EI", 1), col("EI", 0), 7, AL.bitwise_and)
-            tt(A("DF", 0, 80), A("FL", 0, 80), A("DF", 80, 160), AL.mult)
-        cp(A("GS", 0, 16 * nu), gat("X", 0, W + 16, A("LU", 0, nu)))
-        distances(A("LH"))
+        ts(A("DP", 0, 12), B, float(V), AL.is_ge)
+        ts(A("BH"), gat("IOF", 0, 1472, B), CEN, AL.subtract)
+        distances(NEAR, "LU", A("LH"))
+        def pslab(i): return A("P%d" % EQB[i // 2 % len(EQB)], 192 * (i % 2), 192 * (i % 2) + 192)
         def sel_mm(i): mm(pslab(i), A("SEL", 128 * i, 128 * i + 128), A("LH"), True, True)
-        if more:
-            ts(col("EF", 0), col("EI", 1), LOSS0, AL.add)
-            tt(A("RB"), gat("IOF", 0, 1472, B), A("RG", 0, 192), AL.mult)
-        tr(A("TK"), KEY)
-        if more: act(A(MS, 192, 204), A("P6", 0, 12), AF.Copy)
+        least("RS1")
         act(A("SD"), KEY, AF.Sign, col("PC", 7))
-        wrap(A("P4", 0, 12), "F4", "SD", 0, 192)
-        act(A("ND"), A("P4", 0, 12), AF.Copy, 65536.0 - V)
-        mm(A("P3", 256, 448), A("LK"), A("SD"), True, True)
-        scan(A("TS"), A("RS"), A("TK"), 0.0, AL.add, AL.min)
-        ts(A("KI", 0, 12), A("TS", 15, 192, 16), BIGK, AL.min)
-        ts(A("KI", 16, 28), A("KI", 0, 12), 4095, AL.bitwise_and)
-        ts(A("TC", 0, 12), A("KI", 16, 28), float(V), AL.subtract)
         wrap_t(A("P2", 256, 268), A("TC", 0, 12))
-        for i in range(2, 6): sel_mm(i)
-        if more:
-            act(A("RG", 192, 384), A("RG", 0, 192), AF.Copy, 1.0, -1.0)
-            act(A("YB"), gat("Y", 0, 1472, B), AF.Copy, 0.0, -1.0)
+        ts(A("UO"), A("P2", 256, 268), CEN + 8, AL.add)
+        cp(A("MU"), gat("NB", 0, W + 16, A("UO")))
+        wrap(A("P3", 0, 12), "F4", "SD", 0, 192)
+        mm(A("P3", 256, 448), A("LK"), A("SD"), True, True)
+        act(A("ND"), A("P3", 0, 12), AF.Copy, 65536.0 - 2000)
         ts(KO, A("P3", 256, 448), col("PC", 3), AL.is_equal)
-        tt(A("UF", 12, 24), A("P2", 256, 268), A("ND"), AL.min)
-        ts(A("AK", 0, 12), A("UF", 12, 24), 8.0, AL.is_ge)
-        ts(A("UO", 0, 12), A("UF", 12, 24), float(V), AL.add, V + 8.0, AL.min)
+        for i in range(2 * len(EQB)): sel_mm(i)
+        key_open(OFFER)
+        tt(A("UF"), A("P2", 256, 268), A("ND"), AL.min)
+        ts(A("AK", 0, 12), A("UF"), V - CEN, AL.is_ge)
+        ts(A("DP", 16, 28), A("ND"), 0.0, AL.is_lt)
         scan(A("AK", 17, 29), A("AK", 0, 12), A("ONE", 0, 12), 0.0, AL.add, AL.mult)
-        mm(A("P2", 272, 284), A("TRI"), A("AK", 0, 12), True, False)
+        mm(A("P2", 272, 284), A("I256"), A("DP", 0, 12), True, False)
+        mm(A("P2", 272, 284), A("I256"), A("DP", 16, 28), False, False)
+        mm(A("P2", 272, 284), A("TRA"), A("AK", 0, 12), False, False)
         mm(A("P2", 272, 284), A("BO"), A("AK", 16, 28), False, True)
-        for i in (6, 7, 0, 1): sel_mm(i)
+        ts(A("DP", 32, 44), A("P2", 272, 284), 224.0, AL.is_gt)
+        for q in range(16): mm(A("P0", q, 192, 16), A("SELB", 128 * q, 128 * q + 128), A("DP", 32, 44), False, False)
         tt(A("KL"), A("LH"), KO, AL.mult)
-        ts(A("UF", 0, 12), A("P2", 272, 284), 32.0, AL.is_gt, 4096.0, AL.mult)
-        tt(A("UF", 0, 12), A("UF", 0, 12), A("UF", 12, 24), AL.add)
-        key_open()
-        ts(A("UO", 12, 24), A("UF", 0, 12), 0.0, AL.max, V + 8.0, AL.min)
         mm(A("P2", 0, 192), A("BOH"), A("KL"), True, True)
         if more: wrap(A("P2", 288, 300), "FH", "KL", 0, 192)
-        mm(A("P3", 256, 448), A("KC"), A("ONE", 0, 192), True, False)
-        mm(A("P3", 256, 448), A("IDH"), A("LH"), False, False)
-        mm(A("P3", 256, 448), A("NIH"), A("KL"), False, not more)
-        ts(A("LG"), gat("GH", 0, 1480, A("UO", 12, 24)), float(G), AL.min, float(V), AL.add)
-        tt(A("L2"), gat("NB", 0, 1480, A("UO", 0, 12)), A("LG"), AL.min)
-        cp(A("MU"), A("L2"))
-        nu = 16
-        act(A("GS", 16 * nu, 3072), gat("X", 0, W + 16, A("MU", nu, 192)), AF.Copy)
+        tr(A("TF"), A("P2", 0, 192))
+        if more: ts(A("OO"), A("P2", 288, 300), CEN, AL.add)
+        tt(A("RS2", 0, 192, 16), A("TF", 15, 192, 16), A("SEG"), AL.add)
         ts(A("MH"), A("MU"), CEN, AL.subtract)
-        tt(slab("EQ", 16), gat("IOF", 0, 1472, B), A("L2"), AL.is_equal)
+        tt(slab("EQ", 16), A("BH"), A("MH"), AL.is_equal)
+        mm(KEY, A("IDB"), slab("EQ", 16), False, False)
         for i in range(16):
             tt(slab("EQ", i), pslab(i), A("MH"), AL.is_equal)
-            if i % 2 == 1:
-                if i < 8:
-                    sel_mm(i + 7); sel_mm(i + 8)
-                if i == 11: sub_open()
-                for e in ([16] if i == 1 else []) + [i - 1, i]:
-                    mm(KEY, A("IDB"), slab("EQ", e), False, False)
-        tr(A("TK"), A("P2", 0, 192))
-        if more: ts(A("OO"), A("P2", 288, 300), CEN, AL.add)
-        cp(A("GS", 0, 16 * nu), gat("X", 0, W + 16, A("MU", 0, nu)))
-        ts(A("FK"), A("TK", 15, 192, 16), BIGK + CEN + 8, AL.add)
-        if more: act(A("YO"), gat("Y", 0, W + 16, A("OO")), AF.Copy)
-        distances(A("MH"))
-        if more: tt(A("QP"), gat("QT", 0, 1472, B), A("YO"), AL.subtract)
-        tr(A("TK"), KEY)
-        scan(A("TS"), A("RS"), A("TK"), 0.0, AL.add, AL.min)
-        tt(A("KI", 0, 12), A("TS", 15, 192, 16), A("FK"), AL.min)
-        ts(A("KI", 16, 28), A("KI", 0, 12), 4095, AL.bitwise_and)
+            mm(KEY, A("IDB"), slab("EQ", i), False, False)
+            if i % 2 == 1 and i + 2 * len(EQB) < 17:
+                sel_mm(i + 2 * len(EQB) - 1); sel_mm(i + 2 * len(EQB))
         if more:
-            ts(A("TC", 0, 12), A("KI", 16, 28), CEN + 8, AL.subtract)
-            wrap_t(A("P1", 256, 268), A("TC", 0, 12))
-            ts(A("KF", 0, 12), A("KI", 0, 12), BIGK, AL.is_ge, 4096.0, AL.mult)
-        ts(A("TH"), gat("KI", 16, 28, A("RP")), CEN + 8, AL.subtract)
+            act(A("YB"), gat("Y", 0, 1472, B), AF.Copy, 0.0, -0.5)
+            act(A("YO"), gat("Y", 0, W + 16, A("OO")), AF.Copy)
+            tt(A("QP"), gat("QT", 0, 1472, B), A("YO"), AL.subtract)
+            act(A("FZ", 0, 192), A("QP"), AF.Abs, col("PC", 12), 0.5)
+            act(A("FZ", 192, 384), A("QP"), AF.Abs, col("PC", 13), 0.5)
+            act(A("FZ"), A("FZ"), AF.Relu, col("PC", 11), -1.0)
+            ts(A("RB"), A("BH"), CEN, AL.add)
+            tt(A("RB"), A("RB"), A("RG", 0, 192), AL.mult)
+        distances(OFFER, "MU", A("MH"))
+        if more:
+            for o, s in ((0, "ID"), (192, "NID")):
+                mm(A("P3", o, o + 192), A("ID"), A("FZ", 0, 192), True, False)
+                mm(A("P3", o, o + 192), A(s), A("FZ", 192, 384), False, True)
+            tt(A("ZC"), A("P3", 0, 192), A("YB"), AL.mult)
+            tt(A("ZS"), A("P3", 192, 384), A("YB"), AL.mult)
+        LST = A("P4", 0, 192)
+        mm(LST, A("KC"), A("ONE", 0, 192), True, False)
+        mm(LST, A("IDH"), A("LH"), False, False)
+        mm(LST, A("NIH"), A("KL"), False, not more)
+        least("RS2")
+        tt(A("KN", 0, 12), A("TS", 15, 192, 16), A("KR", 0, 12), AL.subtract)
         if not more:
-            tr(A("WR", 0, 192), A("TH"))
-            tt(A("LF"), A("WR", 0, 192), KO, AL.mult)
-            tt(A(MS, 0, 192), A("LF"), A("P3", 256, 448), AL.add)
-            cp(gat("NB", 8, 1480, B), A(MS, 0, 192))
+            act(A("LW"), LST, AF.Copy)
+            cp(A("TH"), gat("KN", 0, 12, A("RP")))
+            tr(A("WR"), A("TH"))
+            tt(A("LF"), A("WR"), KO, AL.mult)
+            tt(gat("NB", 8, 1480, B), A("LF"), A("LW"), AL.add)
             store("S", T.yn[:, 0:640], A("NB", 8, 648), "s_y0")
             store("A", T.yn[:, 640:V], A("NB", 648, 8 + V), "s_y1")
             break
-        ts(A("WO", 0, 12), A("P1", 256, 268), CEN, AL.add)
-        tr(A("WR", 0, 192), A("TH"))
-        tt(A("QN", 0, 192), gat("Y", 0, W + 16, A("WO", 0, 12)), A("QP"), AL.add)
-        act(A("QN", 192, 384), A("QN", 0, 192), AF.Abs, col("PC", 6), 0.5)
-        act(A("QN", 192, 384), A("QN", 192, 384), AF.Relu, col("PC", 11), -1.0)
-        tt(A("TH"), A("WR", 0, 192), KO, AL.mult)
-        mm(A("P3", 256, 448), A("IDH"), A("TH"), False, True)
-        act(A(MS, 0, 192), A("P3", 256, 448), AF.Copy)
-        send("u%d" % t, A("MR%d" % t), A(MS))
-        tt(A("KF", 16, 28), A("KF", 0, 12), A("KI", 16, 28), AL.add)
-        ts(A("KF", 0, 12), A("KF", 16, 28), V + 8.0, AL.is_ge, 4096.0, AL.mult)
-        tt(A("KF", 16, 28), A("KF", 0, 12), A("KF", 16, 28), AL.add)
-        tt(gat("Z", 0, 1472, B), A("QN", 192, 384), A("YB"), AL.mult)
-        z_gather(0, 0)
-        ts(A("TC", 16, 28), A("KF", 16, 28), 8.0, AL.subtract, 2000.0, AL.min)
+        wrap_t(A("P5", 0, 12), A("TC", 0, 12))
+        ts(A("WO", 0, 12), A("P5", 0, 12), CEN, AL.add)
+        tt(A("ZW"), gat("Y", 0, W + 16, A("WO", 0, 12)), A("ZS"), AL.mult)
+        tt(gat("Z", 0, 1472, B), A("ZW"), A("ZC"), AL.add)
+        cp(A("TH"), gat("KN", 0, 12, A("RP")))
+        tr(A("WR"), A("TH"))
+        tt(A("TW"), A("WR"), KO, AL.mult)
+        mm(LST, A("IDH"), A("TW"), False, True)
+        act(A("MS"), LST, AF.Copy)
+        ts(A(MC, 0, 192), A("MS"), float(G), AL.min, float(V), AL.add)
+        send("u%d" % t, A("MR%d" % t), A(MC))
+        cp(gat("NB", 8, 1480, B), A("MS"))
+        if t == 0:
+            tt(A("QN"), gat("Y", 0, W + 16, A("WO", 0, 12)), A("QP"), AL.add)
+            cp(gat("QT", 0, 1472, B), A("QN"))
+        ts(A("KR", 16, 28), A("TS", 15, 192, 16), RND, AL.add, RND + BIGK - 4096, AL.subtract)
+        tt(A("TC", 16, 28), A("KN", 0, 12), A("KR", 16, 28), AL.max)
+        ts(A("TC", 32, 44), A("KN", 0, 12), V - CEN, AL.is_ge, 4096.0, AL.mult)
         wrap_t(A("P2", 304, 316), A("TC", 16, 28))
-        wrap_t(A("P7", 0, 12), A("TC", 16, 28), False)
-        ts(A("MH"), gat("KF", 16, 28, A("RP")), 8.0, AL.subtract, 2000.0, AL.min)
+        wrap_t(A("P7", 0, 12), A("TC", 16, 28), True, False)
+        wrap_t(A("P7", 0, 12), A("TC", 32, 44), False, False)
         cp(A("WF", 0, 12), A("P2", 304, 316))
-        tr(A("WR", 192, 384), A("MH"))
-        ts(A("WO", 12, 24), A("P2", 304, 316), 1440.0, AL.min)
-        mm(A("P5", 0, 192), A("ZR"), A("ONE", 0, 192), True, False)
+        ts(A("WO", 12, 24), A("P2", 304, 316), CEN, AL.add, 1440.0, AL.min)
+        mm(A("P6", 256, 448), A("ZR"), A("ONE", 0, 192), True, False)
         for c in range(12):
-            ts(A("EE", 208 * c, 192 * (c + 1)), A("WR", 192 + 16 * c, 384), col("WF", c), AL.is_equal)
-            if c < 11: mm(A("P5", 16 * (c + 1), 192), A("BO"), A("EE", 208 * c + 16, 192 * (c + 1)), False, c == 10)
-        act(A("LS"), A("P5", 0, 192), AF.Sign)
+            ts(A("EE", 208 * c, 192 * (c + 1)), A("WR", 16 * c, 192), col("WF", c), AL.is_equal)
+            if c < 11: mm(A("P6", 256 + 16 * (c + 1), 448), A("BO"), A("EE", 208 * c + 16, 192 * (c + 1)), False, c == 10)
+        act(A("LS"), A("P6", 256, 448), AF.Sign)
         for q in range(1, 16):
             mm(A("P7", 0, 12), A("LQ", 128 * q, 128 * q + 128), A("EE", q, 2304, 208), False, False)
-        tt(A("TH"), gat("ASC", 0, 1632, A("WO", 12, 24)), A("RG", 0, 192), AL.mult)
-        wrap(A("P2", 288, 300), "FH", "TH", 0, 192)
         wrap(A("P7", 0, 12), "FA", "LS", 0, 192, False, True)
-        cp(gat("NB", 8, 1480, B), A(MS, 0, 192))
-        cp(A("OO"), A("P2", 288, 300))
-        cand_names(t + 1)
-        act(A("YO"), gat("Z", 0, 1472, B), AF.Copy)
-        act(A("QP"), gat("Z", 0, 1472, A("OO")), AF.Copy, 0.0, -1.0)
-        tt(A("MH"), gat("ASC", 0, 1632, A("WO", 12, 24)), A("RG", 192, 384), AL.mult)
-        mm(A("P2", 0, 192), A("IDH"), A("RB"), True, False)
-        mm(A("P2", 0, 192), A("IDH"), A("MH"), False, True)
-        z_sum(0)
-        z_gather(1, 0)
         tt(A("WF", 12, 24), A("P7", 0, 12), A("DU"), AL.min)
+        ts(A("WS"), A("WF", 12, 24), CEN, AL.add)
+        tt(A("TA"), gat("ASC", 0, 1632, A("WO", 12, 24)), A("RG", 0, 192), AL.mult)
+        wrap(A("P2", 288, 300), "FH", "TA", 0, 192)
+        cp(A("OZ"), A("P2", 288, 300))
+        act(A("ZN"), gat("Z", 0, 1472, B), AF.Copy)
+        act(A("ZO"), gat("Z", 0, 1472, A("OZ")), AF.Copy, 0.0, -1.0)
+        tt(gat("DZ%d" % t, 0, 1632, A("WS")), A("ZN"), A("ZO"), AL.add)
+        tt(A("MA"), gat("ASC", 0, 1632, A("WO", 12, 24)), A("RG", 192, 384), AL.mult)
+        mm(A("P3", 0, 192), A("IDH"), A("RB"), True, False)
+        mm(A("P3", 0, 192), A("IDH"), A("MA"), False, True)
+        act(A("L2"), A("P3", 0, 192), AF.Copy)
         cand_terms(t + 1)
-        cp(A("WS"), A("WF", 12, 24))
-        act(A("L2"), A("P2", 0, 192), AF.Copy)
-        cand_terms1()
-        tt(gat("DZ%d" % t, 0, 1632, A("WS")), A("YO"), A("QP"), AL.add)
-        z_gather(2, NLAST)
-        z_sum(1)
-        for h, (c0, c2, pb) in enumerate(parts):
-            if h == 2: z_sum(2)
-            mm(A(pb, 0, c2 - c0), A("ID"), A("DZ%d" % t, t + 1 + 5 * c0, t + 1 + 5 * c2 - 4, 5), False, True)
-        cand_terms2()
+        z_sums(ZG1, ("DZ%d" % t, t + 1))
         cp(gat("ASC", 0, 1632, A("WS")), A("L2"))
-        scan(A("CT", 1, 81), A("DF", 0, 80), A("ONE", 0, 80), 0.0, AL.add, AL.mult)
 
     emit_all(ops, Q, T)
 
 
-def emit_all(ops, Q, T):
-    hist = {}
-    deps = []
-    for n, (q, emit, rd, wr, token) in enumerate(ops):
-        d = set()
+CY, PCY, LAT = 0.83e-3, 0.45e-3, 0.2
+WIDE = {"float32": 4, "int32": 4}
+PLAN = {}
+
+
+def span(a):
+    return 16 * span(a[5]) if a[5] else -(-(a[2] - a[1]) // (a[3] or 1))
+
+
+def call_time(q, kind, outs, ins):
+    full = [a for a in outs[:1] + ins if isinstance(a, tuple)]
+    if kind == "wait": return 0.0, 0.0
+    if kind in ("dma", "send"):
+        a = full[0] if kind == "dma" else ins[0]
+        by = 128 * span(a) * WIDE.get(SB[a[0]][1], 2)
+        return (0.1, 1.6 + by / 180e3) if kind == "dma" else (0.3, 1.3 + by / 60e3)
+    if q == "P": t = max(64, span(ins[1])) * PCY * (4 if SB[ins[1][0]][1] == "float32" else 1)
+    elif q == "G": t = 0.17 + 2 * span(full[0]) * CY
+    elif full[0][5]: t = 0.05 + 3.8 * span(full[0]) * CY
+    elif len(full) > 1 and full[1][5]: t = 0.06 + 1.56 * span(full[1]) * CY
+    else:
+        n = span(full[min(1, len(full) - 1)])
+        wide = kind == "wide" or any(a[0] not in SB or SB[a[0]][1] in WIDE for a in full if span(a) == n)
+        if q == "V" and kind == "tt": n *= 2 if all(a[0] in SB for a in full[1:]) else 1
+        elif q == "V" and not wide: n /= 2
+        t = max(64, n) * CY
+    return t, t
+
+
+def conflicts(ops):
+    hist = {}; deps = []
+    for n, (q, emit, rd, wr, token, cost, kind) in enumerate(ops):
+        d = {}
         for a, w in [(a, False) for a in rd] + [(a, True) for a in wr]:
             bank = a[0] not in SB
             for m, lo, hi, w2 in hist.get(a[0], ()):
                 same = ops[m][0] == q and ops[m][4] is None and token is None
                 meet = lo < a[2] and a[1] < hi
                 if same:
-                    if meet and q != "P" and w2: d.add(m)
-                elif bank or (meet and (w or w2)): d.add(m)
-        d.discard(n)
+                    if q == "P":
+                        if bank and not (kind == "mid" == ops[m][6]): d[m] = False
+                    elif meet and (w or w2): d[m] = True
+                elif bank or (meet and (w or w2)): d[m] = True
+        d.pop(n, None)
         deps.append(d)
         for a, w in [(a, False) for a in rd] + [(a, True) for a in wr]:
             hist.setdefault(a[0], []).append((n, a[1], a[2], w))
+    return deps
+
+
+def arrange(ops, deps):
+    n = len(ops)
+    edge = [dict((m, ops[m][5][1] + LAT if w else ops[m][5][0]) for m, w in d.items()) for d in deps]
+    for k, o in enumerate(ops):
+        if o[0] == "X": edge[k][k - 1] = ops[k - 1][5][1] + 1.0
+    tail = [o[5][1] for o in ops]
+    for k in range(n - 1, -1, -1):
+        for m, lag in edge[k].items(): tail[m] = max(tail[m], lag + tail[k] + 1e-6)
+    busy = {}; start = [0.0] * n
+    for k in sorted(range(n), key=lambda k: (-tail[k], k)):
+        t = max([start[m] + lag for m, lag in edge[k].items()], default=0.0)
+        c = ops[k][5][0]; line = busy.setdefault(ops[k][0], []); at = len(line)
+        for j, (a, b) in enumerate(line):
+            if t + c <= a + 1e-9:
+                at = j; break
+            t = max(t, b)
+        line.insert(at, (t, t + c)); start[k] = t
+    return sorted(range(n), key=lambda k: (start[k], -tail[k], k))
+
+
+def emit_all(ops, Q, T):
+    if "order" not in PLAN:
+        PLAN["order"] = arrange(ops, conflicts(ops))
+        PLAN["deps"] = [[m for m, w in d.items() if w] for d in conflicts([ops[k] for k in PLAN["order"]])]
+    ops = [ops[k][:5] for k in PLAN["order"]]; deps = PLAN["deps"]
     know = {q: ({}, set()) for q in Q}
     after = {}
     waits = []

@@ -6,20 +6,21 @@ BIGK = 4096.0 * 4000
 RND = 1.5 * 2 ** 35
 DEADX = 131072.0
 LOSS0 = 192 * 31.5 * 16
-PAIRS = [128, 128, 128, 112, 72, 40, 32]
-PBANK = [0, 1, 4, 0, 2, 3, 7]
-NSTEP = 28
-NEAR = ([(0, 48, "V"), (48, 96, "A"), (96, 144, "V"), (144, 192, "A")], [(0, 96, "abs", [3, 4, 5, 6]), (96, 192, "max", [])])
-OFFER = ([(0, 64, "A"), (64, 128, "A"), (128, 176, "A"), (176, 192, "V")], [(0, 64, "abs", [3, 4]), (64, 128, "max", []), (128, 192, "max", [])])
+SUMS = [(128, 128, "P0", 0, 256), (128, 128, "P1", 0, 256), (128, 128, "P4", 0, 256), (112, 112, "P3", 0, 256), (72, 72, "P7", 16, 256), (40, 40, "P7", 160, 400), (32, 32, "P2", 256, 320)]
+NSTEP = 30
+NEAR = ([(0, 32, "V"), (32, 64, "A"), (64, 128, "V"), (128, 192, "A")], [(0, 64, "abs", [3, 4]), (64, 128, "max", []), (128, 192, "max", [])])
+OFFER = ([(0, 64, "A"), (64, 128, "A"), (128, 160, "A"), (160, 192, "V")], [(0, 64, "abs", [3, 4]), (64, 128, "sub", []), (128, 192, "max", [])])
 EQB = [5, 6, 7]
+OAP = [(0, 96), (96, 256)]
 ZG0 = [(0, 48, "V"), (48, 96, "A"), (96, 144, "V"), (144, 192, "A"), (192, 224, "V"), (224, 256, "A")]
-ZG1 = [(0, 48, "A"), (48, 96, "A"), (96, 144, "A"), (144, 192, "A"), (192, 224, "V"), (224, 256, "V")]
+ZG1 = ZG0
+URGE = {"VTW": 1.0, "AMS": 1.0, "VNB": 1.0, "VZ": 1.0, "AFZ": 1.0, "AYN": 1.0, "VTN": 1.0}
 
 SB = {
     "NBI": (1280, "int32"), "NBU": (1280, "uint16"), "NB": (2760, "float32"), "NBC": (1056, "float32"),
     "ASC": (1632, "int32"), "X": (2880, "bfloat16"), "Y": (2352, "bfloat16"), "GS": (20480, "bfloat16"),
     "Z": (1472, "bfloat16"), "QT": (1472, "bfloat16"), "ZA": (1280, "bfloat16"), "YD": (1440, "float32"),
-    "ONE": (384, "bfloat16"), "BO": (128, "bfloat16"), "BN": (128, "bfloat16"), "ID": (128, "bfloat16"), "NID": (128, "bfloat16"), "ZR": (128, "bfloat16"),
+    "ONE": (384, "bfloat16"), "BO": (128, "bfloat16"), "BN": (128, "bfloat16"), "ID": (128, "bfloat16"), "NID": (128, "bfloat16"), "ICN": (128, "bfloat16"),
     "ID16": (128, "bfloat16"), "IDB": (128, "bfloat16"), "IDF": (128, "float32"), "IDH": (128, "float16"), "NIH": (128, "float16"),
     "BOH": (128, "float16"), "BO4": (128, "bfloat16"), "TRI": (128, "bfloat16"), "TRA": (128, "bfloat16"), "I256": (128, "bfloat16"),
     "LK": (128, "bfloat16"), "N32": (128, "bfloat16"), "I192": (128, "bfloat16"),
@@ -27,28 +28,26 @@ SB = {
     "F1": (144, "bfloat16"), "FA": (144, "bfloat16"), "FB": (144, "bfloat16"), "FN": (144, "bfloat16"),
     "FH": (144, "float16"), "FE": (144, "float16"),
     "KU": (128, "bfloat16"), "KC": (128, "bfloat16"), "KT": (192, "float32"),
-    "PI": (8, "int32"), "PC": (16, "float32"), "IP": (128, "bfloat16"), "IS": (192, "bfloat16"), "IOF": (1472, "float32"),
+    "PI": (8, "int32"), "PC": (16, "float32"), "IP": (128, "bfloat16"), "IS": (192, "bfloat16"),
     "SG": (81, "float32"), "SJ": (81, "bfloat16"), "ST": (12, "float32"), "DU": (12, "float32"), "SEG": (12, "float32"),
-    "RS1": (192, "float32"), "RS2": (192, "float32"), "RPI": (12, "int32"), "RP": (12, "uint16"), "C32": (288, "bfloat16"),
+    "RS1": (192, "float32"), "RS2": (192, "float32"), "RM": (192, "float16"), "NMS": (192, "float16"), "C32": (288, "bfloat16"),
     "CX": (32, "bfloat16"), "CD": (96, "float32"), "JK": (1680, "bfloat16"), "HM": (256, "bfloat16"), "HS": (512, "bfloat16"), "HH": (512, "float16"),
     "TC": (64, "float16"), "F4": (144, "bfloat16"), "ND": (12, "float32"), "AK": (32, "bfloat16"), "DP": (48, "bfloat16"),
-    "OA": (256, "uint16"), "NO": (16, "uint16"), "EP": (256, "bfloat16"), "C1": (256, "bfloat16"), "C2": (256, "bfloat16"),
+    "OA": (256, "uint16"), "NO": (16, "uint16"), "YN": (256, "bfloat16"), "C1": (256, "bfloat16"), "C2": (256, "bfloat16"),
     "SM": (256, "bfloat16"), "T1": (256, "float16"), "TN": (256, "float16"), "T2": (256, "bfloat16"), "WL": (288, "bfloat16"), "CC": (288, "bfloat16"),
     "EI": (8, "int32"), "EF": (8, "float32"), "AC": (12, "float32"), "AD": (8, "float32"), "DV": (8, "float32"), "DX": (8, "uint16"),
     "DO0": (8, "uint16"), "DO1": (8, "uint16"), "DO2": (8, "uint16"), "DR0": (8, "uint16"), "DR1": (8, "uint16"), "DR2": (8, "uint16"),
-    "NA": (34, "float32"), "NJ": (8, "float32"), "LI": (34, "int32"), "LO": (34, "float32"), "OH": (34 * 128, "bfloat16"), "SN": (34 * 81, "bfloat16"),
+    "NA": (34, "float32"), "NJ": (8, "float32"), "LI": (34, "int32"), "LO": (34, "float32"), "OH": (32 * 128, "bfloat16"), "SN": (32 * 81, "bfloat16"),
     "CS": (80, "float32"), "FL": (92, "bfloat16"), "FS": (93, "bfloat16"), "CU": (96, "float32"), "DF": (160, "float32"), "DG": (80, "float32"), "CT": (81, "float32"),
     "HU": (12, "uint16"), "HB": (12, "bfloat16"), "CM": (192, "bfloat16"), "BU": (12, "uint16"),
     "LU": (192, "uint16"), "LH": (192, "float16"), "LF": (192, "float32"), "LW": (192, "float32"), "XB": (192, "bfloat16"), "DD": (3072, "bfloat16"), "EQ": (17 * 192, "bfloat16"),
-    "TK": (192, "float32"), "TF": (192, "float32"), "TS": (192, "float32"), "KR": (32, "float32"), "KN": (16, "float32"), "TH": (192, "float16"), "TW": (192, "float16"), "TA": (192, "float16"),
+    "TK": (192, "float32"), "TF": (192, "float32"), "TS": (192, "float32"), "KR": (16, "float32"), "TH": (192, "float16"), "TW": (192, "float16"),
     "SD": (192, "bfloat16"), "KL": (192, "float16"), "UO": (12, "uint16"), "UF": (12, "float32"),
-    "L2": (192, "float32"), "MU": (192, "uint16"), "MH": (192, "float16"), "MA": (192, "float16"), "BH": (192, "float16"),
-    "OO": (12, "uint16"), "OZ": (12, "uint16"), "QP": (192, "bfloat16"), "YO": (192, "bfloat16"), "ZN": (192, "bfloat16"), "ZO": (192, "bfloat16"), "YB": (192, "bfloat16"),
-    "FZ": (384, "bfloat16"), "ZC": (192, "bfloat16"), "ZS": (192, "bfloat16"), "ZW": (192, "bfloat16"),
-    "RG": (384, "float32"), "RB": (192, "float16"), "LQ": (2048, "bfloat16"), "LV": (768, "bfloat16"),
-    "DZ0": (1632, "bfloat16"), "DZ1": (1632, "bfloat16"), "WS": (12, "uint16"), "LT": (128, "bfloat16"),
+    "L2": (192, "float32"), "MU": (192, "uint16"), "MH": (192, "float16"), "MA": (192, "float16"), "BH": (12, "float16"),
+    "OO": (12, "uint16"), "QP": (192, "bfloat16"), "YO": (192, "bfloat16"), "YB": (192, "bfloat16"), "YW": (192, "bfloat16"), "FZ": (192, "bfloat16"),
+    "RG": (384, "bfloat16"), "RB": (192, "float16"), "LQ": (2048, "bfloat16"), "WS": (12, "uint16"), "LT": (128, "bfloat16"),
     "WR": (192, "float16"), "WO": (24, "uint16"), "WF": (48, "float32"), "QN": (192, "bfloat16"), "EE": (12 * 192, "bfloat16"), "LS": (192, "bfloat16"),
-    "MS": (192, "float32"), "MC0": (204, "float32"), "MC1": (204, "float32"), "MR0": (204, "float32"), "MR1": (204, "float32"), "MO": (12, "uint16"),
+    "MS": (192, "float32"), "MD": (192, "float32"), "MC0": (204, "float32"), "MC1": (204, "float32"), "MR0": (204, "float32"), "MR1": (204, "float32"), "MO": (12, "uint16"),
 }
 PLACE = {}
 SCRATCH = {}
@@ -117,7 +116,6 @@ def rank_program(g, core, T, topo):
             add("G", lambda: g.iota(R(o), pat, base, cm), [o], [])
         else:
             add("G", lambda: g.iota(R(o), pat, base, cm, allow_small_or_imprecise_dtypes=True), [o], [])
-    def fill(o, c): iota(o, [[0, o[2] - o[1]]], c)
     def sel(o, i, pat, op, base, cm): add("G", lambda: g.affine_select(R(o), R(i), pat, op, 0.0, base, cm), [o], [i])
     def load(q, o, src, sem): add(q, lambda: Q[q].dma_start(R(o), src).then_inc(T.sem[sem], 16), [o], [], (sem, 16), "dma")
     def store(q, d, i, sem): add(q, lambda: Q[q].dma_start(d, R(i)).then_inc(T.sem[sem], 16), [], [i], (sem, 16), "dma")
@@ -146,7 +144,7 @@ def rank_program(g, core, T, topo):
     send("lab", A("Y", V, W), A("Y", 0, G), [col("JK", 0), col("X", 0), col("ASC", 0)])
     load("S", A("X", 0, V), T.xf[:], "l_xf")
     load("S", A("ASC", 0, V), T.asc[:], "l_asc")
-    for f in ["F1", "FA", "FB", "FN", "F4", "FH", "FE", "KU", "KC", "ZR"]: ms(A(f), 0.0)
+    for f in ["F1", "FA", "FB", "FN", "F4", "FH", "FE", "KU", "KC", "NMS"]: ms(A(f), 0.0)
     ms(col("AK", 16), 0.0)
     ts(col("PI", 1), col("PI", 0), 15, AL.bitwise_and)
     ms(A("Y", W), 0.0); ms(A("WL", 256), 1.0); ms(A("C32"), 32.0); ms(A("CX"), DEADX)
@@ -154,7 +152,7 @@ def rank_program(g, core, T, topo):
     tt(P16, col("PI", 0), col("PI", 1), AL.subtract)
     ms(A("FL", 80), 1.0); ms(col("FS", 0), 0.0); ms(col("CT", 0), 0.0); ms(A("O16"), 1.0 / 16); ms(col("EF", 0), LOSS0)
     ms(col("PC", 5), 31.5); ms(col("PC", 6), -31.5 / 64); ms(col("PC", 7), -1.6e7)
-    ms(col("PC", 12), 0.5 / 64); ms(col("PC", 13), -63.5 / 64)
+    ms(col("PC", 12), float(G)); ms(A("RM"), 1.0); ms(A("RM", 0, 192, 16), 0.0)
     ts(A("QM"), A("KT", 0, 16), PQ, AL.is_equal)
     ts(A("QB"), A("QM"), 2.0 ** 25, AL.mult)
     ms(A("RS1"), -1e9); ms(A("RS2"), -1e9); ms(A("RS1", 0, 192, 16), BIGK - CEN - 8)
@@ -167,18 +165,19 @@ def rank_program(g, core, T, topo):
     for f, c in [("F1", 1.0), ("FA", 65536.0), ("FB", 131072.0), ("FN", -65536.0), ("F4", 4096.0)]:
         act(A(f, 16, 144, 16), A("BO", 0, 128, 16), AF.Copy, 0.0, c)
     for f, s, c in [("NID", "ID", -1.0), ("ID16", "ID", 16.0), ("IDB", "ID", 2.0 ** 25), ("IDF", "ID", 1.0), ("N32", "ID", -32.0), ("BO4", "BO", 192.0),
-                    ("BN", "BO", -65536.0), ("I192", "ID", 192.0), ("I256", "ID", 256.0)]:
+                    ("BN", "BO", -65536.0), ("I192", "ID", 192.0), ("I256", "ID", 256.0), ("ICN", "ID", CEN)]:
         act(A(f), A(s), AF.Copy, 0.0, c)
     act(A("KU", p=(0, 1)), A("KT", 0, 128, p=(0, 1)), AF.Copy, 0.0, 4096.0)
     ms(A("KC", p=(0, 1)), CEN)
     cp(A("BOH"), A("BO")); cp(A("IDH"), A("ID")); ts(A("NIH"), A("ID"), -1.0, AL.mult)
-    for t in range(3): act(A("LV", 256 * t, 256 * t + 256), A("Y", t, t + 1276, 5), AF.Copy)
     ms(A("LQ"), 0.0)
     cp(A("NBU", 0, 256), A("NBI", 0, 256)); cp(A("NBU", 256), A("NBI", 256))
-    cp(A("NB", 8, 8 + V), A("NBI"))
-    ts(A("NBC"), A("NBI", 0, G), float(G), AL.min, float(V), AL.add)
+    for c in range(0, V, 256): cp(A("NB", 8 + c, 264 + c), A("NBI", c, c + 256))
+    for c in range(0, G, 352):
+        act(A("NBC", c, c + 352), A("NB", 8 + c, 360 + c), AF.Relu, col("PC", 12), -1.0)
+        act(A("NBC", c, c + 352), A("NBC", c, c + 352), AF.Copy, float(W), -1.0)
     iota(A("IP"), [[1, 128]]); iota(A("IS"), [[1, 192]]); iota(A("SG"), [[16, 81]]); iota(A("SJ"), [[1, 81]])
-    iota(A("ST"), [[16, 12]]); iota(A("RPI"), [[1, 12]])
+    iota(A("ST"), [[16, 12]])
     sel(A("TRI"), A("BO"), [[1, 128]], AL.is_ge, 0, -1)
     sel(A("LT"), A("BO"), [[1, 128]], AL.is_gt, 0, -1)
     iota(A("HM", 0, 128), [[0, 4], [-1, 2], [0, 16]], 1); iota(A("HM", 128, 256), [[0, 4], [1, 2], [0, 16]])
@@ -187,20 +186,22 @@ def rank_program(g, core, T, topo):
             sel(A("HS", 256 * e + 128 * h, 256 * e + 128 * h + 128), A("HM", 128 * h, 128 * h + 128), [[-1, 128]], AL.is_equal, 16 * (h - e), 1)
     send("xf", A("X", V, W), A("X", 0, G))
     send("nb", A("NB", 8 + V, 8 + W), A("NBC"), [col("JK", 0)])
-    fill(A("ASC", V), V); fill(A("X", W), int(DEADX)); fill(A("NB", 0, 8), W); fill(A("NB", 8 + W), W)
-    fill(A("Z", V), 0); fill(A("QT", V), 0)
+    ms(A("ASC", V), V); ms(A("X", W), DEADX); ms(A("NB", 0, 8), float(W)); ms(A("NB", 8 + W), float(W))
+    ms(A("Z", V), 0.0); ms(A("QT", V), 0.0)
     iota(A("CD"), [[1, 3], [0, 32]], 1)
-    iota(A("IOF"), [[1, 1472]]); fill(A("YD"), 0); fill(A("DZ0"), 0); fill(A("DZ1"), 0)
+    iota(A("YD"), [[0, 1440]])
     for q in range(1, 16): act(A("LQ", 129 * q, 128 * q + 128, 16), A("LT", q, 128, 16), AF.Copy, 0.0, 2048.0)
 
     def cand_terms(t):
-        ts(A("TN"), A("NB", 8 + t, 8 + t + 1276, 5), CEN, AL.subtract)
+        ts(A("TN"), A("NB", 8 + t, 8 + t + 1276, 5) if t else A("NBI", 0, 1276, 5), CEN, AL.subtract)
         wrap(A("P5", 0, 16), "FE", "TN", 0, 256)
         ts(A("NO"), A("P5", 0, 16), CEN, AL.add)
-        tt(A("EP"), gat("Y", 0, W, A("NO")), A("LV", 256 * t, 256 * t + 256), AL.subtract)
-        ts(A("C1"), A("EP"), 2.0, AL.is_equal, 64.0, AL.mult)
-        act(A("C2"), A("EP"), AF.Abs, col("PC", 5), 32.0)
-        ts(A("P6", 0, 256), A("C2"), -1.0, AL.mult, 31.5, AL.add)
+        act(A("YN"), gat("Y", 0, W, A("NO")), AF.Copy)
+        mm(A("P5", 256, 512), A("NID"), A("Y", t, t + 1276, 5), True, False)
+        mm(A("P5", 256, 512), A("ID"), A("YN"), False, True)
+        act(A("C2"), A("P5", 256, 512), AF.Abs, col("PC", 5), 32.0)
+        act(A("C1"), A("P5", 256, 512), AF.Relu, 0.0, 32.0)
+        act(A("P6", 0, 256), A("C2"), AF.Copy, 31.5, -1.0)
 
     cand_terms(0)
     for i in range(16):
@@ -210,35 +211,29 @@ def rank_program(g, core, T, topo):
     ts(A("DU"), A("ST"), PQ, AL.add, 1440.0 - CEN, AL.add)
     ts(A("SEG"), A("ST"), 256.0, AL.mult, BIGK, AL.add)
     ts(A("ST"), A("ST"), PQ, AL.add, 0.5, AL.add)
-    cp(A("RP"), A("RPI"))
-    cp(A("OA"), A("ASC", 0, 1276, 5))
     tt(A("LK"), A("LT"), A("N32"), AL.add); tt(A("TRA"), A("TRI"), A("I192"), AL.add); cp(A("HH"), A("HS"))
 
     lo = 0; later = []
-    for j, n in zip(PBANK, PAIRS):
-        pb = "P%d" % j
-        cp(A("GS", 16 * lo, 16 * (lo + n)), gat("Y", 0, W, A("NBU", lo, lo + n)))
-        act(A("GS", 16 * (lo + n), 16 * (lo + 2 * n)), gat("Y", 0, W, A("NBU", lo + n, lo + 2 * n)), AF.Copy)
-        n = 2 * n
-        mm(A(pb, 256, 256 + n), A("ID"), A("Y", lo, lo + n), True, True)
-        mm(A(pb, 0, n), A("NID"), A("Y", lo, lo + n), True, False)
+    for nv, na, pb, at, ay in SUMS:
+        n = nv + na; q, y = A(pb, at, at + n), A(pb, ay, ay + n)
+        cp(A("GS", 16 * lo, 16 * (lo + nv)), gat("Y", 0, W, A("NBU", lo, lo + nv)))
+        act(A("GS", 16 * (lo + nv), 16 * (lo + n)), gat("Y", 0, W, A("NBU", lo + nv, lo + n)), AF.Copy)
+        mm(y, A("ID"), A("Y", lo, lo + n), True, True)
+        mm(q, A("NID"), A("Y", lo, lo + n), True, False)
         for i in range(16):
-            mm(A(pb, 0, n), A("ID"), A("GS", 16 * lo + i, 16 * (lo + n), 16), False, i == 15)
-        act(A("ZA", lo, lo + n), A(pb, 0, n), AF.Abs, col("PC", 6), 0.5)
-        if j in (3, 7): later.append((A("QT", lo, lo + n), A(pb, 0, n)))
-        else: act(A("QT", lo, lo + n), A(pb, 0, n), AF.Copy)
+            mm(q, A("ID"), A("GS", 16 * lo + i, 16 * (lo + n), 16), False, i == 15)
+        act(A("ZA", lo, lo + n), q, AF.Abs, col("PC", 6), 0.5)
+        later.append((A("QT", lo, lo + n), q))
         ts(A("ZA", lo, lo + n), A("ZA", lo, lo + n), 64.5 / 64, AL.min, 64.5 / 64, AL.subtract)
-        tt(A("Z", lo, lo + n), A("ZA", lo, lo + n), A(pb, 256, 256 + n), AL.mult)
+        tt(A("Z", lo, lo + n), A("ZA", lo, lo + n), y, AL.mult)
         lo += n
-    for o, i in later: act(o, i, AF.Copy)
 
     KEY, XP, KO = A("P0", 0, 192), A("P1", 0, 192), A("P1", 192, 384)
     def wrap_t(o, src, first=True, last=True):
-        if first: mm(o, A("ZR"), A("ONE", 0, 12), True, False)
         for e in range(2):
             for h in range(2):
                 mm(A(o[0], o[1] + e, o[2], 2), A("HH", 256 * e + 128 * h, 256 * e + 128 * h + 128), A(src[0], src[1] + h, src[2], 2),
-                   False, last and e + h == 2)
+                   first and e + h == 0, last and e + h == 2)
     def rows(c0, c1, banks, i, n=1):
         per = 16 // len(banks)
         return A("P%d" % banks[i // per], (c1 - c0) * (i % per), (c1 - c0) * (i % per + n))
@@ -248,9 +243,7 @@ def rank_program(g, core, T, topo):
             if how == "max": mm(A("P0", c0, c1), A("BN"), A("XB", c0, c1), False, False)
             if how == "abs":
                 per = 16 // len(banks)
-                for i in range(16):
-                    if i % per == 0: mm(A("P%d" % banks[i // per]), A("ZR"), A("ZA", 0, 512), True, False)
-                    mm(rows(c0, c1, banks, i), A("NID"), A("XB", c0, c1), False, False)
+                for i in range(16): mm(rows(c0, c1, banks, i), A("NID"), A("XB", c0, c1), i % per == 0, False)
     def distances(plan, off, names):
         for c0, c1, q in plan[0]: fetch(q, A("GS", 16 * c0, 16 * c1), gat("X", 0, W + 16, A(off, c0, c1)))
         for c0, c1, how, banks in plan[1]:
@@ -270,27 +263,27 @@ def rank_program(g, core, T, topo):
                     tt(dd(i), gi(i), A("P1", c0, c1), AL.max)
             for i in range(16): mm(key, A("FB" if how == "max" else "FA", 16 - i, 144 - i), dd(i), False, False)
         mm(KEY, A("IDH"), names, False, True)
-    def least(rs):
+    def least(rs, name=True):
         tr(A("TK"), KEY)
         scan(A("TS"), A(rs), A("TK"), 0.0, AL.max, AL.min)
         ts(A("KR", 0, 12), A("TS", 15, 192, 16), RND, AL.add, RND, AL.subtract)
-        tt(A("TC", 0, 12), A("TS", 15, 192, 16), A("KR", 0, 12), AL.subtract)
+        if name: tt(A("TC", 0, 12), A("TS", 15, 192, 16), A("KR", 0, 12), AL.subtract)
 
     parts = [(0, 96, "P0"), (96, 192, "P1"), (192, 256, "P4")]
-    def z_sums(plan, dz):
+    def z_sums(plan, t):
+        for c0, c1 in OAP: cp(A("OA", c0, c1), A("ASC", t + 5 * c0, t + 5 * c1 - 4, 5))
         for c0, c1, q in plan: fetch(q, A("GS", 16 * c0, 16 * c1), gat("Z", 0, V, A("OA", c0, c1)))
         for c0, c2, pb in parts:
             for j in range(16):
-                mm(A(pb, 0, c2 - c0), A("ID"), A("GS", 16 * c0 + j, 16 * c2, 16), j == 0, dz is None and j == 15)
-            if dz: mm(A(pb, 0, c2 - c0), A("ID"), A(dz[0], dz[1] + 5 * c0, dz[1] + 5 * c2 - 4, 5), False, True)
+                mm(A(pb, 384, 384 + c2 - c0), A("ID"), A("GS", 16 * c0 + j, 16 * c2, 16), j == 0, j == 15)
 
-    z_sums(ZG0, None)
+    z_sums(ZG0, 0)
     for t in range(3):
         more = t < 2
         DO, DR, MC = A("DO%d" % t, 0, 2), A("DR%d" % t, 0, 2), "MC%d" % t
         for c0, c2, pb in parts:
-            act(A("SM", c0, c2), A(pb, 0, c2 - c0), AF.Copy, 192.0)
-            tt(A("T1", c0, c2), A(pb, 0, c2 - c0), A("C1", c0, c2), AL.mult)
+            act(A("SM", c0, c2), A(pb, 384, 384 + c2 - c0), AF.Copy, 192.0)
+            tt(A("T1", c0, c2), A(pb, 384, 384 + c2 - c0), A("C1", c0, c2), AL.mult)
             if c0 > 0:
                 c0 = 0 if c2 < 256 else c0
                 tt(A("T2", c0, c2), A("SM", c0, c2), A("P6", c0, c2), AL.mult)
@@ -298,6 +291,8 @@ def rank_program(g, core, T, topo):
                 mm(A("P2", c0, c2), A("BOH"), A("T1", c0, c2), False, False)
                 mm(A("P2", c0, c2), A("BO"), A("T2", c0, c2), False, True)
         ts(A("WL", 0, 256), A("P2", 0, 256), col("EF", 0), AL.is_le)
+        if t == 0:
+            for o, i in later: act(o, i, AF.Copy)
         scan(A("CC"), A("WL"), A("C32"), 0.0, AL.add, AL.min)
         act(A("JK", 0, 288), A("CC"), AF.Sign, col("ST", 0), -1.0, col("AD", 0))
         ts(A("JK", 288, 576), A("CC"), col("ST", 1), AL.is_le)
@@ -349,7 +344,6 @@ def rank_program(g, core, T, topo):
         if more:
             mm(A("P7", 64, 256), A("BO"), A("CM"), True, True)
             ts(A("DF", 80, 160), A("CU", 0, 80), 192.0, AL.is_gt, 512.0, AL.mult)
-            cp(A("OA"), A("ASC", t + 1, t + 1277, 5))
             cp(col("EI", 0), col("P7", 0))
             ts(A("RG", 0, 192), A("P7", 64, 256), col("PC", 10) if t else PQ, AL.is_equal)
             ts(col("EI", 1), col("EI", 0), 7, AL.bitwise_and)
@@ -365,7 +359,10 @@ def rank_program(g, core, T, topo):
         key_open(NEAR)
         ts(A("LH"), A("LU"), CEN, AL.subtract)
         ts(A("DP", 0, 12), B, float(V), AL.is_ge)
-        ts(A("BH"), gat("IOF", 0, 1472, B), CEN, AL.subtract)
+        ts(A("BH"), B, CEN, AL.subtract)
+        BP = A("P2", 320, 512)
+        for q in range(16): mm(A("P2", 320 + q, 512, 16), A("SEL", 128 * q, 128 * q + 128), A("BH"), q == 0, q == 15)
+        if more: tt(A("RB"), BP, A("RG", 0, 192), AL.mult)
         distances(NEAR, "LU", A("LH"))
         def pslab(i): return A("P%d" % EQB[i // 2 % len(EQB)], 192 * (i % 2), 192 * (i % 2) + 192)
         def sel_mm(i): mm(pslab(i), A("SEL", 128 * i, 128 * i + 128), A("LH"), True, True)
@@ -374,119 +371,110 @@ def rank_program(g, core, T, topo):
         wrap_t(A("P2", 256, 268), A("TC", 0, 12))
         ts(A("UO"), A("P2", 256, 268), CEN + 8, AL.add)
         cp(A("MU"), gat("NB", 0, W + 16, A("UO")))
-        wrap(A("P3", 0, 12), "F4", "SD", 0, 192)
-        mm(A("P3", 256, 448), A("LK"), A("SD"), True, True)
-        act(A("ND"), A("P3", 0, 12), AF.Copy, 65536.0 - 2000)
-        ts(KO, A("P3", 256, 448), col("PC", 3), AL.is_equal)
+        mm(KO, A("LK"), A("SD"), True, True)
+        wrap(A("P1", 384, 396), "F4", "SD", 0, 192)
+        ts(KO, KO, col("PC", 3), AL.is_equal)
+        act(A("ND"), A("P1", 384, 396), AF.Copy, 65536.0 - 2000)
         for i in range(2 * len(EQB)): sel_mm(i)
         key_open(OFFER)
         tt(A("UF"), A("P2", 256, 268), A("ND"), AL.min)
+        ts(A("MH"), A("MU"), CEN, AL.subtract)
+        tt(slab("EQ", 16), BP, A("MH"), AL.is_equal)
+        mm(KEY, A("IDB"), slab("EQ", 16), False, False)
         ts(A("AK", 0, 12), A("UF"), V - CEN, AL.is_ge)
         ts(A("DP", 16, 28), A("ND"), 0.0, AL.is_lt)
         scan(A("AK", 17, 29), A("AK", 0, 12), A("ONE", 0, 12), 0.0, AL.add, AL.mult)
+        tt(A("KL"), A("LH"), KO, AL.mult)
         mm(A("P2", 272, 284), A("I256"), A("DP", 0, 12), True, False)
         mm(A("P2", 272, 284), A("I256"), A("DP", 16, 28), False, False)
         mm(A("P2", 272, 284), A("TRA"), A("AK", 0, 12), False, False)
         mm(A("P2", 272, 284), A("BO"), A("AK", 16, 28), False, True)
+        mm(A("P2", 0, 192), A("BOH"), A("KL"), True, True)
         ts(A("DP", 32, 44), A("P2", 272, 284), 224.0, AL.is_gt)
         for q in range(16): mm(A("P0", q, 192, 16), A("SELB", 128 * q, 128 * q + 128), A("DP", 32, 44), False, False)
-        tt(A("KL"), A("LH"), KO, AL.mult)
-        mm(A("P2", 0, 192), A("BOH"), A("KL"), True, True)
-        if more: wrap(A("P2", 288, 300), "FH", "KL", 0, 192)
         tr(A("TF"), A("P2", 0, 192))
-        if more: ts(A("OO"), A("P2", 288, 300), CEN, AL.add)
         tt(A("RS2", 0, 192, 16), A("TF", 15, 192, 16), A("SEG"), AL.add)
-        ts(A("MH"), A("MU"), CEN, AL.subtract)
-        tt(slab("EQ", 16), A("BH"), A("MH"), AL.is_equal)
-        mm(KEY, A("IDB"), slab("EQ", 16), False, False)
         for i in range(16):
             tt(slab("EQ", i), pslab(i), A("MH"), AL.is_equal)
             mm(KEY, A("IDB"), slab("EQ", i), False, False)
             if i % 2 == 1 and i + 2 * len(EQB) < 17:
                 sel_mm(i + 2 * len(EQB) - 1); sel_mm(i + 2 * len(EQB))
         if more:
-            act(A("YB"), gat("Y", 0, 1472, B), AF.Copy, 0.0, -0.5)
-            act(A("YO"), gat("Y", 0, W + 16, A("OO")), AF.Copy)
-            tt(A("QP"), gat("QT", 0, 1472, B), A("YO"), AL.subtract)
-            act(A("FZ", 0, 192), A("QP"), AF.Abs, col("PC", 12), 0.5)
-            act(A("FZ", 192, 384), A("QP"), AF.Abs, col("PC", 13), 0.5)
-            act(A("FZ"), A("FZ"), AF.Relu, col("PC", 11), -1.0)
-            ts(A("RB"), A("BH"), CEN, AL.add)
-            tt(A("RB"), A("RB"), A("RG", 0, 192), AL.mult)
+            act(A("YB"), gat("Y", 0, 1472, B), AF.Copy, 0.0, -1.0)
+            act(A("QP"), gat("QT", 0, 1472, B), AF.Copy)
         distances(OFFER, "MU", A("MH"))
         if more:
-            for o, s in ((0, "ID"), (192, "NID")):
-                mm(A("P3", o, o + 192), A("ID"), A("FZ", 0, 192), True, False)
-                mm(A("P3", o, o + 192), A(s), A("FZ", 192, 384), False, True)
-            tt(A("ZC"), A("P3", 0, 192), A("YB"), AL.mult)
-            tt(A("ZS"), A("P3", 192, 384), A("YB"), AL.mult)
+            wrap(A("P6", 0, 12), "FH", "KL", 0, 192)
+            ts(A("OO"), A("P6", 0, 12), CEN, AL.add)
+            act(A("YO"), gat("Y", 0, W + 16, A("OO")), AF.Copy)
         LST = A("P4", 0, 192)
         mm(LST, A("KC"), A("ONE", 0, 192), True, False)
         mm(LST, A("IDH"), A("LH"), False, False)
         mm(LST, A("NIH"), A("KL"), False, not more)
-        least("RS2")
-        tt(A("KN", 0, 12), A("TS", 15, 192, 16), A("KR", 0, 12), AL.subtract)
+        least("RS2", more)
+        tt(A("NMS", 0, 192, 16), A("TS", 15, 192, 16), A("KR", 0, 12), AL.subtract)
+        scan(A("TH"), A("RM"), A("NMS"), 0.0, AL.mult, AL.add)
+        tr(A("WR"), A("TH"))
         if not more:
             act(A("LW"), LST, AF.Copy)
-            cp(A("TH"), gat("KN", 0, 12, A("RP")))
-            tr(A("WR"), A("TH"))
             tt(A("LF"), A("WR"), KO, AL.mult)
             tt(gat("NB", 8, 1480, B), A("LF"), A("LW"), AL.add)
             store("S", T.yn[:, 0:640], A("NB", 8, 648), "s_y0")
             store("A", T.yn[:, 640:V], A("NB", 648, 8 + V), "s_y1")
             break
+        ts(A("TC", 16, 28), A("TS", 15, 192, 16), BIGK - 2048, AL.is_ge, 4096.0, AL.mult)
+        ts(A("TC", 32, 44), A("TC", 0, 12), V - CEN, AL.is_ge, 4096.0, AL.mult)
         wrap_t(A("P5", 0, 12), A("TC", 0, 12))
+        wrap_t(A("P2", 304, 316), A("TC", 16, 28), True, False); wrap_t(A("P2", 304, 316), A("TC", 0, 12), False, True)
+        cp(A("WF", 0, 12), A("P2", 304, 316))
+        ts(A("WO", 12, 24), A("P2", 304, 316), CEN, AL.add, 1440.0, AL.min)
         ts(A("WO", 0, 12), A("P5", 0, 12), CEN, AL.add)
-        tt(A("ZW"), gat("Y", 0, W + 16, A("WO", 0, 12)), A("ZS"), AL.mult)
-        tt(gat("Z", 0, 1472, B), A("ZW"), A("ZC"), AL.add)
-        cp(A("TH"), gat("KN", 0, 12, A("RP")))
-        tr(A("WR"), A("TH"))
+        act(A("YW"), gat("Y", 0, W + 16, A("WO", 0, 12)), AF.Copy)
+        mm(A("P3", 0, 192), A("ID"), A("QP"), True, False)
+        mm(A("P3", 0, 192), A("NID"), A("YO"), False, False)
+        mm(A("P3", 0, 192), A("ID"), A("YW"), False, True)
+        act(A("FZ"), A("P3", 0, 192), AF.Abs, col("PC", 6), 0.5)
+        act(A("FZ"), A("FZ"), AF.Relu, col("PC", 11), -1.0)
+        tt(gat("Z", 0, 1472, B), A("FZ"), A("YB"), AL.mult)
+        if t == 0:
+            act(A("QN"), A("P3", 0, 192), AF.Copy)
+            cp(gat("QT", 0, 1472, B), A("QN"))
         tt(A("TW"), A("WR"), KO, AL.mult)
         mm(LST, A("IDH"), A("TW"), False, True)
         act(A("MS"), LST, AF.Copy)
-        ts(A(MC, 0, 192), A("MS"), float(G), AL.min, float(V), AL.add)
+        act(A("MD"), LST, AF.Relu, col("PC", 12), -1.0)
+        act(A(MC, 0, 192), A("MD"), AF.Copy, float(W), -1.0)
         send("u%d" % t, A("MR%d" % t), A(MC))
         cp(gat("NB", 8, 1480, B), A("MS"))
-        if t == 0:
-            tt(A("QN"), gat("Y", 0, W + 16, A("WO", 0, 12)), A("QP"), AL.add)
-            cp(gat("QT", 0, 1472, B), A("QN"))
-        ts(A("KR", 16, 28), A("TS", 15, 192, 16), RND, AL.add, RND + BIGK - 4096, AL.subtract)
-        tt(A("TC", 16, 28), A("KN", 0, 12), A("KR", 16, 28), AL.max)
-        ts(A("TC", 32, 44), A("KN", 0, 12), V - CEN, AL.is_ge, 4096.0, AL.mult)
-        wrap_t(A("P2", 304, 316), A("TC", 16, 28))
-        wrap_t(A("P7", 0, 12), A("TC", 16, 28), True, False)
-        wrap_t(A("P7", 0, 12), A("TC", 32, 44), False, False)
-        cp(A("WF", 0, 12), A("P2", 304, 316))
-        ts(A("WO", 12, 24), A("P2", 304, 316), CEN, AL.add, 1440.0, AL.min)
-        mm(A("P6", 256, 448), A("ZR"), A("ONE", 0, 192), True, False)
+        for k, c in enumerate((16, 0, 32)): wrap_t(A("P7", 0, 12), A("TC", c, c + 12), k == 0, False)
         for c in range(12):
             ts(A("EE", 208 * c, 192 * (c + 1)), A("WR", 16 * c, 192), col("WF", c), AL.is_equal)
-            if c < 11: mm(A("P6", 256 + 16 * (c + 1), 448), A("BO"), A("EE", 208 * c + 16, 192 * (c + 1)), False, c == 10)
-        act(A("LS"), A("P6", 256, 448), AF.Sign)
+            if c < 11: mm(A("P6", 256 + 16 * (c + 1), 448), A("BO"), A("EE", 208 * c + 16, 192 * (c + 1)), c == 0, c == 10)
+        act(A("LS", 16, 192), A("P6", 272, 448), AF.Sign)
         for q in range(1, 16):
             mm(A("P7", 0, 12), A("LQ", 128 * q, 128 * q + 128), A("EE", q, 2304, 208), False, False)
-        wrap(A("P7", 0, 12), "FA", "LS", 0, 192, False, True)
+        for q in range(16): mm(A("P7", 1, 12), A("FA", 16 - q, 144 - q), A("LS", 16 + q, 192, 16), False, q == 15)
         tt(A("WF", 12, 24), A("P7", 0, 12), A("DU"), AL.min)
         ts(A("WS"), A("WF", 12, 24), CEN, AL.add)
-        tt(A("TA"), gat("ASC", 0, 1632, A("WO", 12, 24)), A("RG", 0, 192), AL.mult)
-        wrap(A("P2", 288, 300), "FH", "TA", 0, 192)
-        cp(A("OZ"), A("P2", 288, 300))
-        act(A("ZN"), gat("Z", 0, 1472, B), AF.Copy)
-        act(A("ZO"), gat("Z", 0, 1472, A("OZ")), AF.Copy, 0.0, -1.0)
-        tt(gat("DZ%d" % t, 0, 1632, A("WS")), A("ZN"), A("ZO"), AL.add)
         tt(A("MA"), gat("ASC", 0, 1632, A("WO", 12, 24)), A("RG", 192, 384), AL.mult)
-        mm(A("P3", 0, 192), A("IDH"), A("RB"), True, False)
-        mm(A("P3", 0, 192), A("IDH"), A("MA"), False, True)
-        act(A("L2"), A("P3", 0, 192), AF.Copy)
-        cand_terms(t + 1)
-        z_sums(ZG1, ("DZ%d" % t, t + 1))
+        mm(A("P3", 256, 448), A("IDH"), A("RB"), True, False)
+        mm(A("P3", 256, 448), A("ICN"), A("RG", 0, 192), False, False)
+        mm(A("P3", 256, 448), A("IDH"), A("MA"), False, True)
+        act(A("L2"), A("P3", 256, 448), AF.Copy)
         cp(gat("ASC", 0, 1632, A("WS")), A("L2"))
+        cand_terms(t + 1)
+        z_sums(ZG1, t + 1)
 
     emit_all(ops, Q, T)
 
 
-CY, PCY, LAT = 0.83e-3, 0.45e-3, 0.2
+LAT = 0.18
+CY, PCY = 0.83e-3, 0.45e-3
 WIDE = {"float32": 4, "int32": 4}
+PASSES = 2
+FIRST = 3.0
+RATE = 60e3
+REACH = 300
 PLAN = {}
 
 
@@ -500,7 +488,7 @@ def call_time(q, kind, outs, ins):
     if kind in ("dma", "send"):
         a = full[0] if kind == "dma" else ins[0]
         by = 128 * span(a) * WIDE.get(SB[a[0]][1], 2)
-        return (0.1, 1.6 + by / 180e3) if kind == "dma" else (0.3, 1.3 + by / 60e3)
+        return (by / 300e3, 1.0 + by / 300e3) if kind == "dma" else (FIRST if a[0] == "Y" else 0.3, 1.3 + by / RATE)
     if q == "P": t = max(64, span(ins[1])) * PCY * (4 if SB[ins[1][0]][1] == "float32" else 1)
     elif q == "G": t = 0.17 + 2 * span(full[0]) * CY
     elif full[0][5]: t = 0.05 + 3.8 * span(full[0]) * CY
@@ -535,24 +523,52 @@ def conflicts(ops):
     return deps
 
 
+def place(ops, order, edge, free):
+    busy = {}; start = [0.0] * len(ops)
+    for k in order:
+        t = max([start[m] + lag for m, lag in edge[k].items()] + [free[k]])
+        c = ops[k][5][0]; line = busy.setdefault(ops[k][0], [])
+        j = len(line)
+        while j > 0 and line[j - 1][1] > t: j -= 1
+        while j < len(line) and t + c > line[j][0] + 1e-9:
+            t = max(t, line[j][1]); j += 1
+        line.insert(j, (t, t + c)); start[k] = t
+    return start
+
+
 def arrange(ops, deps):
     n = len(ops)
     edge = [dict((m, ops[m][5][1] + LAT if w else ops[m][5][0]) for m, w in d.items()) for d in deps]
     for k, o in enumerate(ops):
         if o[0] == "X": edge[k][k - 1] = ops[k - 1][5][1] + 1.0
+    back = [{} for _ in ops]
     tail = [o[5][1] for o in ops]
+    floor = [0.0] * n; below = [0] * n; line = {}
     for k in range(n - 1, -1, -1):
-        for m, lag in edge[k].items(): tail[m] = max(tail[m], lag + tail[k] + 1e-6)
-    busy = {}; start = [0.0] * n
-    for k in sorted(range(n), key=lambda k: (-tail[k], k)):
-        t = max([start[m] + lag for m, lag in edge[k].items()], default=0.0)
-        c = ops[k][5][0]; line = busy.setdefault(ops[k][0], []); at = len(line)
-        for j, (a, b) in enumerate(line):
-            if t + c <= a + 1e-9:
-                at = j; break
-            t = max(t, b)
-        line.insert(at, (t, t + c)); start[k] = t
-    return sorted(range(n), key=lambda k: (start[k], -tail[k], k))
+        for q, calls in line.items():
+            load = 0.0
+            for rest, d in calls[:-REACH:-1]:
+                if below[k] >> d & 1:
+                    load += ops[d][5][0]
+                    tail[k] = max(tail[k], ops[k][5][1] + LAT + load + rest)
+        tail[k] = max(floor[k], tail[k] + URGE.get(ops[k][0] + (ops[k][3][0][0] if ops[k][3] else ""), 0.0))
+        calls = line.setdefault(ops[k][0], []); j = len(calls); rest = tail[k] - ops[k][5][0]
+        while j > 0 and calls[j - 1][0] > rest: j -= 1
+        calls.insert(j, (rest, k))
+        for m, lag in edge[k].items():
+            tail[m] = max(tail[m], lag + tail[k])
+            floor[m] = max(floor[m], tail[k] + 1e-6)
+            below[m] |= below[k] | 1 << k
+            back[m][k] = lag + ops[k][5][0] - ops[m][5][0]
+    order = sorted(range(n), key=lambda k: (-tail[k], k)); best = None
+    for _ in range(PASSES):
+        start = place(ops, order, edge, [0.0] * n)
+        end = max(start[k] + ops[k][5][1] for k in range(n))
+        if best is None or end < best[0]: best = (end, start)
+        late = place(ops, sorted(range(n), key=lambda k: (-start[k] - ops[k][5][0], -k)), back, [o[5][1] - o[5][0] for o in ops])
+        order = sorted(range(n), key=lambda k: (-late[k] - ops[k][5][0], k))
+    PLAN["end"] = best[0]
+    return sorted(range(n), key=lambda k: (best[1][k], k))
 
 
 def emit_all(ops, Q, T):

from concourse.mybir import AluOpType as AL, ActivationFunctionType as AF, AxisListType as AX

V, G, W = 1280, 1056, 2336
CEN = 1168.0
BIGK = 4096.0 * 4000
RND = 1.5 * 2 ** 35
DEADX = 131072.0
LOSS0 = 192 * 31.5 * 16
SUMS = [(128, 128, "P0", 0, 256), (128, 128, "P1", 0, 256), (128, 128, "P4", 0, 256), (112, 112, "P3", 0, 256), (72, 72, "P7", 16, 256), (40, 40, "P7", 160, 400), (32, 32, "P2", 256, 320)]
NSTEP = 30
NEAR = ([(0, 32, "V"), (32, 64, "A"), (64, 128, "V"), (128, 192, "A")], [(0, 64, "abs", [3, 4]), (64, 128, "max", []), (128, 192, "max", [])])
OFFER = ([(0, 64, "A"), (64, 128, "A"), (128, 160, "A"), (160, 192, "V")], [(0, 64, "abs", [3, 4]), (64, 128, "sub", []), (128, 192, "max", [])])
EQB = [5, 6, 7]
OAP = [(0, 96), (96, 256)]
ZG0 = [(0, 48, "V"), (48, 96, "A"), (96, 144, "V"), (144, 192, "A"), (192, 224, "V"), (224, 256, "A")]
ZG1 = ZG0
URGE = {"VTW": 1.0, "AMS": 1.0, "VNB": 1.0, "VZ": 1.0, "AFZ": 1.0, "AYN": 1.0, "VTN": 1.0}

SB = {
    "NBI": (1280, "int32"), "NBU": (1280, "uint16"), "NB": (2760, "float32"), "NBC": (1056, "float32"),
    "ASC": (1632, "int32"), "X": (2880, "bfloat16"), "Y": (2352, "bfloat16"), "GS": (20480, "bfloat16"),
    "Z": (1472, "bfloat16"), "QT": (1472, "bfloat16"), "ZA": (1280, "bfloat16"), "YD": (1440, "float32"),
    "ONE": (384, "bfloat16"), "BO": (128, "bfloat16"), "BN": (128, "bfloat16"), "ID": (128, "bfloat16"), "NID": (128, "bfloat16"), "ICN": (128, "bfloat16"),
    "ID16": (128, "bfloat16"), "IDB": (128, "bfloat16"), "IDF": (128, "float32"), "IDH": (128, "float16"), "NIH": (128, "float16"),
    "BOH": (128, "float16"), "BO4": (128, "bfloat16"), "TRI": (128, "bfloat16"), "TRA": (128, "bfloat16"), "I256": (128, "bfloat16"),
    "LK": (128, "bfloat16"), "N32": (128, "bfloat16"), "I192": (128, "bfloat16"),
    "O16": (128, "bfloat16"), "SEL": (2048, "float16"), "SELB": (2048, "bfloat16"), "QM": (16, "float32"), "QB": (16, "float32"),
    "F1": (144, "bfloat16"), "FA": (144, "bfloat16"), "FB": (144, "bfloat16"), "FN": (144, "bfloat16"),
    "FH": (144, "float16"), "FE": (144, "float16"),
    "KU": (128, "bfloat16"), "KC": (128, "bfloat16"), "KT": (192, "float32"),
    "PI": (8, "int32"), "PC": (16, "float32"), "IP": (128, "bfloat16"), "IS": (192, "bfloat16"),
    "SG": (81, "float32"), "SJ": (81, "bfloat16"), "ST": (12, "float32"), "DU": (12, "float32"), "SEG": (12, "float32"),
    "RS1": (192, "float32"), "RS2": (192, "float32"), "RM": (192, "float16"), "NMS": (192, "float16"), "C32": (288, "bfloat16"),
    "CX": (32, "bfloat16"), "CD": (96, "float32"), "JK": (1680, "bfloat16"), "HM": (256, "bfloat16"), "HS": (512, "bfloat16"), "HH": (512, "float16"),
    "TC": (64, "float16"), "F4": (144, "bfloat16"), "ND": (12, "float32"), "AK": (32, "bfloat16"), "DP": (48, "bfloat16"),
    "OA": (256, "uint16"), "NO": (16, "uint16"), "YN": (256, "bfloat16"), "C1": (256, "bfloat16"), "C2": (256, "bfloat16"),
    "SM": (256, "bfloat16"), "T1": (256, "float16"), "TN": (256, "float16"), "T2": (256, "bfloat16"), "WL": (288, "bfloat16"), "CC": (288, "bfloat16"),
    "EI": (8, "int32"), "EF": (8, "float32"), "AC": (12, "float32"), "AD": (8, "float32"), "DV": (8, "float32"), "DX": (8, "uint16"),
    "DO0": (8, "uint16"), "DO1": (8, "uint16"), "DO2": (8, "uint16"), "DR0": (8, "uint16"), "DR1": (8, "uint16"), "DR2": (8, "uint16"),
    "NA": (34, "float32"), "NJ": (8, "float32"), "LI": (34, "int32"), "LO": (34, "float32"), "OH": (32 * 128, "bfloat16"), "SN": (32 * 81, "bfloat16"),
    "CS": (80, "float32"), "FL": (92, "bfloat16"), "FS": (93, "bfloat16"), "CU": (96, "float32"), "DF": (160, "float32"), "DG": (80, "float32"), "CT": (81, "float32"),
    "HU": (12, "uint16"), "HB": (12, "bfloat16"), "CM": (192, "bfloat16"), "BU": (12, "uint16"),
    "LU": (192, "uint16"), "LH": (192, "float16"), "LF": (192, "float32"), "LW": (192, "float32"), "XB": (192, "bfloat16"), "DD": (3072, "bfloat16"), "EQ": (17 * 192, "bfloat16"),
    "TK": (192, "float32"), "TF": (192, "float32"), "TS": (192, "float32"), "KR": (16, "float32"), "TH": (192, "float16"), "TW": (192, "float16"),
    "SD": (192, "bfloat16"), "KL": (192, "float16"), "UO": (12, "uint16"), "UF": (12, "float32"),
    "L2": (192, "float32"), "MU": (192, "uint16"), "MH": (192, "float16"), "MA": (192, "float16"), "BH": (12, "float16"),
    "OO": (12, "uint16"), "QP": (192, "bfloat16"), "YO": (192, "bfloat16"), "YB": (192, "bfloat16"), "YW": (192, "bfloat16"), "FZ": (192, "bfloat16"),
    "RG": (384, "bfloat16"), "RB": (192, "float16"), "LQ": (2048, "bfloat16"), "WS": (12, "uint16"), "LT": (128, "bfloat16"),
    "WR": (192, "float16"), "WO": (24, "uint16"), "WF": (48, "float32"), "QN": (192, "bfloat16"), "EE": (12 * 192, "bfloat16"), "LS": (192, "bfloat16"),
    "MS": (192, "float32"), "MD": (192, "float32"), "MC0": (204, "float32"), "MC1": (204, "float32"), "MR0": (204, "float32"), "MR1": (204, "float32"), "MO": (12, "uint16"),
}
PLACE = {}
SCRATCH = {}
for _k, (_n, _d) in SB.items():
    if _n <= 200 and _k[:2] not in ("DO", "DR"):
        _at = SCRATCH.get("pool_" + _d, (0, [128, 0]))[1][1]
        PLACE[_k] = ("pool_" + _d, _at)
        SCRATCH["pool_" + _d] = ("sbuf", [128, _at + (_n + 15) // 16 * 16], _d)
    else:
        SCRATCH[_k] = ("sbuf", [128, _n], _d)
for _b in range(8):
    SCRATCH["P%d" % _b] = ("psum", [128, 512], "float32")
LOADS = ["l_lab", "l_nb", "l_asc", "l_xf", "s_yd", "s_y0", "s_y1"]
MSGS = ["lab", "xf", "nb", "d0", "d1", "d2", "u0", "u1"]
SEMAPHORES = ["qV", "qA", "qP", "qG"] + LOADS + ["r_" + m for m in MSGS] + ["w_" + m for m in MSGS]


def A(name, lo=None, hi=None, st=None, p=None, ind=None):
    n = SB[name][0] if name in SB else 512
    return (name, 0 if lo is None else lo, n if hi is None else hi, st, p, ind)


def rank_program(g, core, T, topo):
    rank = T.rank_of(core)
    if rank is None:
        return
    dst = T.cores[(rank - 1) % len(T.cores)]
    rid, pid = topo.addr(dst)[0], topo.addr(dst)[1]
    mask = topo.mask(core, dst)
    ne = len(topo.engines(core, dst))
    Q = {"V": g.vector, "A": g.scalar, "P": g.tensor, "G": g, "S": g.sync}
    ops = []

    def R(a):
        if not isinstance(a, tuple):
            return a
        ps = slice(None) if a[4] is None else slice(*a[4])
        nm, at = PLACE.get(a[0], (a[0], 0))
        r = T[nm][ps, at + a[1]:at + a[2]:a[3]] if a[3] else T[nm][ps, at + a[1]:at + a[2]]
        return r.indirect(R(a[5])) if a[5] else r

    def add(q, emit, outs, ins, token=None, kind=None):
        rd = [a for a in ins if isinstance(a, tuple)]
        rd = rd + [a[5] for a in rd + outs if a[5]]
        ops.append([q, emit, rd, outs, token, call_time(q, kind, outs, ins), kind])

    def cp(o, i): add("V", lambda: g.vector.tensor_copy(R(o), R(i)), [o], [i])
    def tt(o, a, b, op): add("V", lambda: g.vector.tensor_tensor(R(o), R(a), R(b), op), [o], [a, b], None, "tt")
    def ts(o, a, s1, op0, s2=None, op1=None):
        if op1 is None:
            add("V", lambda: g.vector.tensor_scalar(R(o), R(a), R(s1), None, op0), [o], [a, s1])
        else:
            add("V", lambda: g.vector.tensor_scalar(R(o), R(a), R(s1), R(s2), op0, op1), [o], [a, s1, s2])
    def scan(o, a, b, init, op0, op1): add("V", lambda: g.vector.tensor_tensor_scan(R(o), R(a), R(b), init, op0, op1), [o], [a, b])
    def tr(o, i): add("V", lambda: g.vector.transpose(R(o), R(i)), [o], [i])
    def ms(o, c): add("V", lambda: g.vector.memset(R(o), c), [o], [])
    def act(o, i, f, bias=0.0, scale=1.0, acc=None):
        if acc is None:
            add("A", lambda: g.scalar.activation(R(o), R(i), f, bias=R(bias), scale=R(scale)), [o], [i, bias, scale])
        else:
            add("A", lambda: g.scalar.activation(R(o), R(i), f, bias=R(bias), scale=scale, accum_out=R(acc)), [o, acc], [i, bias])
    def mm(o, l, r, start, stop):
        add("P", lambda: g.tensor.matmul(R(o), R(l), R(r), start, stop), [o], [l, r], None, None if start or stop else "mid")
    def iota(o, pat, base=0, cm=0):
        if SB[o[0]][1] == "int32":
            add("G", lambda: g.iota(R(o), pat, base, cm), [o], [])
        else:
            add("G", lambda: g.iota(R(o), pat, base, cm, allow_small_or_imprecise_dtypes=True), [o], [])
    def sel(o, i, pat, op, base, cm): add("G", lambda: g.affine_select(R(o), R(i), pat, op, 0.0, base, cm), [o], [i])
    def load(q, o, src, sem): add(q, lambda: Q[q].dma_start(R(o), src).then_inc(T.sem[sem], 16), [o], [], (sem, 16), "dma")
    def store(q, d, i, sem): add(q, lambda: Q[q].dma_start(d, R(i)).then_inc(T.sem[sem], 16), [], [i], (sem, 16), "dma")
    def send(m, o, i, after=()):
        add("G", lambda: g.remote_dma(R(o), R(i), T.sem["r_" + m], T.sem["w_" + m], pid, rid, mask), list(after), [i], ("w_" + m, ne), "send")
        add("X", None, [o], [], ("r_" + m, ne), "wait")
    def wrap(o, f, buf, lo, n, first=True, last=True):
        for q in range(16):
            mm(o, A(f, 16 - q, 144 - q), A(buf, lo + q, lo + n, 16), first and q == 0, last and q == 15)
    def col(name, c): return A(name, c, c + 1)
    def gat(name, lo, hi, off): return A(name, lo, hi, ind=off)
    def slab(name, i, n=1): return A(name, 192 * i, 192 * (i + n))
    def fetch(q, o, i):
        if q == "V": cp(o, i)
        else: act(o, i, AF.Copy)
    PQ, P16 = col("PC", 0), col("PC", 1)

    load("S", A("Y", 0, V), T.lab[:], "l_lab")
    load("S", A("NBI"), T.nb[:], "l_nb")
    iota(col("PI", 0), [[0, 1]], 0, 1)
    ms(A("ONE"), 1.0)
    iota(A("KT"), [[0, 12], [1, 16]])
    sel(A("BO"), A("ONE", 0, 128), [[-16, 8], [0, 16]], AL.is_ge, 0, 1)
    sel(A("BO"), A("BO"), [[16, 8], [0, 16]], AL.is_ge, 15, -1)
    sel(A("ID"), A("ONE", 0, 128), [[-1, 128]], AL.is_equal, 0, 1)
    send("lab", A("Y", V, W), A("Y", 0, G), [col("JK", 0), col("X", 0), col("ASC", 0)])
    load("S", A("X", 0, V), T.xf[:], "l_xf")
    load("S", A("ASC", 0, V), T.asc[:], "l_asc")
    for f in ["F1", "FA", "FB", "FN", "F4", "FH", "FE", "KU", "KC", "NMS"]: ms(A(f), 0.0)
    ms(col("AK", 16), 0.0)
    ts(col("PI", 1), col("PI", 0), 15, AL.bitwise_and)
    ms(A("Y", W), 0.0); ms(A("WL", 256), 1.0); ms(A("C32"), 32.0); ms(A("CX"), DEADX)
    cp(PQ, col("PI", 1))
    tt(P16, col("PI", 0), col("PI", 1), AL.subtract)
    ms(A("FL", 80), 1.0); ms(col("FS", 0), 0.0); ms(col("CT", 0), 0.0); ms(A("O16"), 1.0 / 16); ms(col("EF", 0), LOSS0)
    ms(col("PC", 5), 31.5); ms(col("PC", 6), -31.5 / 64); ms(col("PC", 7), -1.6e7)
    ms(col("PC", 12), float(G)); ms(A("RM"), 1.0); ms(A("RM", 0, 192, 16), 0.0)
    ts(A("QM"), A("KT", 0, 16), PQ, AL.is_equal)
    ts(A("QB"), A("QM"), 2.0 ** 25, AL.mult)
    ms(A("RS1"), -1e9); ms(A("RS2"), -1e9); ms(A("RS1", 0, 192, 16), BIGK - CEN - 8)
    ms(col("PC", 11), 64.5 / 64)
    ts(col("PC", 8), PQ, 1.0, AL.is_lt, 16.0, AL.mult)
    ts(col("PC", 10), col("PC", 8), PQ, AL.add, -1.0, AL.add)
    ts(col("PC", 3), PQ, -1.0, AL.mult, -32.0, AL.add)
    ts(A("FE", 16, 144, 16), A("BO", 0, 128, 16), col("QM", 0), AL.mult)
    cp(A("FH", 16, 144, 16), A("BO", 0, 128, 16))
    for f, c in [("F1", 1.0), ("FA", 65536.0), ("FB", 131072.0), ("FN", -65536.0), ("F4", 4096.0)]:
        act(A(f, 16, 144, 16), A("BO", 0, 128, 16), AF.Copy, 0.0, c)
    for f, s, c in [("NID", "ID", -1.0), ("ID16", "ID", 16.0), ("IDB", "ID", 2.0 ** 25), ("IDF", "ID", 1.0), ("N32", "ID", -32.0), ("BO4", "BO", 192.0),
                    ("BN", "BO", -65536.0), ("I192", "ID", 192.0), ("I256", "ID", 256.0), ("ICN", "ID", CEN)]:
        act(A(f), A(s), AF.Copy, 0.0, c)
    act(A("KU", p=(0, 1)), A("KT", 0, 128, p=(0, 1)), AF.Copy, 0.0, 4096.0)
    ms(A("KC", p=(0, 1)), CEN)
    cp(A("BOH"), A("BO")); cp(A("IDH"), A("ID")); ts(A("NIH"), A("ID"), -1.0, AL.mult)
    ms(A("LQ"), 0.0)
    cp(A("NBU", 0, 256), A("NBI", 0, 256)); cp(A("NBU", 256), A("NBI", 256))
    for c in range(0, V, 256): cp(A("NB", 8 + c, 264 + c), A("NBI", c, c + 256))
    for c in range(0, G, 352):
        act(A("NBC", c, c + 352), A("NB", 8 + c, 360 + c), AF.Relu, col("PC", 12), -1.0)
        act(A("NBC", c, c + 352), A("NBC", c, c + 352), AF.Copy, float(W), -1.0)
    iota(A("IP"), [[1, 128]]); iota(A("IS"), [[1, 192]]); iota(A("SG"), [[16, 81]]); iota(A("SJ"), [[1, 81]])
    iota(A("ST"), [[16, 12]])
    sel(A("TRI"), A("BO"), [[1, 128]], AL.is_ge, 0, -1)
    sel(A("LT"), A("BO"), [[1, 128]], AL.is_gt, 0, -1)
    iota(A("HM", 0, 128), [[0, 4], [-1, 2], [0, 16]], 1); iota(A("HM", 128, 256), [[0, 4], [1, 2], [0, 16]])
    for e in range(2):
        for h in range(2):
            sel(A("HS", 256 * e + 128 * h, 256 * e + 128 * h + 128), A("HM", 128 * h, 128 * h + 128), [[-1, 128]], AL.is_equal, 16 * (h - e), 1)
    send("xf", A("X", V, W), A("X", 0, G))
    send("nb", A("NB", 8 + V, 8 + W), A("NBC"), [col("JK", 0)])
    ms(A("ASC", V), V); ms(A("X", W), DEADX); ms(A("NB", 0, 8), float(W)); ms(A("NB", 8 + W), float(W))
    ms(A("Z", V), 0.0); ms(A("QT", V), 0.0)
    iota(A("CD"), [[1, 3], [0, 32]], 1)
    iota(A("YD"), [[0, 1440]])
    for q in range(1, 16): act(A("LQ", 129 * q, 128 * q + 128, 16), A("LT", q, 128, 16), AF.Copy, 0.0, 2048.0)

    def cand_terms(t):
        ts(A("TN"), A("NB", 8 + t, 8 + t + 1276, 5) if t else A("NBI", 0, 1276, 5), CEN, AL.subtract)
        wrap(A("P5", 0, 16), "FE", "TN", 0, 256)
        ts(A("NO"), A("P5", 0, 16), CEN, AL.add)
        act(A("YN"), gat("Y", 0, W, A("NO")), AF.Copy)
        mm(A("P5", 256, 512), A("NID"), A("Y", t, t + 1276, 5), True, False)
        mm(A("P5", 256, 512), A("ID"), A("YN"), False, True)
        act(A("C2"), A("P5", 256, 512), AF.Abs, col("PC", 5), 32.0)
        act(A("C1"), A("P5", 256, 512), AF.Relu, 0.0, 32.0)
        act(A("P6", 0, 256), A("C2"), AF.Copy, 31.5, -1.0)

    cand_terms(0)
    for i in range(16):
        ts(A("SEL", 128 * i, 128 * i + 128), A("BO"), col("QM", i), AL.mult)
        act(A("SELB", 128 * i, 128 * i + 128), A("BO"), AF.Copy, 0.0, col("QB", i))
    act(A("SG"), A("SG"), AF.Copy, -0.5)
    ts(A("DU"), A("ST"), PQ, AL.add, 1440.0 - CEN, AL.add)
    ts(A("SEG"), A("ST"), 256.0, AL.mult, BIGK, AL.add)
    ts(A("ST"), A("ST"), PQ, AL.add, 0.5, AL.add)
    tt(A("LK"), A("LT"), A("N32"), AL.add); tt(A("TRA"), A("TRI"), A("I192"), AL.add); cp(A("HH"), A("HS"))

    lo = 0; later = []
    for nv, na, pb, at, ay in SUMS:
        n = nv + na; q, y = A(pb, at, at + n), A(pb, ay, ay + n)
        cp(A("GS", 16 * lo, 16 * (lo + nv)), gat("Y", 0, W, A("NBU", lo, lo + nv)))
        act(A("GS", 16 * (lo + nv), 16 * (lo + n)), gat("Y", 0, W, A("NBU", lo + nv, lo + n)), AF.Copy)
        mm(y, A("ID"), A("Y", lo, lo + n), True, True)
        mm(q, A("NID"), A("Y", lo, lo + n), True, False)
        for i in range(16):
            mm(q, A("ID"), A("GS", 16 * lo + i, 16 * (lo + n), 16), False, i == 15)
        act(A("ZA", lo, lo + n), q, AF.Abs, col("PC", 6), 0.5)
        later.append((A("QT", lo, lo + n), q))
        ts(A("ZA", lo, lo + n), A("ZA", lo, lo + n), 64.5 / 64, AL.min, 64.5 / 64, AL.subtract)
        tt(A("Z", lo, lo + n), A("ZA", lo, lo + n), y, AL.mult)
        lo += n

    KEY, XP, KO = A("P0", 0, 192), A("P1", 0, 192), A("P1", 192, 384)
    def wrap_t(o, src, first=True, last=True):
        for e in range(2):
            for h in range(2):
                mm(A(o[0], o[1] + e, o[2], 2), A("HH", 256 * e + 128 * h, 256 * e + 128 * h + 128), A(src[0], src[1] + h, src[2], 2),
                   first and e + h == 0, last and e + h == 2)
    def rows(c0, c1, banks, i, n=1):
        per = 16 // len(banks)
        return A("P%d" % banks[i // per], (c1 - c0) * (i % per), (c1 - c0) * (i % per + n))
    def key_open(plan):
        mm(KEY, A("KU"), A("ONE", 0, 192), True, False)
        for c0, c1, how, banks in plan[1]:
            if how == "max": mm(A("P0", c0, c1), A("BN"), A("XB", c0, c1), False, False)
            if how == "abs":
                per = 16 // len(banks)
                for i in range(16): mm(rows(c0, c1, banks, i), A("NID"), A("XB", c0, c1), i % per == 0, False)
    def distances(plan, off, names):
        for c0, c1, q in plan[0]: fetch(q, A("GS", 16 * c0, 16 * c1), gat("X", 0, W + 16, A(off, c0, c1)))
        for c0, c1, how, banks in plan[1]:
            n = c1 - c0; key = A("P0", c0, c1)
            def gi(i): return A("GS", 16 * c0 + i, 16 * c1, 16)
            def dd(i, k=1): return A("DD", 16 * c0 + n * i, 16 * c0 + n * (i + k))
            per = 16 // len(banks) if banks else 4
            for i in range(16):
                if how == "abs":
                    mm(rows(c0, c1, banks, i), A("ID"), gi(i), False, i % per == per - 1)
                    if i % per == per - 1: act(dd(i + 1 - per, per), rows(c0, c1, banks, i + 1 - per, per), AF.Abs)
                elif how == "sub":
                    tt(dd(i), gi(i), A("P1", c0, c1), AL.subtract)
                    if i % per == per - 1: act(dd(i + 1 - per, per), dd(i + 1 - per, per), AF.Abs)
                else:
                    mm(key, A("FN", 16 - i, 144 - i), gi(i), False, False)
                    tt(dd(i), gi(i), A("P1", c0, c1), AL.max)
            for i in range(16): mm(key, A("FB" if how == "max" else "FA", 16 - i, 144 - i), dd(i), False, False)
        mm(KEY, A("IDH"), names, False, True)
    def least(rs, name=True):
        tr(A("TK"), KEY)
        scan(A("TS"), A(rs), A("TK"), 0.0, AL.max, AL.min)
        ts(A("KR", 0, 12), A("TS", 15, 192, 16), RND, AL.add, RND, AL.subtract)
        if name: tt(A("TC", 0, 12), A("TS", 15, 192, 16), A("KR", 0, 12), AL.subtract)

    parts = [(0, 96, "P0"), (96, 192, "P1"), (192, 256, "P4")]
    def z_sums(plan, t):
        for c0, c1 in OAP: cp(A("OA", c0, c1), A("ASC", t + 5 * c0, t + 5 * c1 - 4, 5))
        for c0, c1, q in plan: fetch(q, A("GS", 16 * c0, 16 * c1), gat("Z", 0, V, A("OA", c0, c1)))
        for c0, c2, pb in parts:
            for j in range(16):
                mm(A(pb, 384, 384 + c2 - c0), A("ID"), A("GS", 16 * c0 + j, 16 * c2, 16), j == 0, j == 15)

    z_sums(ZG0, 0)
    for t in range(3):
        more = t < 2
        DO, DR, MC = A("DO%d" % t, 0, 2), A("DR%d" % t, 0, 2), "MC%d" % t
        for c0, c2, pb in parts:
            act(A("SM", c0, c2), A(pb, 384, 384 + c2 - c0), AF.Copy, 192.0)
            tt(A("T1", c0, c2), A(pb, 384, 384 + c2 - c0), A("C1", c0, c2), AL.mult)
            if c0 > 0:
                c0 = 0 if c2 < 256 else c0
                tt(A("T2", c0, c2), A("SM", c0, c2), A("P6", c0, c2), AL.mult)
                mm(A("P2", c0, c2), A("BO4"), A("C2", c0, c2), True, False)
                mm(A("P2", c0, c2), A("BOH"), A("T1", c0, c2), False, False)
                mm(A("P2", c0, c2), A("BO"), A("T2", c0, c2), False, True)
        ts(A("WL", 0, 256), A("P2", 0, 256), col("EF", 0), AL.is_le)
        if t == 0:
            for o, i in later: act(o, i, AF.Copy)
        scan(A("CC"), A("WL"), A("C32"), 0.0, AL.add, AL.min)
        act(A("JK", 0, 288), A("CC"), AF.Sign, col("ST", 0), -1.0, col("AD", 0))
        ts(A("JK", 288, 576), A("CC"), col("ST", 1), AL.is_le)
        add("V", lambda: g.vector.tensor_reduce(R(col("AD", 1)), R(A("JK", 288, 576)), AX.X, AL.add), [col("AD", 1)], [A("JK", 288, 576)], None, "wide")
        ts(col(DO[0], 0), col("AD", 0), 2.5, AL.mult, 720.0 + t, AL.add)
        ts(col(DO[0], 1), col("AD", 1), 5.0, AL.mult, float(t), AL.add)
        send("d%d" % t, DR, DO)
        ts(A("LI", 0, 32), gat("ASC", 0, 1440, DO), 15, AL.bitwise_and)
        ts(A("NA", 0, 32), gat("ASC", 0, 1440, DO), -1.0, AL.mult)
        ts(A("NA", 32, 34), DO, -1.0, AL.mult)
        ts(A("LO", 0, 32), A("LI", 0, 32), P16, AL.add)
        ts(A("DV", 0, 2), DO, float(V), AL.is_ge, 1440.0, AL.mult)
        tt(A("DV", 2, 4), A("DV", 0, 2), A("NA", 32, 34), AL.subtract)
        cp(A("DX", 0, 2), A("DV", 2, 4))
        cp(gat("X", 0, 2880, A("DX", 0, 2)), A("CX"))
        wrap(A("P4", 0, 80), "F1", "X", 0, V)
        act(A("DF", 0, 80), A("P4", 0, 80), AF.Copy)
        if more: mm(A("P7", 0, 1), A("O16"), col("CC", 255), True, True)
        ts(A("NJ", 0, 32 - NSTEP), A("NA", NSTEP, 32), -1.0 / 16, AL.mult, 1.0 / 32, AL.add)
        if t > 0: mm(A("P3", 0, 81), A("IDF"), A("CT"), True, False)
        for d in range(32):
            if d < NSTEP:
                act(A("SN", 81 * d, 81 * d + 81), A("SG"), AF.Sign, col("NA", d))
            else:
                ts(A("SN", 81 * d, 81 * d + 81), A("SJ"), col("NJ", d - NSTEP), AL.is_gt, 2.0, AL.mult)
            ts(A("OH", 128 * d, 128 * d + 128), A("IP"), col("LO", d), AL.is_equal, 256.0, AL.mult)
            mm(A("P3", 0, 81), A("OH", 128 * d, 128 * d + 128), A("SN", 81 * d, 81 * d + 81), t == 0 and d == 0, d == 31)
        tt(A("CS"), A("P3", 0, 80), A("DF", 0, 80), AL.add)
        tt(A("FL", 0, 80), A("P3", 1, 81), A("CS"), AL.is_gt)
        scan(A("FS", 1, 93), A("FL"), A("ONE", 0, 92), 0.0, AL.add, AL.mult)
        mm(A("P5", 0, 92), A("BO"), A("FS", 1, 93), True, True)
        mm(A("P4", 0, 92), A("BO"), A("FS", 0, 92), True, False)
        mm(A("P4", 0, 92), A("TRI"), A("FL"), False, True)
        for c in range(12):
            act(A("JK", 576 + 92 * c, 668 + 92 * c), A("P5", 0, 92), AF.Sign, col("ST", c), -1.0, col("AC", c))
        cp(A("CU", 0, 92), A("P4", 0, 92))
        cp(gat("YD", 0, 1440, DO), A("CD", 32 * t, 32 * t + 32))
        if not more: store("S", T.yd[:], A("YD", 0, V, p=(0, 128, 16)), "s_yd")
        if t > 0:
            cp(A("MO"), A("MR%d" % (t - 1), 192, 204))
            cp(gat("NB", 8 + V, 2760, A("MO")), A("MR%d" % (t - 1), 0, 192))
        cp(gat("X", V, 2720, DR), A("CX"))
        ts(A("HU"), A("AC"), 92.0, AL.add, 0.5, AL.mult)
        act(A("HB"), A("AC"), AF.Copy, 46.0, 0.5)
        tt(A("CM"), gat("CU", 0, 92, A("HU")), A("IS"), AL.is_le)
        mm(A("P6", 0, 12), A("ID16"), A("HB"), True, False)
        wrap(A("P6", 0, 12), "F1", "CM", 0, 192, False, True)
        cp(A("BU"), A("P6", 0, 12))
        if more:
            mm(A("P7", 64, 256), A("BO"), A("CM"), True, True)
            ts(A("DF", 80, 160), A("CU", 0, 80), 192.0, AL.is_gt, 512.0, AL.mult)
            cp(col("EI", 0), col("P7", 0))
            ts(A("RG", 0, 192), A("P7", 64, 256), col("PC", 10) if t else PQ, AL.is_equal)
            ts(col("EI", 1), col("EI", 0), 7, AL.bitwise_and)
            ts(col("EF", 0), col("EI", 1), LOSS0, AL.add)
            tt(A("DG"), A("FL", 0, 80), A("DF", 80, 160), AL.mult)
            scan(A("CT", 1, 81), A("DG"), A("ONE", 0, 80), 0.0, AL.add, AL.mult)
            cp(A(MC, 192, 204), A("BU"))
            act(A("RG", 192, 384), A("RG", 0, 192), AF.Copy, 1.0, -1.0)
        B = A("BU")
        cp(A("LU"), gat("NB", 8, 1480, B))
        act(A("XB"), gat("X", 0, 1472, B), AF.Copy)
        mm(XP, A("ID"), A("XB"), True, True)
        key_open(NEAR)
        ts(A("LH"), A("LU"), CEN, AL.subtract)
        ts(A("DP", 0, 12), B, float(V), AL.is_ge)
        ts(A("BH"), B, CEN, AL.subtract)
        BP = A("P2", 320, 512)
        for q in range(16): mm(A("P2", 320 + q, 512, 16), A("SEL", 128 * q, 128 * q + 128), A("BH"), q == 0, q == 15)
        if more: tt(A("RB"), BP, A("RG", 0, 192), AL.mult)
        distances(NEAR, "LU", A("LH"))
        def pslab(i): return A("P%d" % EQB[i // 2 % len(EQB)], 192 * (i % 2), 192 * (i % 2) + 192)
        def sel_mm(i): mm(pslab(i), A("SEL", 128 * i, 128 * i + 128), A("LH"), True, True)
        least("RS1")
        act(A("SD"), KEY, AF.Sign, col("PC", 7))
        wrap_t(A("P2", 256, 268), A("TC", 0, 12))
        ts(A("UO"), A("P2", 256, 268), CEN + 8, AL.add)
        cp(A("MU"), gat("NB", 0, W + 16, A("UO")))
        mm(KO, A("LK"), A("SD"), True, True)
        wrap(A("P1", 384, 396), "F4", "SD", 0, 192)
        ts(KO, KO, col("PC", 3), AL.is_equal)
        act(A("ND"), A("P1", 384, 396), AF.Copy, 65536.0 - 2000)
        for i in range(2 * len(EQB)): sel_mm(i)
        key_open(OFFER)
        tt(A("UF"), A("P2", 256, 268), A("ND"), AL.min)
        ts(A("MH"), A("MU"), CEN, AL.subtract)
        tt(slab("EQ", 16), BP, A("MH"), AL.is_equal)
        mm(KEY, A("IDB"), slab("EQ", 16), False, False)
        ts(A("AK", 0, 12), A("UF"), V - CEN, AL.is_ge)
        ts(A("DP", 16, 28), A("ND"), 0.0, AL.is_lt)
        scan(A("AK", 17, 29), A("AK", 0, 12), A("ONE", 0, 12), 0.0, AL.add, AL.mult)
        tt(A("KL"), A("LH"), KO, AL.mult)
        mm(A("P2", 272, 284), A("I256"), A("DP", 0, 12), True, False)
        mm(A("P2", 272, 284), A("I256"), A("DP", 16, 28), False, False)
        mm(A("P2", 272, 284), A("TRA"), A("AK", 0, 12), False, False)
        mm(A("P2", 272, 284), A("BO"), A("AK", 16, 28), False, True)
        mm(A("P2", 0, 192), A("BOH"), A("KL"), True, True)
        ts(A("DP", 32, 44), A("P2", 272, 284), 224.0, AL.is_gt)
        for q in range(16): mm(A("P0", q, 192, 16), A("SELB", 128 * q, 128 * q + 128), A("DP", 32, 44), False, False)
        tr(A("TF"), A("P2", 0, 192))
        tt(A("RS2", 0, 192, 16), A("TF", 15, 192, 16), A("SEG"), AL.add)
        for i in range(16):
            tt(slab("EQ", i), pslab(i), A("MH"), AL.is_equal)
            mm(KEY, A("IDB"), slab("EQ", i), False, False)
            if i % 2 == 1 and i + 2 * len(EQB) < 17:
                sel_mm(i + 2 * len(EQB) - 1); sel_mm(i + 2 * len(EQB))
        if more:
            act(A("YB"), gat("Y", 0, 1472, B), AF.Copy, 0.0, -1.0)
            act(A("QP"), gat("QT", 0, 1472, B), AF.Copy)
        distances(OFFER, "MU", A("MH"))
        if more:
            wrap(A("P6", 0, 12), "FH", "KL", 0, 192)
            ts(A("OO"), A("P6", 0, 12), CEN, AL.add)
            act(A("YO"), gat("Y", 0, W + 16, A("OO")), AF.Copy)
        LST = A("P4", 0, 192)
        mm(LST, A("KC"), A("ONE", 0, 192), True, False)
        mm(LST, A("IDH"), A("LH"), False, False)
        mm(LST, A("NIH"), A("KL"), False, not more)
        least("RS2", more)
        tt(A("NMS", 0, 192, 16), A("TS", 15, 192, 16), A("KR", 0, 12), AL.subtract)
        scan(A("TH"), A("RM"), A("NMS"), 0.0, AL.mult, AL.add)
        tr(A("WR"), A("TH"))
        if not more:
            act(A("LW"), LST, AF.Copy)
            tt(A("LF"), A("WR"), KO, AL.mult)
            tt(gat("NB", 8, 1480, B), A("LF"), A("LW"), AL.add)
            store("S", T.yn[:, 0:640], A("NB", 8, 648), "s_y0")
            store("A", T.yn[:, 640:V], A("NB", 648, 8 + V), "s_y1")
            break
        ts(A("TC", 16, 28), A("TS", 15, 192, 16), BIGK - 2048, AL.is_ge, 4096.0, AL.mult)
        ts(A("TC", 32, 44), A("TC", 0, 12), V - CEN, AL.is_ge, 4096.0, AL.mult)
        wrap_t(A("P5", 0, 12), A("TC", 0, 12))
        wrap_t(A("P2", 304, 316), A("TC", 16, 28), True, False); wrap_t(A("P2", 304, 316), A("TC", 0, 12), False, True)
        cp(A("WF", 0, 12), A("P2", 304, 316))
        ts(A("WO", 12, 24), A("P2", 304, 316), CEN, AL.add, 1440.0, AL.min)
        ts(A("WO", 0, 12), A("P5", 0, 12), CEN, AL.add)
        act(A("YW"), gat("Y", 0, W + 16, A("WO", 0, 12)), AF.Copy)
        mm(A("P3", 0, 192), A("ID"), A("QP"), True, False)
        mm(A("P3", 0, 192), A("NID"), A("YO"), False, False)
        mm(A("P3", 0, 192), A("ID"), A("YW"), False, True)
        act(A("FZ"), A("P3", 0, 192), AF.Abs, col("PC", 6), 0.5)
        act(A("FZ"), A("FZ"), AF.Relu, col("PC", 11), -1.0)
        tt(gat("Z", 0, 1472, B), A("FZ"), A("YB"), AL.mult)
        if t == 0:
            act(A("QN"), A("P3", 0, 192), AF.Copy)
            cp(gat("QT", 0, 1472, B), A("QN"))
        tt(A("TW"), A("WR"), KO, AL.mult)
        mm(LST, A("IDH"), A("TW"), False, True)
        act(A("MS"), LST, AF.Copy)
        act(A("MD"), LST, AF.Relu, col("PC", 12), -1.0)
        act(A(MC, 0, 192), A("MD"), AF.Copy, float(W), -1.0)
        send("u%d" % t, A("MR%d" % t), A(MC))
        cp(gat("NB", 8, 1480, B), A("MS"))
        for k, c in enumerate((16, 0, 32)): wrap_t(A("P7", 0, 12), A("TC", c, c + 12), k == 0, False)
        for c in range(12):
            ts(A("EE", 208 * c, 192 * (c + 1)), A("WR", 16 * c, 192), col("WF", c), AL.is_equal)
            if c < 11: mm(A("P6", 256 + 16 * (c + 1), 448), A("BO"), A("EE", 208 * c + 16, 192 * (c + 1)), c == 0, c == 10)
        act(A("LS", 16, 192), A("P6", 272, 448), AF.Sign)
        for q in range(1, 16):
            mm(A("P7", 0, 12), A("LQ", 128 * q, 128 * q + 128), A("EE", q, 2304, 208), False, False)
        for q in range(16): mm(A("P7", 1, 12), A("FA", 16 - q, 144 - q), A("LS", 16 + q, 192, 16), False, q == 15)
        tt(A("WF", 12, 24), A("P7", 0, 12), A("DU"), AL.min)
        ts(A("WS"), A("WF", 12, 24), CEN, AL.add)
        tt(A("MA"), gat("ASC", 0, 1632, A("WO", 12, 24)), A("RG", 192, 384), AL.mult)
        mm(A("P3", 256, 448), A("IDH"), A("RB"), True, False)
        mm(A("P3", 256, 448), A("ICN"), A("RG", 0, 192), False, False)
        mm(A("P3", 256, 448), A("IDH"), A("MA"), False, True)
        act(A("L2"), A("P3", 256, 448), AF.Copy)
        cp(gat("ASC", 0, 1632, A("WS")), A("L2"))
        cand_terms(t + 1)
        z_sums(ZG1, t + 1)

    emit_all(ops, Q, T)


LAT = 0.18
CY, PCY = 0.83e-3, 0.45e-3
WIDE = {"float32": 4, "int32": 4}
PASSES = 2
FIRST = 3.0
RATE = 60e3
REACH = 300
PLAN = {}


def span(a):
    return 16 * span(a[5]) if a[5] else -(-(a[2] - a[1]) // (a[3] or 1))


def call_time(q, kind, outs, ins):
    full = [a for a in outs[:1] + ins if isinstance(a, tuple)]
    if kind == "wait": return 0.0, 0.0
    if kind in ("dma", "send"):
        a = full[0] if kind == "dma" else ins[0]
        by = 128 * span(a) * WIDE.get(SB[a[0]][1], 2)
        return (by / 300e3, 1.0 + by / 300e3) if kind == "dma" else (FIRST if a[0] == "Y" else 0.3, 1.3 + by / RATE)
    if q == "P": t = max(64, span(ins[1])) * PCY * (4 if SB[ins[1][0]][1] == "float32" else 1)
    elif q == "G": t = 0.17 + 2 * span(full[0]) * CY
    elif full[0][5]: t = 0.05 + 3.8 * span(full[0]) * CY
    elif len(full) > 1 and full[1][5]: t = 0.06 + 1.56 * span(full[1]) * CY
    else:
        n = span(full[min(1, len(full) - 1)])
        wide = kind == "wide" or any(a[0] not in SB or SB[a[0]][1] in WIDE for a in full if span(a) == n)
        if q == "V" and kind == "tt": n *= 2 if all(a[0] in SB for a in full[1:]) else 1
        elif q == "V" and not wide: n /= 2
        t = max(64, n) * CY
    return t, t


def conflicts(ops):
    hist = {}; deps = []
    for n, (q, emit, rd, wr, token, cost, kind) in enumerate(ops):
        d = {}
        for a, w in [(a, False) for a in rd] + [(a, True) for a in wr]:
            bank = a[0] not in SB
            for m, lo, hi, w2 in hist.get(a[0], ()):
                same = ops[m][0] == q and ops[m][4] is None and token is None
                meet = lo < a[2] and a[1] < hi
                if same:
                    if q == "P":
                        if bank and not (kind == "mid" == ops[m][6]): d[m] = False
                    elif meet and (w or w2): d[m] = True
                elif bank or (meet and (w or w2)): d[m] = True
        d.pop(n, None)
        deps.append(d)
        for a, w in [(a, False) for a in rd] + [(a, True) for a in wr]:
            hist.setdefault(a[0], []).append((n, a[1], a[2], w))
    return deps


def place(ops, order, edge, free):
    busy = {}; start = [0.0] * len(ops)
    for k in order:
        t = max([start[m] + lag for m, lag in edge[k].items()] + [free[k]])
        c = ops[k][5][0]; line = busy.setdefault(ops[k][0], [])
        j = len(line)
        while j > 0 and line[j - 1][1] > t: j -= 1
        while j < len(line) and t + c > line[j][0] + 1e-9:
            t = max(t, line[j][1]); j += 1
        line.insert(j, (t, t + c)); start[k] = t
    return start


def arrange(ops, deps):
    n = len(ops)
    edge = [dict((m, ops[m][5][1] + LAT if w else ops[m][5][0]) for m, w in d.items()) for d in deps]
    for k, o in enumerate(ops):
        if o[0] == "X": edge[k][k - 1] = ops[k - 1][5][1] + 1.0
    back = [{} for _ in ops]
    tail = [o[5][1] for o in ops]
    floor = [0.0] * n; below = [0] * n; line = {}
    for k in range(n - 1, -1, -1):
        for q, calls in line.items():
            load = 0.0
            for rest, d in calls[:-REACH:-1]:
                if below[k] >> d & 1:
                    load += ops[d][5][0]
                    tail[k] = max(tail[k], ops[k][5][1] + LAT + load + rest)
        tail[k] = max(floor[k], tail[k] + URGE.get(ops[k][0] + (ops[k][3][0][0] if ops[k][3] else ""), 0.0))
        calls = line.setdefault(ops[k][0], []); j = len(calls); rest = tail[k] - ops[k][5][0]
        while j > 0 and calls[j - 1][0] > rest: j -= 1
        calls.insert(j, (rest, k))
        for m, lag in edge[k].items():
            tail[m] = max(tail[m], lag + tail[k])
            floor[m] = max(floor[m], tail[k] + 1e-6)
            below[m] |= below[k] | 1 << k
            back[m][k] = lag + ops[k][5][0] - ops[m][5][0]
    order = sorted(range(n), key=lambda k: (-tail[k], k)); best = None
    for _ in range(PASSES):
        start = place(ops, order, edge, [0.0] * n)
        end = max(start[k] + ops[k][5][1] for k in range(n))
        if best is None or end < best[0]: best = (end, start)
        late = place(ops, sorted(range(n), key=lambda k: (-start[k] - ops[k][5][0], -k)), back, [o[5][1] - o[5][0] for o in ops])
        order = sorted(range(n), key=lambda k: (-late[k] - ops[k][5][0], k))
    PLAN["end"] = best[0]
    return sorted(range(n), key=lambda k: (best[1][k], k))


def emit_all(ops, Q, T):
    if "order" not in PLAN:
        PLAN["order"] = arrange(ops, conflicts(ops))
        PLAN["deps"] = [[m for m, w in d.items() if w] for d in conflicts([ops[k] for k in PLAN["order"]])]
    ops = [ops[k][:5] for k in PLAN["order"]]; deps = PLAN["deps"]
    know = {q: ({}, set()) for q in Q}
    after = {}
    waits = []
    for n, (q, emit, rd, wr, token) in enumerate(ops):
        if q == "X":
            after[n] = ({}, {n}); waits.append([]); continue
        kq, kd = know[q]
        ws = []
        for m in sorted(deps[n], reverse=True):
            if ops[m][4] is None:
                if kq.get(ops[m][0], -1) >= m: continue
            elif m in kd: continue
            ws.append(m)
            for e, v in after[m][0].items(): kq[e] = max(kq.get(e, -1), v)
            kd |= after[m][1]
        waits.append(ws)
        a0, a1 = dict(kq), set(kd)
        if token is None: a0[q] = n
        else: a1.add(n)
        after[n] = (a0, a1)
    needed = set(m for ws in waits for m in ws)
    count = {}; tok = {}
    for n, (q, emit, rd, wr, token) in enumerate(ops):
        if token is not None: tok[n] = token
        elif n in needed:
            count[q] = count.get(q, 0) + 1; tok[n] = ("q" + q, count[q])
    for n, (q, emit, rd, wr, token) in enumerate(ops):
        if q == "X": continue
        for m in waits[n]: Q[q].wait_ge(T.sem[tok[m][0]], tok[m][1])
        ins = emit()
        if token is None and n in needed: ins.then_inc(T.sem[tok[n][0]], 1)
    for n, (q, emit, rd, wr, token) in enumerate(ops):
        if token is not None and n not in needed: Q["S"].wait_ge(T.sem[token[0]], token[1])
